import numpy as np
import ml_dtypes


def mxq(x, axis, fmt="e4m3"):
    dtype, down = {"e4m3": (ml_dtypes.float8_e4m3fn, 7), "e5m2": (ml_dtypes.float8_e5m2, 14)}[fmt]
    v = np.moveaxis(np.asarray(x, np.float32).astype(ml_dtypes.bfloat16).astype(np.float64), axis, -1)
    blocks = v.reshape(v.shape[:-1] + (-1, 32))
    amax = np.abs(blocks).max(-1, keepdims=True)
    byte = np.maximum(np.where(amax > 0, np.frexp(amax)[1] - 1 + 127, 0) - down, 1)
    scale = np.exp2(byte - 127.0)
    codes = (blocks / scale).astype(np.float32).astype(dtype).astype(np.float64)
    return np.moveaxis((codes * scale).reshape(v.shape), -1, axis)


WIDE = False


def mx_kscale(k):
    if not WIDE:
        return np.ones(k)
    levels = np.array([10, -10, 5, -5, 0])
    if k % 512:
        return np.exp2(np.random.permutation(np.resize(levels, k // 32))).repeat(32)
    a = np.empty((k // 512, 16))
    for p in range(k // 512):
        a[p, :8] = np.random.permutation(np.resize(levels, 8))
        for g in range(8):
            far = levels[np.abs(levels - a[p, g]) >= 10]
            a[p, g + 8] = far[np.random.randint(len(far))]
    return np.exp2(a.ravel()).repeat(32)


def f64(x):
    return np.asarray(x).astype(np.float64)


def striped(idx):
    return np.tile(idx.reshape(-1, 16).T, (8, 1)).astype(np.uint16)


def unstriped(offs):
    return offs[:16].T.reshape(-1).astype(np.int64)


def pack_weight(w):
    k, n = w.shape
    w = f64(np.asarray(w, np.float32).astype(ml_dtypes.bfloat16)).reshape(k // 32, 32, n)
    amax = np.abs(w).max(1)
    byte = np.clip(np.where(amax > 0, np.frexp(amax)[1] - 1 + 127 - 7, 1), 1, 254)
    scaled = (w * np.exp2(127.0 - byte)[:, None, :]).reshape(k, n).astype(np.float32)
    words = np.ascontiguousarray(scaled.reshape(k // 512, 128, 4, n).transpose(0, 1, 3, 2)).astype(ml_dtypes.float8_e4m3fn).view(np.uint8)
    return words, np.ascontiguousarray(byte.astype(np.uint8).reshape(k // 512, 16, n))


def unpack_weight(words, scales):
    g, p, n, _ = words.shape
    vals = np.ascontiguousarray(words).view(ml_dtypes.float8_e4m3fn).astype(np.float64) * np.repeat(np.exp2(scales.astype(np.float64) - 127.0), 8, axis=1)[..., None]
    return vals.transpose(0, 1, 3, 2).reshape(g * 512, n)


def sigmoid(v):
    return 1.0 / (1.0 + np.exp(-np.maximum(v, -700.0)))


K, T, S, V, N = 512, 1024, 512, 256, 256


def setup_inputs():
    n = np.random.standard_normal
    s = mx_kscale(K)[:, None]
    near = np.random.permutation(S)
    packed_xT = pack_weight(n((K, T)) * s)
    return {
        "x_words": packed_xT[0],
        "x_scales": packed_xT[1],
        "eT": (n((K, V)) * s).astype(np.float32),
        "w1": (n((K, N)) / np.sqrt(2 * K) / s).astype(np.float32),
        "w2": (n((K, N)) / np.sqrt(2 * K) / s).astype(np.float32),
        "w3": (n((K, N)) / np.sqrt(2 * K) / s).astype(np.float32),
        "v1": (n((K, N)) / np.sqrt(2 * K) / s).astype(np.float32),
        "v2": (n((K, N)) / np.sqrt(2 * K) / s).astype(np.float32),
        "v3": (n((K, N)) / np.sqrt(2 * K) / s).astype(np.float32),
        "cell": (n((N, S))).astype(np.float32),
        "offs": striped(np.random.permutation(T)[:S]),
        "pos1": striped(near[:V]),
        "pos2": striped(near[V:]),
    }


def reference(x_words, x_scales, eT, w1, w2, w3, v1, v2, v3, cell, offs, pos1, pos2):
    eTq = mxq(f64(eT), 0, "e4m3")
    e1 = mxq(f64(w1), 0, "e4m3").T @ eTq
    xq = unpack_weight(x_words, x_scales)[:, unstriped(offs)]
    h1 = mxq(f64(v1), 0, "e4m3").T @ xq
    a = sigmoid(e1 + h1[:, unstriped(pos1)] + h1[:, unstriped(pos2)])
    e2 = mxq(f64(w2), 0, "e4m3").T @ eTq
    h2 = mxq(f64(v2), 0, "e4m3").T @ xq
    g = np.tanh(e2 + h2[:, unstriped(pos1)] + h2[:, unstriped(pos2)])
    e3 = mxq(f64(w3), 0, "e4m3").T @ eTq
    h3 = mxq(f64(v3), 0, "e4m3").T @ xq
    return np.tanh(a * g + (sigmoid(e3 + h3[:, unstriped(pos1)])) * f64(cell)[:, unstriped(pos1)] + (sigmoid(e3 + h3[:, unstriped(pos2)])) * f64(cell)[:, unstriped(pos2)])

@@ -1,0 +1,155 @@
+from contextlib import ExitStack
+
+import concourse.mybir as mybir
+
+K, T, S, V, N = 512, 1024, 512, 256, 256
+FLOPS = 2 * K * N * 3 * (V + S)
+
+F32 = mybir.dt.float32
+BF16 = mybir.dt.bfloat16
+I32 = mybir.dt.int32
+U32 = mybir.dt.uint32
+U16 = mybir.dt.uint16
+U8 = mybir.dt.uint8
+FP8X4 = mybir.dt.float8_e4m3fn_x4
+ACT = mybir.ActivationFunctionType
+ALU = mybir.AluOpType
+
+P = 128
+PACK = 4
+RUN = 4
+BLOCKS = N // P
+
+
+def tile_picked_ztree_tanh_p_kernel(tc, x_words, x_scales, eT, w1, w2, w3, v1, v2, v3, cell, offs, pos1, pos2, out):
+    nc = tc.nc
+    with ExitStack() as ctx:
+        keep = ctx.enter_context(tc.tile_pool(name="keep", bufs=1))
+        hbanks = ctx.enter_context(tc.psum_pool(name="hbanks", bufs=4))
+        ebanks = ctx.enter_context(tc.psum_pool(name="ebanks", bufs=3))
+
+        def load_list(src, name):
+            lst = keep.tile(list(src.shape), U16, name=name)
+            nc.sync.dma_start(lst[:], src)
+            return lst
+
+        def load_matrix(src, name):
+            raw = keep.tile([P, PACK, src.shape[1]], F32, name=name)
+            nc.sync.dma_start(out=raw[:], in_=src.rearrange("(p j) c -> p j c", j=PACK))
+            return raw
+
+        def round_and_weave(raw, name, copy):
+            width = raw.shape[2]
+            woven = keep.tile([P, width, PACK], BF16, name=name, align_bytes=64)
+            copy(out=woven[:].rearrange("p (c i) j -> p c j i", i=RUN), in_=raw[:].rearrange("p j (c i) -> p c j i", i=RUN))
+            return woven
+
+        def quantise(woven, name):
+            width = woven.shape[1]
+            codes = keep.tile([P, width], U32, name=name + "_codes", align_bytes=64)
+            scales = keep.tile([P, width], U8, name=name + "_scales", align_bytes=64)
+            nc.vector.quantize_mx(out=codes[:].bitcast(FP8X4), scales=scales[:], in_=woven[:].rearrange("p c j -> p (c j)"))
+            return codes, scales
+
+        def product(dst, weights, b, moving):
+            cols = slice(b * P, (b + 1) * P)
+            nc.tensor.matmul_mx(out=dst, lhsT=weights[0][:, cols].bitcast(FP8X4), lhsT_scale=weights[1][:, cols],
+                                rhs=moving[0][:].bitcast(FP8X4), rhs_scale=moving[1][:], start=True, stop=True)
+
+        def first_scalar_copy(out, in_):
+            nc.scalar.activation(out, in_, ACT.Copy)
+
+        scale_table = keep.tile([P, T], U8, align_bytes=64)
+        nc.vector.memset(scale_table[:].bitcast(I32), 0)
+        word_table = keep.tile([P, T], U32, align_bytes=64)
+        nc.sync.dma_start(out=word_table[:].bitcast(I32), in_=x_words[0].rearrange("p c r -> p (c r)").bitcast(I32))
+        for q in range(4):
+            nc.sync.dma_start(out=scale_table[32 * q : 32 * q + 4, :].bitcast(I32), in_=x_scales[0, 4 * q : 4 * q + 4, :].bitcast(I32))
+        offs_t = load_list(offs, "offs_t")
+        raw = {}
+        raw["v1"] = load_matrix(v1, "raw_v1")
+        raw["e"] = load_matrix(eT, "raw_e")
+        raw["w1"] = load_matrix(w1, "raw_w1")
+        pos = [load_list(pos1, "pos1_t"), load_list(pos2, "pos2_t")]
+        for name, src in (("v3", v3), ("w3", w3)):
+            raw[name] = load_matrix(src, "raw_" + name)
+        cells = []
+        for b in range(BLOCKS):
+            rows = keep.tile([P, S], F32, name="cell%d" % b)
+            nc.sync.dma_start(out=rows[:], in_=cell[b * P : (b + 1) * P, :])
+            cells.append(rows)
+        for name, src in (("v2", v2), ("w2", w2)):
+            raw[name] = load_matrix(src, "raw_" + name)
+
+        x_codes = keep.tile([P, S], U32, align_bytes=64)
+        x_bytes = keep.tile([P, S], U8, align_bytes=64)
+        nc.vector.tensor_copy(x_codes[:], word_table[:].indirect(offs_t[:]))
+        nc.vector.tensor_copy(x_bytes[:], scale_table[:].indirect(offs_t[:]))
+        picked = (x_codes, x_bytes)
+
+        def state_product(name, copy):
+            quantised = quantise(round_and_weave(raw[name], "woven_" + name, copy), name)
+            rows = []
+            for b in range(BLOCKS):
+                bank = hbanks.tile([P, S], F32, name="hbank")
+                product(bank[:], quantised, b, picked)
+                h = keep.tile([P, S], F32, name="h_%s_%d" % (name, b))
+                nc.scalar.copy(out=h[:], in_=bank[:])
+                rows.append(h)
+            return rows
+
+        def node_product(name, copy, nodes):
+            quantised = quantise(round_and_weave(raw[name], "woven_" + name, copy), name)
+            bank = ebanks.tile([P, BLOCKS, V], F32, name="ebank")
+            for b in range(BLOCKS):
+                product(bank[:, b, :], quantised, b, nodes)
+            e = keep.tile([P, BLOCKS, V], F32, name="e_" + name)
+            nc.scalar.copy(out=e[:], in_=bank[:])
+            return e
+
+        def gather(window, d, other, op, name):
+            dst = keep.tile([P, V], F32, name=name)
+            nc.vector.tensor_tensor(dst[:], window[:].indirect(pos[d][:]), other, op)
+            return dst
+
+        def activate(src, func, name):
+            dst = keep.tile([P, V], F32, name=name)
+            nc.scalar.activation(dst[:], src[:], func)
+            return dst
+
+        def summed_gate(h, e, func, name):
+            first = [gather(h[b], 0, e[:, b, :], ALU.add, "%s_first%d" % (name, b)) for b in range(BLOCKS)]
+            both = [gather(h[b], 1, first[b][:], ALU.add, "%s_both%d" % (name, b)) for b in range(BLOCKS)]
+            return [activate(both[b], func, "%s%d" % (name, b)) for b in range(BLOCKS)]
+
+        h1 = state_product("v1", first_scalar_copy)
+        nodes = quantise(round_and_weave(raw["e"], "woven_e", nc.vector.tensor_copy), "e")
+        e1 = node_product("w1", nc.vector.tensor_copy, nodes)
+        h3 = state_product("v3", nc.scalar.copy)
+        e3 = node_product("w3", nc.scalar.copy, nodes)
+        a = summed_gate(h1, e1, ACT.Sigmoid, "a")
+        h2 = state_product("v2", nc.scalar.copy)
+        e2 = node_product("w2", nc.scalar.copy, nodes)
+
+        kept = []
+        for b in range(BLOCKS):
+            pre = [gather(h3[b], d, e3[:, b, :], ALU.add, "fpre%d_%d" % (b, d)) for d in range(2)]
+            kept.append([activate(pre[d], ACT.Sigmoid, "f%d_%d" % (b, d)) for d in range(2)])
+        remembered = []
+        for b in range(BLOCKS):
+            fc = [gather(cells[b], d, kept[b][d][:], ALU.mult, "fc%d_%d" % (b, d)) for d in range(2)]
+            remembered.append(fc)
+        memory = []
+        for b in range(BLOCKS):
+            both = keep.tile([P, V], F32, name="memory%d" % b)
+            nc.vector.tensor_tensor(both[:], remembered[b][0][:], remembered[b][1][:], ALU.add)
+            memory.append(both)
+
+        g = summed_gate(h2, e2, ACT.Tanh, "g")
+        for b in range(BLOCKS):
+            fresh = keep.tile([P, V], F32, name="fresh%d" % b)
+            nc.vector.tensor_tensor(fresh[:], a[b][:], g[b][:], ALU.mult)
+            state = keep.tile([P, V], F32, name="state%d" % b)
+            nc.vector.tensor_tensor(state[:], fresh[:], memory[b][:], ALU.add)
+            result = activate(state, ACT.Tanh, "result%d" % b)
+            nc.sync.dma_start(out=out[b * P : (b + 1) * P, :], in_=result[:])

@@ -28,128 +28,155 @@ def tile_picked_ztree_tanh_p_kernel(tc, x_words, x_scales, eT, w1, w2, w3, v1, v
         hbanks = ctx.enter_context(tc.psum_pool(name="hbanks", bufs=4))
         ebanks = ctx.enter_context(tc.psum_pool(name="ebanks", bufs=3))
 
+        def sbuf(shape, dtype, name, tag=None):
+            return keep.tile(shape, dtype, name=name, tag=tag or name, align_bytes=64)
+
         def load_list(src, name):
             lst = keep.tile(list(src.shape), U16, name=name)
             nc.sync.dma_start(lst[:], src)
             return lst
 
         def load_matrix(src, name):
-            raw = keep.tile([P, PACK, src.shape[1]], F32, name=name)
+            raw = sbuf([P, PACK, src.shape[1]], F32, "raw_" + name)
             nc.sync.dma_start(out=raw[:], in_=src.rearrange("(p j) c -> p j c", j=PACK))
             return raw
 
-        def round_and_weave(raw, name, copy):
-            width = raw.shape[2]
-            woven = keep.tile([P, width, PACK], BF16, name=name, align_bytes=64)
-            copy(out=woven[:].rearrange("p (c i) j -> p c j i", i=RUN), in_=raw[:].rearrange("p j (c i) -> p c j i", i=RUN))
+        def load_cells(b):
+            rows = sbuf([P, S], F32, "cell%d" % b)
+            nc.sync.dma_start(out=rows[:], in_=cell[b * P : (b + 1) * P, :])
+            return rows
+
+        def weave(name, copy):
+            width = raw[name].shape[2]
+            woven = sbuf([P, width, PACK], BF16, "woven_" + name)
+            copy(out=woven[:].rearrange("p (c i) j -> p c j i", i=RUN), in_=raw[name][:].rearrange("p j (c i) -> p c j i", i=RUN))
             return woven
 
         def quantise(woven, name):
             width = woven.shape[1]
-            codes = keep.tile([P, width], U32, name=name + "_codes", align_bytes=64)
-            scales = keep.tile([P, width], U8, name=name + "_scales", align_bytes=64)
+            codes = sbuf([P, width], U32, name + "_codes")
+            scales = sbuf([P, width], U8, name + "_scales")
             nc.vector.quantize_mx(out=codes[:].bitcast(FP8X4), scales=scales[:], in_=woven[:].rearrange("p c j -> p (c j)"))
             return codes, scales
 
-        def product(dst, weights, b, moving):
-            cols = slice(b * P, (b + 1) * P)
+        def product(dst, weights, first, moving):
+            cols = slice(first, first + P)
             nc.tensor.matmul_mx(out=dst, lhsT=weights[0][:, cols].bitcast(FP8X4), lhsT_scale=weights[1][:, cols],
                                 rhs=moving[0][:].bitcast(FP8X4), rhs_scale=moving[1][:], start=True, stop=True)
 
-        def first_scalar_copy(out, in_):
-            nc.scalar.activation(out, in_, ACT.Copy)
+        def state_product(weights, first):
+            bank = hbanks.tile([P, S], F32, name="hbank")
+            product(bank[:], weights, first, picked)
+            return bank
 
-        scale_table = keep.tile([P, T], U8, align_bytes=64)
-        nc.vector.memset(scale_table[:].bitcast(I32), 0)
-        word_table = keep.tile([P, T], U32, align_bytes=64)
-        nc.sync.dma_start(out=word_table[:].bitcast(I32), in_=x_words[0].rearrange("p c r -> p (c r)").bitcast(I32))
-        for q in range(4):
-            nc.sync.dma_start(out=scale_table[32 * q : 32 * q + 4, :].bitcast(I32), in_=x_scales[0, 4 * q : 4 * q + 4, :].bitcast(I32))
-        offs_t = load_list(offs, "offs_t")
-        raw = {}
-        raw["v1"] = load_matrix(v1, "raw_v1")
-        raw["e"] = load_matrix(eT, "raw_e")
-        raw["w1"] = load_matrix(w1, "raw_w1")
-        pos = [load_list(pos1, "pos1_t"), load_list(pos2, "pos2_t")]
-        for name, src in (("v3", v3), ("w3", w3)):
-            raw[name] = load_matrix(src, "raw_" + name)
-        cells = []
-        for b in range(BLOCKS):
-            rows = keep.tile([P, S], F32, name="cell%d" % b)
-            nc.sync.dma_start(out=rows[:], in_=cell[b * P : (b + 1) * P, :])
-            cells.append(rows)
-        for name, src in (("v2", v2), ("w2", w2)):
-            raw[name] = load_matrix(src, "raw_" + name)
-
-        x_codes = keep.tile([P, S], U32, align_bytes=64)
-        x_bytes = keep.tile([P, S], U8, align_bytes=64)
-        nc.vector.tensor_copy(x_codes[:], word_table[:].indirect(offs_t[:]))
-        nc.vector.tensor_copy(x_bytes[:], scale_table[:].indirect(offs_t[:]))
-        picked = (x_codes, x_bytes)
-
-        def state_product(name, copy):
-            quantised = quantise(round_and_weave(raw[name], "woven_" + name, copy), name)
-            rows = []
-            for b in range(BLOCKS):
-                bank = hbanks.tile([P, S], F32, name="hbank")
-                product(bank[:], quantised, b, picked)
-                h = keep.tile([P, S], F32, name="h_%s_%d" % (name, b))
-                nc.scalar.copy(out=h[:], in_=bank[:])
-                rows.append(h)
-            return rows
-
-        def node_product(name, copy, nodes):
-            quantised = quantise(round_and_weave(raw[name], "woven_" + name, copy), name)
+        def node_product(weights):
             bank = ebanks.tile([P, BLOCKS, V], F32, name="ebank")
             for b in range(BLOCKS):
-                product(bank[:, b, :], quantised, b, nodes)
-            e = keep.tile([P, BLOCKS, V], F32, name="e_" + name)
-            nc.scalar.copy(out=e[:], in_=bank[:])
-            return e
+                product(bank[:, b, :], weights, b * P, nodes)
+            return bank
 
-        def gather(window, d, other, op, name):
-            dst = keep.tile([P, V], F32, name=name)
+        def leave_psum(bank, name):
+            rows = sbuf(list(bank.shape), F32, name)
+            nc.scalar.copy(out=rows[:], in_=bank[:])
+            return rows
+
+        def fetch(window, d, name, tag=None):
+            dst = sbuf([P, V], F32, name, tag)
+            nc.vector.tensor_copy(dst[:], window[:].indirect(pos[d][:]))
+            return dst
+
+        def fetch_with(window, d, other, op, name, tag=None):
+            dst = sbuf([P, V], F32, name, tag)
             nc.vector.tensor_tensor(dst[:], window[:].indirect(pos[d][:]), other, op)
             return dst
 
+        def combine(left, right, op, name):
+            dst = sbuf([P, V], F32, name)
+            nc.vector.tensor_tensor(dst[:], left, right, op)
+            return dst
+
         def activate(src, func, name):
-            dst = keep.tile([P, V], F32, name=name)
+            dst = sbuf([P, V], F32, name)
             nc.scalar.activation(dst[:], src[:], func)
             return dst
 
-        def summed_gate(h, e, func, name):
-            first = [gather(h[b], 0, e[:, b, :], ALU.add, "%s_first%d" % (name, b)) for b in range(BLOCKS)]
-            both = [gather(h[b], 1, first[b][:], ALU.add, "%s_both%d" % (name, b)) for b in range(BLOCKS)]
-            return [activate(both[b], func, "%s%d" % (name, b)) for b in range(BLOCKS)]
+        on_scalar, on_vector = nc.scalar.copy, nc.vector.tensor_copy
 
-        h1 = state_product("v1", first_scalar_copy)
-        nodes = quantise(round_and_weave(raw["e"], "woven_e", nc.vector.tensor_copy), "e")
-        e1 = node_product("w1", nc.vector.tensor_copy, nodes)
-        h3 = state_product("v3", nc.scalar.copy)
-        e3 = node_product("w3", nc.scalar.copy, nodes)
-        a = summed_gate(h1, e1, ACT.Sigmoid, "a")
-        h2 = state_product("v2", nc.scalar.copy)
-        e2 = node_product("w2", nc.scalar.copy, nodes)
+        scale_table = sbuf([P, T], U8, "scale_table")
+        nc.vector.memset(scale_table[:].bitcast(I32), 0)
+        for q in (0, 2, 1, 3):
+            queue = nc.sync if q < 2 else nc.scalar
+            queue.dma_start(out=scale_table[32 * q : 32 * q + 4, :].bitcast(I32), in_=x_scales[0, 4 * q : 4 * q + 4, :].bitcast(I32))
+        offs_t = load_list(offs, "offs_t")
+        word_table = sbuf([P, T], U32, "word_table")
+        nc.sync.dma_start(out=word_table[:].bitcast(I32), in_=x_words[0].rearrange("p c r -> p (c r)").bitcast(I32))
+        raw = {}
+        for b in range(BLOCKS):
+            raw["v1_%d" % b] = load_matrix(v1[:, b * P : (b + 1) * P], "v1_%d" % b)
+        raw["v3"] = load_matrix(v3, "v3")
+        pos = [load_list(pos1, "pos1_t"), load_list(pos2, "pos2_t")]
+        for name, src in (("e", eT), ("w3", w3), ("w1", w1), ("v2", v2), ("w2", w2)):
+            raw[name] = load_matrix(src, name)
+        cells = [load_cells(b) for b in range(BLOCKS)]
 
-        kept = []
-        for b in range(BLOCKS):
-            pre = [gather(h3[b], d, e3[:, b, :], ALU.add, "fpre%d_%d" % (b, d)) for d in range(2)]
-            kept.append([activate(pre[d], ACT.Sigmoid, "f%d_%d" % (b, d)) for d in range(2)])
-        remembered = []
-        for b in range(BLOCKS):
-            fc = [gather(cells[b], d, kept[b][d][:], ALU.mult, "fc%d_%d" % (b, d)) for d in range(2)]
-            remembered.append(fc)
-        memory = []
-        for b in range(BLOCKS):
-            both = keep.tile([P, V], F32, name="memory%d" % b)
-            nc.vector.tensor_tensor(both[:], remembered[b][0][:], remembered[b][1][:], ALU.add)
-            memory.append(both)
+        warm = sbuf([P, 16], F32, "warm")
+        nc.vector.memset(warm[:, 0:8], 0.0)
+        nc.scalar.activation(warm[:, 8:16], warm[:, 0:8], ACT.Sigmoid)
 
-        g = summed_gate(h2, e2, ACT.Tanh, "g")
+        x_bytes = sbuf([P, S], U8, "x_bytes")
+        x_codes = sbuf([P, S], U32, "x_codes")
+        nc.vector.tensor_copy(x_bytes[:], scale_table[:].indirect(offs_t[:]))
+        nc.vector.tensor_copy(x_codes[:], word_table[:].indirect(offs_t[:]))
+        picked = (x_codes, x_bytes)
+
+        bank1 = [state_product(quantise(weave("v1_%d" % b, on_scalar), "v1_%d" % b), 0) for b in range(BLOCKS)]
+        woven_v3 = weave("v3", on_vector)
+        h1 = [leave_psum(bank1[0], "h1_0")]
+        q_v3 = quantise(woven_v3, "v3")
+        bank3 = [state_product(q_v3, b * P) for b in range(BLOCKS)]
+        woven_e = weave("e", on_vector)
+        h1.append(leave_psum(bank1[1], "h1_1"))
+        h3 = [leave_psum(bank3[b], "h3_%d" % b) for b in range(BLOCKS)]
+
+        a_first0 = fetch(h1[0], 0, "a_first0", "raw_e")
+        nodes = quantise(woven_e, "e")
+        woven_w3 = weave("w3", on_vector)
+        woven_w1 = weave("w1", on_scalar)
+        a_both0 = fetch_with(h1[0], 1, a_first0[:], ALU.add, "a_both0", "raw_w3")
+        ebank3 = node_product(quantise(woven_w3, "w3"))
+        a_first1 = fetch(h1[1], 0, "a_first1", "woven_w3")
+        woven_v2 = weave("v2", on_scalar)
+        e3 = leave_psum(ebank3, "e3")
+        ebank1 = node_product(quantise(woven_w1, "w1"))
+        a_both1 = fetch_with(h1[1], 1, a_first1[:], ALU.add, "a_both1", "woven_w1")
+        q_v2 = quantise(woven_v2, "v2")
+        bank2 = [state_product(q_v2, b * P) for b in range(BLOCKS)]
+        woven_w2 = weave("w2", on_scalar)
+
+        fpre0 = [fetch_with(h3[0], d, e3[:, 0, :], ALU.add, "fpre0_%d" % d, "woven_v2" if d == 0 else None) for d in range(2)]
+        ebank2 = node_product(quantise(woven_w2, "w2"))
+        h2 = [leave_psum(bank2[0], "h2_0")]
+        f0 = [activate(fpre0[d], ACT.Sigmoid, "f0_%d" % d) for d in range(2)]
+        e2 = leave_psum(ebank2, "e2")
+        fpre1 = [fetch_with(h3[1], d, e3[:, 1, :], ALU.add, "fpre1_%d" % d, "woven_w2" if d == 0 else None) for d in range(2)]
+        h2.append(leave_psum(bank2[1], "h2_1"))
+        f1 = [activate(fpre1[d], ACT.Sigmoid, "f1_%d" % d) for d in range(2)]
+
+        a_pre = [combine(both[:], ebank1[:, b, :], ALU.add, "a_pre%d" % b) for b, both in enumerate((a_both0, a_both1))]
+        a = [activate(a_pre[b], ACT.Sigmoid, "a%d" % b) for b in range(BLOCKS)]
+        g_first = [fetch_with(h2[b], 0, e2[:, b, :], ALU.add, "g_first%d" % b) for b in range(BLOCKS)]
+        g = []
         for b in range(BLOCKS):
-            fresh = keep.tile([P, V], F32, name="fresh%d" % b)
-            nc.vector.tensor_tensor(fresh[:], a[b][:], g[b][:], ALU.mult)
-            state = keep.tile([P, V], F32, name="state%d" % b)
-            nc.vector.tensor_tensor(state[:], fresh[:], memory[b][:], ALU.add)
-            result = activate(state, ACT.Tanh, "result%d" % b)
-            nc.sync.dma_start(out=out[b * P : (b + 1) * P, :], in_=result[:])
+            g.append(activate(fetch_with(h2[b], 1, g_first[b][:], ALU.add, "g_both%d" % b), ACT.Tanh, "g%d" % b))
+
+        fc0 = [fetch_with(cells[0], d, f0[d][:], ALU.mult, "fc0_%d" % d) for d in range(2)]
+        ag0 = combine(a[0][:], g[0][:], ALU.mult, "ag0")
+        m0 = combine(fc0[0][:], fc0[1][:], ALU.add, "m0")
+        fc10 = fetch_with(cells[1], 0, f1[0][:], ALU.mult, "fc1_0")
+        st0 = combine(ag0[:], m0[:], ALU.add, "st0")
+        nc.sync.dma_start(out=out[0:P, :], in_=activate(st0, ACT.Tanh, "r0")[:])
+        ag1 = combine(a[1][:], g[1][:], ALU.mult, "ag1")
+        m1 = combine(ag1[:], fc10[:], ALU.add, "m1")
+        fc11 = fetch_with(cells[1], 1, f1[1][:], ALU.mult, "fc1_1")
+        st1 = combine(fc11[:], m1[:], ALU.add, "st1")
+        nc.scalar.dma_start(out=out[P : 2 * P, :], in_=activate(st1, ACT.Tanh, "r1")[:])

@@ -46,10 +46,13 @@ def tile_picked_ztree_tanh_p_kernel(tc, x_words, x_scales, eT, w1, w2, w3, v1, v
             nc.sync.dma_start(out=rows[:], in_=cell[b * P : (b + 1) * P, :])
             return rows
 
-        def weave(name, copy):
+        def weave(name, copies):
             width = raw[name].shape[2]
             woven = sbuf([P, width, PACK], BF16, "woven_" + name)
-            copy(out=woven[:].rearrange("p (c i) j -> p c j i", i=RUN), in_=raw[name][:].rearrange("p j (c i) -> p c j i", i=RUN))
+            share = width // len(copies)
+            for part, copy in enumerate(copies):
+                cols = slice(part * share, (part + 1) * share)
+                copy(out=woven[:, cols, :].rearrange("p (c i) j -> p c j i", i=RUN), in_=raw[name][:, :, cols].rearrange("p j (c i) -> p c j i", i=RUN))
             return woven
 
         def quantise(woven, name):
@@ -75,8 +78,8 @@ def tile_picked_ztree_tanh_p_kernel(tc, x_words, x_scales, eT, w1, w2, w3, v1, v
                 product(bank[:, b, :], weights, b * P, nodes)
             return bank
 
-        def leave_psum(bank, name):
-            rows = sbuf(list(bank.shape), F32, name)
+        def leave_psum(bank, name, tag=None):
+            rows = sbuf(list(bank.shape), F32, name, tag)
             nc.scalar.copy(out=rows[:], in_=bank[:])
             return rows
 
@@ -90,32 +93,30 @@ def tile_picked_ztree_tanh_p_kernel(tc, x_words, x_scales, eT, w1, w2, w3, v1, v
             nc.vector.tensor_tensor(dst[:], window[:].indirect(pos[d][:]), other, op)
             return dst
 
-        def combine(left, right, op, name):
-            dst = sbuf([P, V], F32, name)
+        def combine(left, right, op, name, tag=None):
+            dst = sbuf([P, V], F32, name, tag)
             nc.vector.tensor_tensor(dst[:], left, right, op)
             return dst
 
-        def activate(src, func, name):
-            dst = sbuf([P, V], F32, name)
+        def activate(src, func, name, tag=None):
+            dst = sbuf([P, V], F32, name, tag)
             nc.scalar.activation(dst[:], src[:], func)
             return dst
 
-        on_scalar, on_vector = nc.scalar.copy, nc.vector.tensor_copy
+        on_scalar, on_vector, shared = (nc.scalar.copy,), (nc.vector.tensor_copy,), (nc.vector.tensor_copy, nc.scalar.copy)
 
         scale_table = sbuf([P, T], U8, "scale_table")
         nc.vector.memset(scale_table[:].bitcast(I32), 0)
-        for q in (0, 2, 1, 3):
-            queue = nc.sync if q < 2 else nc.scalar
-            queue.dma_start(out=scale_table[32 * q : 32 * q + 4, :].bitcast(I32), in_=x_scales[0, 4 * q : 4 * q + 4, :].bitcast(I32))
-        offs_t = load_list(offs, "offs_t")
         word_table = sbuf([P, T], U32, "word_table")
         nc.sync.dma_start(out=word_table[:].bitcast(I32), in_=x_words[0].rearrange("p c r -> p (c r)").bitcast(I32))
-        raw = {}
-        for b in range(BLOCKS):
-            raw["v1_%d" % b] = load_matrix(v1[:, b * P : (b + 1) * P], "v1_%d" % b)
-        raw["v3"] = load_matrix(v3, "v3")
-        pos = [load_list(pos1, "pos1_t"), load_list(pos2, "pos2_t")]
-        for name, src in (("e", eT), ("w3", w3), ("w1", w1), ("v2", v2), ("w2", w2)):
+        for q in range(4):
+            nc.sync.dma_start(out=scale_table[32 * q : 32 * q + 4, :].bitcast(I32), in_=x_scales[0, 4 * q : 4 * q + 4, :].bitcast(I32))
+        offs_t = load_list(offs, "offs_t")
+        raw = {name: load_matrix(src, name) for name, src in (("v1", v1), ("v3", v3), ("w3", w3), ("e", eT))}
+        pos = [load_list(pos1, "pos1_t")]
+        raw["w1"] = load_matrix(w1, "w1")
+        pos.append(load_list(pos2, "pos2_t"))
+        for name, src in (("v2", v2), ("w2", w2)):
             raw[name] = load_matrix(src, name)
         cells = [load_cells(b) for b in range(BLOCKS)]
 
@@ -125,58 +126,59 @@ def tile_picked_ztree_tanh_p_kernel(tc, x_words, x_scales, eT, w1, w2, w3, v1, v
 
         x_bytes = sbuf([P, S], U8, "x_bytes")
         x_codes = sbuf([P, S], U32, "x_codes")
-        nc.vector.tensor_copy(x_bytes[:], scale_table[:].indirect(offs_t[:]))
         nc.vector.tensor_copy(x_codes[:], word_table[:].indirect(offs_t[:]))
+        nc.vector.tensor_copy(x_bytes[:], scale_table[:].indirect(offs_t[:]))
         picked = (x_codes, x_bytes)
 
-        bank1 = [state_product(quantise(weave("v1_%d" % b, on_scalar), "v1_%d" % b), 0) for b in range(BLOCKS)]
-        woven_v3 = weave("v3", on_vector)
-        h1 = [leave_psum(bank1[0], "h1_0")]
+        woven_v1 = weave("v1", on_scalar)
+        woven_v3 = weave("v3", shared)
+        q_v1 = quantise(woven_v1, "v1")
+        bank1 = [state_product(q_v1, b * P) for b in range(BLOCKS)]
+        woven_w3 = weave("w3", on_vector)
         q_v3 = quantise(woven_v3, "v3")
         bank3 = [state_product(q_v3, b * P) for b in range(BLOCKS)]
-        woven_e = weave("e", on_vector)
+        q_w3 = quantise(woven_w3, "w3")
+        h1 = [leave_psum(bank1[0], "h1_0")]
+        woven_e = weave("e", shared)
+        a_first = [fetch(h1[0], 0, "a_first0")]
         h1.append(leave_psum(bank1[1], "h1_1"))
-        h3 = [leave_psum(bank3[b], "h3_%d" % b) for b in range(BLOCKS)]
-
-        a_first0 = fetch(h1[0], 0, "a_first0", "raw_e")
+        woven_w1 = weave("w1", shared)
         nodes = quantise(woven_e, "e")
-        woven_w3 = weave("w3", on_vector)
-        woven_w1 = weave("w1", on_scalar)
-        a_both0 = fetch_with(h1[0], 1, a_first0[:], ALU.add, "a_both0", "raw_w3")
-        ebank3 = node_product(quantise(woven_w3, "w3"))
-        a_first1 = fetch(h1[1], 0, "a_first1", "woven_w3")
-        woven_v2 = weave("v2", on_scalar)
-        e3 = leave_psum(ebank3, "e3")
+        ebank3 = node_product(q_w3)
+        a_first.append(fetch(h1[1], 0, "a_first1"))
         ebank1 = node_product(quantise(woven_w1, "w1"))
-        a_both1 = fetch_with(h1[1], 1, a_first1[:], ALU.add, "a_both1", "woven_w1")
-        q_v2 = quantise(woven_v2, "v2")
-        bank2 = [state_product(q_v2, b * P) for b in range(BLOCKS)]
+        h3 = [leave_psum(bank3[0], "h3_0")]
+        e3 = leave_psum(ebank3, "e3")
+        h3.append(leave_psum(bank3[1], "h3_1"))
+        a_both = sbuf([P, BLOCKS, V], F32, "a_both")
+        for b in range(BLOCKS):
+            nc.vector.tensor_tensor(a_both[:, b, :], h1[b][:].indirect(pos[1][:]), a_first[b][:], ALU.add)
+        woven_v2 = weave("v2", on_scalar)
         woven_w2 = weave("w2", on_scalar)
 
-        fpre0 = [fetch_with(h3[0], d, e3[:, 0, :], ALU.add, "fpre0_%d" % d, "woven_v2" if d == 0 else None) for d in range(2)]
+        fpre = [[fetch_with(h3[0], d, e3[:, 0, :], ALU.add, "fpre0_%d" % d) for d in range(2)]]
+        fpre.append([fetch_with(h3[1], 0, e3[:, 1, :], ALU.add, "fpre1_0")])
+        q_v2 = quantise(woven_v2, "v2")
+        bank2 = [state_product(q_v2, b * P) for b in range(BLOCKS)]
+        fpre[1].append(fetch_with(h3[1], 1, e3[:, 1, :], ALU.add, "fpre1_1", "raw_v2"))
         ebank2 = node_product(quantise(woven_w2, "w2"))
-        h2 = [leave_psum(bank2[0], "h2_0")]
-        f0 = [activate(fpre0[d], ACT.Sigmoid, "f0_%d" % d) for d in range(2)]
+        f = [[activate(fpre[b][d], ACT.Sigmoid, "f%d_%d" % (b, d), "woven_v2" if b + d == 0 else None) for d in range(2)] for b in range(BLOCKS)]
+        h2 = [leave_psum(bank2[b], "h2_%d" % b) for b in range(BLOCKS)]
         e2 = leave_psum(ebank2, "e2")
-        fpre1 = [fetch_with(h3[1], d, e3[:, 1, :], ALU.add, "fpre1_%d" % d, "woven_w2" if d == 0 else None) for d in range(2)]
-        h2.append(leave_psum(bank2[1], "h2_1"))
-        f1 = [activate(fpre1[d], ACT.Sigmoid, "f1_%d" % d) for d in range(2)]
 
-        a_pre = [combine(both[:], ebank1[:, b, :], ALU.add, "a_pre%d" % b) for b, both in enumerate((a_both0, a_both1))]
-        a = [activate(a_pre[b], ACT.Sigmoid, "a%d" % b) for b in range(BLOCKS)]
-        g_first = [fetch_with(h2[b], 0, e2[:, b, :], ALU.add, "g_first%d" % b) for b in range(BLOCKS)]
-        g = []
+        a_pre = sbuf([P, BLOCKS, V], F32, "a_pre", "raw_w2")
+        nc.vector.tensor_tensor(a_pre[:], a_both[:], ebank1[:], ALU.add)
+        a = sbuf([P, BLOCKS, V], F32, "a")
+        nc.scalar.activation(a[:], a_pre[:], ACT.Sigmoid)
+        fc = [sbuf([P, BLOCKS, V], F32, "fc%d" % d) for d in range(2)]
         for b in range(BLOCKS):
-            g.append(activate(fetch_with(h2[b], 1, g_first[b][:], ALU.add, "g_both%d" % b), ACT.Tanh, "g%d" % b))
-
-        fc0 = [fetch_with(cells[0], d, f0[d][:], ALU.mult, "fc0_%d" % d) for d in range(2)]
-        ag0 = combine(a[0][:], g[0][:], ALU.mult, "ag0")
-        m0 = combine(fc0[0][:], fc0[1][:], ALU.add, "m0")
-        fc10 = fetch_with(cells[1], 0, f1[0][:], ALU.mult, "fc1_0")
-        st0 = combine(ag0[:], m0[:], ALU.add, "st0")
-        nc.sync.dma_start(out=out[0:P, :], in_=activate(st0, ACT.Tanh, "r0")[:])
-        ag1 = combine(a[1][:], g[1][:], ALU.mult, "ag1")
-        m1 = combine(ag1[:], fc10[:], ALU.add, "m1")
-        fc11 = fetch_with(cells[1], 1, f1[1][:], ALU.mult, "fc1_1")
-        st1 = combine(fc11[:], m1[:], ALU.add, "st1")
-        nc.scalar.dma_start(out=out[P : 2 * P, :], in_=activate(st1, ACT.Tanh, "r1")[:])
+            for d in range(2):
+                nc.vector.tensor_tensor(fc[d][:, b, :], cells[b][:].indirect(pos[d][:]), f[b][d][:], ALU.mult)
+        g_first = [fetch_with(h2[b], 0, e2[:, b, :], ALU.add, "g_first%d" % b) for b in range(BLOCKS)]
+        g = [activate(fetch_with(h2[b], 1, g_first[b][:], ALU.add, "g_both%d" % b), ACT.Tanh, "g%d" % b) for b in range(BLOCKS)]
+        kept = sbuf([P, BLOCKS, V], F32, "kept", "e2")
+        nc.vector.tensor_tensor(kept[:], fc[0][:], fc[1][:], ALU.add)
+        fresh = [combine(a[:, b, :], g[b][:], ALU.mult, "fresh%d" % b) for b in range(BLOCKS)]
+        state = [combine(fresh[b][:], kept[:, b, :], ALU.add, "state%d" % b) for b in range(BLOCKS)]
+        for b in range(BLOCKS):
+            nc.sync.dma_start(out=out[b * P : (b + 1) * P, :], in_=activate(state[b], ACT.Tanh, "result%d" % b)[:])

@@ -25,10 +25,12 @@ def tile_picked_ztree_tanh_p_kernel(tc, x_words, x_scales, eT, w1, w2, w3, v1, v
     nc = tc.nc
     with ExitStack() as ctx:
         keep = ctx.enter_context(tc.tile_pool(name="keep", bufs=1))
-        hbanks = ctx.enter_context(tc.psum_pool(name="hbanks", bufs=4))
-        ebanks = ctx.enter_context(tc.psum_pool(name="ebanks", bufs=3))
+        shared = ctx.enter_context(tc.tile_pool(name="shared", bufs=1))
+        banks = ctx.enter_context(tc.psum_pool(name="banks", bufs=8))
 
         def sbuf(shape, dtype, name, tag=None):
+            if isinstance(tag, int):
+                return shared.tile(shape, dtype, name=name, offset=tag, align_bytes=64)
             return keep.tile(shape, dtype, name=name, tag=tag or name, align_bytes=64)
 
         def load_list(src, name):
@@ -36,46 +38,43 @@ def tile_picked_ztree_tanh_p_kernel(tc, x_words, x_scales, eT, w1, w2, w3, v1, v
             nc.sync.dma_start(lst[:], src)
             return lst
 
-        def load_matrix(src, name):
-            raw = sbuf([P, PACK, src.shape[1]], F32, "raw_" + name)
-            nc.sync.dma_start(out=raw[:], in_=src.rearrange("(p j) c -> p j c", j=PACK))
-            return raw
+        def load_matrix(src, name, tag=None):
+            rows = sbuf([P, PACK, src.shape[1]], F32, "raw_" + name, tag)
+            nc.sync.dma_start(out=rows[:], in_=src.rearrange("(p j) c -> p j c", j=PACK))
+            return rows
 
         def load_cells(b):
             rows = sbuf([P, S], F32, "cell%d" % b)
             nc.sync.dma_start(out=rows[:], in_=cell[b * P : (b + 1) * P, :])
             return rows
 
-        def weave(name, copies):
-            width = raw[name].shape[2]
-            woven = sbuf([P, width, PACK], BF16, "woven_" + name)
-            share = width // len(copies)
-            for part, copy in enumerate(copies):
-                cols = slice(part * share, (part + 1) * share)
-                copy(out=woven[:, cols, :].rearrange("p (c i) j -> p c j i", i=RUN), in_=raw[name][:, :, cols].rearrange("p j (c i) -> p c j i", i=RUN))
-            return woven
+        def weave(copy, dst, src):
+            copy(out=dst.rearrange("p (c i) j -> p c j i", i=RUN), in_=src.rearrange("p j (c i) -> p c j i", i=RUN))
 
-        def quantise(woven, name):
+        def woven_tile(width, name, tag=None):
+            return sbuf([P, width, PACK], BF16, "woven_" + name, tag)
+
+        def quantise(woven, name, tag=None):
             width = woven.shape[1]
-            codes = sbuf([P, width], U32, name + "_codes")
+            codes = sbuf([P, width], U32, name + "_codes", tag)
             scales = sbuf([P, width], U8, name + "_scales")
             nc.vector.quantize_mx(out=codes[:].bitcast(FP8X4), scales=scales[:], in_=woven[:].rearrange("p c j -> p (c j)"))
             return codes, scales
 
-        def product(dst, weights, first, moving):
-            cols = slice(first, first + P)
-            nc.tensor.matmul_mx(out=dst, lhsT=weights[0][:, cols].bitcast(FP8X4), lhsT_scale=weights[1][:, cols],
-                                rhs=moving[0][:].bitcast(FP8X4), rhs_scale=moving[1][:], start=True, stop=True)
+        def product(dst, weights, first, moving, cols):
+            rows = slice(first, first + P)
+            nc.tensor.matmul_mx(out=dst, lhsT=weights[0][:, rows].bitcast(FP8X4), lhsT_scale=weights[1][:, rows],
+                                rhs=moving[0][:, cols].bitcast(FP8X4), rhs_scale=moving[1][:, cols], start=True, stop=True)
 
-        def state_product(weights, first):
-            bank = hbanks.tile([P, S], F32, name="hbank")
-            product(bank[:], weights, first, picked)
+        def state_product(weights, first, cols=slice(0, S)):
+            bank = banks.tile([P, cols.stop - cols.start], F32, name="bank", tag="bank")
+            product(bank[:], weights, first, picked, cols)
             return bank
 
-        def node_product(weights):
-            bank = ebanks.tile([P, BLOCKS, V], F32, name="ebank")
+        def node_product(weights, first):
+            bank = banks.tile([P, BLOCKS, V], F32, name="bank", tag="bank")
             for b in range(BLOCKS):
-                product(bank[:, b, :], weights, b * P, nodes)
+                product(bank[:, b, :], weights, first + b * P, nodes, slice(0, V))
             return bank
 
         def leave_psum(bank, name, tag=None):
@@ -83,102 +82,134 @@ def tile_picked_ztree_tanh_p_kernel(tc, x_words, x_scales, eT, w1, w2, w3, v1, v
             nc.scalar.copy(out=rows[:], in_=bank[:])
             return rows
 
-        def fetch(window, d, name, tag=None):
-            dst = sbuf([P, V], F32, name, tag)
-            nc.vector.tensor_copy(dst[:], window[:].indirect(pos[d][:]))
-            return dst
+        def fetch(dst, window, d):
+            nc.vector.tensor_copy(dst, window[:].indirect(pos[d][:]))
 
-        def fetch_with(window, d, other, op, name, tag=None):
-            dst = sbuf([P, V], F32, name, tag)
-            nc.vector.tensor_tensor(dst[:], window[:].indirect(pos[d][:]), other, op)
-            return dst
+        def fetch_with(dst, window, d, other, op):
+            nc.vector.tensor_tensor(dst, window[:].indirect(pos[d][:]), other, op)
 
-        def combine(left, right, op, name, tag=None):
-            dst = sbuf([P, V], F32, name, tag)
-            nc.vector.tensor_tensor(dst[:], left, right, op)
-            return dst
+        def row(name, tag=None):
+            return sbuf([P, V], F32, name, tag)
 
-        def activate(src, func, name, tag=None):
-            dst = sbuf([P, V], F32, name, tag)
-            nc.scalar.activation(dst[:], src[:], func)
-            return dst
+        def pair(name, tag=None):
+            return sbuf([P, 2, V], F32, name, tag)
 
-        on_scalar, on_vector, shared = (nc.scalar.copy,), (nc.vector.tensor_copy,), (nc.vector.tensor_copy, nc.scalar.copy)
+        on_scalar, on_vector = nc.scalar.copy, nc.vector.tensor_copy
+        lo, hi = slice(0, P), slice(P, 2 * P)
 
         scale_table = sbuf([P, T], U8, "scale_table")
         nc.vector.memset(scale_table[:].bitcast(I32), 0)
         word_table = sbuf([P, T], U32, "word_table")
         nc.sync.dma_start(out=word_table[:].bitcast(I32), in_=x_words[0].rearrange("p c r -> p (c r)").bitcast(I32))
+        offs_t = load_list(offs, "offs_t")
         for q in range(4):
             nc.sync.dma_start(out=scale_table[32 * q : 32 * q + 4, :].bitcast(I32), in_=x_scales[0, 4 * q : 4 * q + 4, :].bitcast(I32))
-        offs_t = load_list(offs, "offs_t")
-        raw = {name: load_matrix(src, name) for name, src in (("v1", v1), ("v3", v3), ("w3", w3), ("e", eT))}
-        pos = [load_list(pos1, "pos1_t")]
-        raw["w1"] = load_matrix(w1, "w1")
+        raw, pos, cells = {}, [], []
+        raw["v1"] = load_matrix(v1, "v1")
+        raw["v3"] = load_matrix(v3, "v3")
+        raw["e"] = load_matrix(eT, "e")
+        raw["w3"] = load_matrix(w3, "w3")
+        pos.append(load_list(pos1, "pos1_t"))
+        raw["v2"] = load_matrix(v2, "v2", 0)
         pos.append(load_list(pos2, "pos2_t"))
-        for name, src in (("v2", v2), ("w2", w2)):
-            raw[name] = load_matrix(src, name)
-        cells = [load_cells(b) for b in range(BLOCKS)]
+        raw["w2"] = load_matrix(w2, "w2")
+        raw["w1"] = load_matrix(w1, "w1")
+        cells.append(load_cells(0))
+        cells.append(load_cells(1))
 
         warm = sbuf([P, 16], F32, "warm")
         nc.vector.memset(warm[:, 0:8], 0.0)
         nc.scalar.activation(warm[:, 8:16], warm[:, 0:8], ACT.Sigmoid)
 
-        x_bytes = sbuf([P, S], U8, "x_bytes")
+        def node_block(weights, b):
+            bank = banks.tile([P, V], F32, name="bank", tag="bank")
+            product(bank[:], weights, b * P, nodes, slice(0, V))
+            return bank
+
         x_codes = sbuf([P, S], U32, "x_codes")
+        x_bytes = sbuf([P, S], U8, "x_bytes")
         nc.vector.tensor_copy(x_codes[:], word_table[:].indirect(offs_t[:]))
         nc.vector.tensor_copy(x_bytes[:], scale_table[:].indirect(offs_t[:]))
         picked = (x_codes, x_bytes)
+        woven_v1 = [woven_tile(P, "v1_%d" % b) for b in range(BLOCKS)]
+        weave(on_scalar, woven_v1[0][:], raw["v1"][:, :, lo])
+        weave(on_scalar, woven_v1[1][:], raw["v1"][:, :, hi])
+        q_v1 = [quantise(woven_v1[b], "v1_%d" % b) for b in range(BLOCKS)]
+        halves = [slice(u * V, (u + 1) * V) for u in range(2)]
+        bank1 = [state_product(q_v1[0], 0, halves[u]) for u in range(2)] + [state_product(q_v1[1], 0)]
 
-        woven_v1 = weave("v1", on_scalar)
-        woven_v3 = weave("v3", shared)
-        q_v1 = quantise(woven_v1, "v1")
-        bank1 = [state_product(q_v1, b * P) for b in range(BLOCKS)]
-        woven_w3 = weave("w3", on_vector)
+        woven_v3 = woven_tile(N, "v3")
+        weave(on_scalar, woven_v3[:], raw["v3"][:])
+        h1 = [sbuf([P, S], F32, "h1_0")]
+        for u in range(2):
+            nc.scalar.copy(out=h1[0][:, halves[u]], in_=bank1[u][:])
+        woven_e = woven_tile(V, "e")
+        weave(on_vector, woven_e[:], raw["e"][:])
         q_v3 = quantise(woven_v3, "v3")
         bank3 = [state_product(q_v3, b * P) for b in range(BLOCKS)]
-        q_w3 = quantise(woven_w3, "w3")
-        h1 = [leave_psum(bank1[0], "h1_0")]
-        woven_e = weave("e", shared)
-        a_first = [fetch(h1[0], 0, "a_first0")]
-        h1.append(leave_psum(bank1[1], "h1_1"))
-        woven_w1 = weave("w1", shared)
         nodes = quantise(woven_e, "e")
-        ebank3 = node_product(q_w3)
-        a_first.append(fetch(h1[1], 0, "a_first1"))
-        ebank1 = node_product(quantise(woven_w1, "w1"))
-        h3 = [leave_psum(bank3[0], "h3_0")]
-        e3 = leave_psum(ebank3, "e3")
-        h3.append(leave_psum(bank3[1], "h3_1"))
-        a_both = sbuf([P, BLOCKS, V], F32, "a_both")
+        h1.append(leave_psum(bank1[2], "h1_1"))
+        woven_w3 = woven_tile(N, "w3")
+        weave(on_scalar, woven_w3[:, lo, :], raw["w3"][:, :, lo])
+        weave(on_vector, woven_w3[:, hi, :], raw["w3"][:, :, hi])
+        a_first, a_both = pair("a_first"), pair("a_both")
         for b in range(BLOCKS):
-            nc.vector.tensor_tensor(a_both[:, b, :], h1[b][:].indirect(pos[1][:]), a_first[b][:], ALU.add)
-        woven_v2 = weave("v2", on_scalar)
-        woven_w2 = weave("w2", on_scalar)
+            fetch(a_first[:, b, :], h1[b], 0)
+        q_w3 = quantise(woven_w3, "w3")
+        ebank3 = [node_block(q_w3, b) for b in range(BLOCKS)]
+        for b in range(BLOCKS):
+            fetch_with(a_both[:, b, :], h1[b], 1, a_first[:, b, :], ALU.add)
 
-        fpre = [[fetch_with(h3[0], d, e3[:, 0, :], ALU.add, "fpre0_%d" % d) for d in range(2)]]
-        fpre.append([fetch_with(h3[1], 0, e3[:, 1, :], ALU.add, "fpre1_0")])
+        woven_v2 = woven_tile(N, "v2")
+        weave(on_scalar, woven_v2[:], raw["v2"][:])
+        h3 = [leave_psum(bank3[0], "h3_0", 0)]
+        e3 = [leave_psum(ebank3[b], "e3_%d" % b, 4 * S + 4 * V * b) for b in range(BLOCKS)]
         q_v2 = quantise(woven_v2, "v2")
         bank2 = [state_product(q_v2, b * P) for b in range(BLOCKS)]
-        fpre[1].append(fetch_with(h3[1], 1, e3[:, 1, :], ALU.add, "fpre1_1", "raw_v2"))
-        ebank2 = node_product(quantise(woven_w2, "w2"))
-        f = [[activate(fpre[b][d], ACT.Sigmoid, "f%d_%d" % (b, d), "woven_v2" if b + d == 0 else None) for d in range(2)] for b in range(BLOCKS)]
-        h2 = [leave_psum(bank2[b], "h2_%d" % b) for b in range(BLOCKS)]
-        e2 = leave_psum(ebank2, "e2")
+        h3.append(leave_psum(bank3[1], "h3_1", "woven_v2"))
+        woven_w2 = woven_tile(N, "w2")
+        weave(on_scalar, woven_w2[:], raw["w2"][:])
 
-        a_pre = sbuf([P, BLOCKS, V], F32, "a_pre", "raw_w2")
-        nc.vector.tensor_tensor(a_pre[:], a_both[:], ebank1[:], ALU.add)
-        a = sbuf([P, BLOCKS, V], F32, "a")
-        nc.scalar.activation(a[:], a_pre[:], ACT.Sigmoid)
-        fc = [sbuf([P, BLOCKS, V], F32, "fc%d" % d) for d in range(2)]
+        f_pre, f = [pair("f_pre%d" % b) for b in range(BLOCKS)], [pair("f%d" % b) for b in range(BLOCKS)]
         for b in range(BLOCKS):
             for d in range(2):
-                nc.vector.tensor_tensor(fc[d][:, b, :], cells[b][:].indirect(pos[d][:]), f[b][d][:], ALU.mult)
-        g_first = [fetch_with(h2[b], 0, e2[:, b, :], ALU.add, "g_first%d" % b) for b in range(BLOCKS)]
-        g = [activate(fetch_with(h2[b], 1, g_first[b][:], ALU.add, "g_both%d" % b), ACT.Tanh, "g%d" % b) for b in range(BLOCKS)]
-        kept = sbuf([P, BLOCKS, V], F32, "kept", "e2")
-        nc.vector.tensor_tensor(kept[:], fc[0][:], fc[1][:], ALU.add)
-        fresh = [combine(a[:, b, :], g[b][:], ALU.mult, "fresh%d" % b) for b in range(BLOCKS)]
-        state = [combine(fresh[b][:], kept[:, b, :], ALU.add, "state%d" % b) for b in range(BLOCKS)]
+                fetch_with(f_pre[b][:, d, :], h3[b], d, e3[b][:], ALU.add)
+        q_w2 = quantise(woven_w2, "w2")
+        ebank2 = [node_block(q_w2, b) for b in range(BLOCKS)]
+        nc.scalar.activation(f[0][:], f_pre[0][:], ACT.Sigmoid)
+        h2 = [leave_psum(bank2[0], "h2_0")]
+        woven_w1 = woven_tile(N, "w1")
+        weave(on_scalar, woven_w1[:], raw["w1"][:])
+        e2 = [leave_psum(ebank2[0], "e2_0")]
+        h2.append(leave_psum(bank2[1], "h2_1", "raw_w1"))
+        e2.append(leave_psum(ebank2[1], "e2_1"))
+        nc.scalar.activation(f[1][:], f_pre[1][:], ACT.Sigmoid)
+
+        fc0 = pair("fc0")
+        for d in range(2):
+            fetch_with(fc0[:, d, :], cells[0], d, f[0][:, d, :], ALU.mult)
+        ebank1 = node_product(quantise(woven_w1, "w1"), 0)
+        g_first, g_pre, g = pair("g_first"), pair("g_pre"), pair("g")
+        fetch_with(g_first[:, 0, :], h2[0], 0, e2[0][:], ALU.add)
+        kept0 = row("kept0", "woven_w1")
+        nc.vector.tensor_tensor(kept0[:], fc0[:, 0, :], fc0[:, 1, :], ALU.add)
+        fetch_with(g_first[:, 1, :], h2[1], 0, e2[1][:], ALU.add)
+        a_pre, a = pair("a_pre"), pair("a")
+        nc.vector.tensor_tensor(a_pre[:], a_both[:], ebank1[:], ALU.add)
+        nc.scalar.activation(a[:], a_pre[:], ACT.Sigmoid)
         for b in range(BLOCKS):
-            nc.sync.dma_start(out=out[b * P : (b + 1) * P, :], in_=activate(state[b], ACT.Tanh, "result%d" % b)[:])
+            fetch_with(g_pre[:, b, :], h2[b], 1, g_first[:, b, :], ALU.add)
+            nc.scalar.activation(g[:, b, :], g_pre[:, b, :], ACT.Tanh)
+        fc1 = pair("fc1", "a_both")
+        for d in range(2):
+            fetch_with(fc1[:, d, :], cells[1], d, f[1][:, d, :], ALU.mult)
+        fresh0, kept1, fresh1 = row("fresh0"), row("kept1"), row("fresh1")
+        nc.vector.tensor_tensor(fresh0[:], a[:, 0, :], g[:, 0, :], ALU.mult)
+        nc.vector.tensor_tensor(kept1[:], fc1[:, 0, :], fc1[:, 1, :], ALU.add)
+        nc.vector.tensor_tensor(fresh1[:], a[:, 1, :], g[:, 1, :], ALU.mult)
+        terms = [(kept0, fresh0), (kept1, fresh1)]
+        for b in range(BLOCKS):
+            state, result = row("state%d" % b), row("result%d" % b)
+            nc.vector.tensor_tensor(state[:], terms[b][0][:], terms[b][1][:], ALU.add)
+            nc.scalar.activation(result[:], state[:], ACT.Tanh)
+            nc.sync.dma_start(out=out[b * P : (b + 1) * P, :], in_=result[:])

@@ -1,6 +1,7 @@
 from contextlib import ExitStack
 
 import concourse.mybir as mybir
+from concourse.masks import make_identity
 
 K, T, S, V, N = 512, 1024, 512, 256, 256
 FLOPS = 2 * K * N * 3 * (V + S)
@@ -94,6 +95,11 @@ def tile_picked_ztree_tanh_p_kernel(tc, x_words, x_scales, eT, w1, w2, w3, v1, v
         def pair(name, tag=None):
             return sbuf([P, 2, V], F32, name, tag)
 
+        def turn(dst, term, start, stop):
+            nc.tensor.matmul(dst, term, identity[:], start=start, stop=stop, is_transpose=True)
+
+        identity = sbuf([P, P], F32, "identity")
+        make_identity(nc, identity[:])
         on_scalar, on_vector = nc.scalar.copy, nc.vector.tensor_copy
         lo, hi = slice(0, P), slice(P, 2 * P)
 
@@ -106,14 +112,14 @@ def tile_picked_ztree_tanh_p_kernel(tc, x_words, x_scales, eT, w1, w2, w3, v1, v
             nc.sync.dma_start(out=scale_table[32 * q : 32 * q + 4, :].bitcast(I32), in_=x_scales[0, 4 * q : 4 * q + 4, :].bitcast(I32))
         raw, pos, cells = {}, [], []
         raw["v1"] = load_matrix(v1, "v1")
-        raw["v3"] = load_matrix(v3, "v3")
+        raw["v2"] = load_matrix(v2, "v2")
         raw["e"] = load_matrix(eT, "e")
-        raw["w3"] = load_matrix(w3, "w3")
         pos.append(load_list(pos1, "pos1_t"))
-        raw["v2"] = load_matrix(v2, "v2", 0)
         pos.append(load_list(pos2, "pos2_t"))
-        raw["w2"] = load_matrix(w2, "w2")
-        raw["w1"] = load_matrix(w1, "w1")
+        raw["v3"] = load_matrix(v3, "v3", 0)
+        raw["w3"] = load_matrix(w3, "w3")
+        raw["w2"] = load_matrix(w2, "w2", 4096)
+        raw["w1"] = load_matrix(w1, "w1", 8192)
         cells.append(load_cells(0))
         cells.append(load_cells(1))
 
@@ -138,78 +144,110 @@ def tile_picked_ztree_tanh_p_kernel(tc, x_words, x_scales, eT, w1, w2, w3, v1, v
         halves = [slice(u * V, (u + 1) * V) for u in range(2)]
         bank1 = [state_product(q_v1[0], 0, halves[u]) for u in range(2)] + [state_product(q_v1[1], 0)]
 
-        woven_v3 = woven_tile(N, "v3")
-        weave(on_scalar, woven_v3[:], raw["v3"][:])
+        cols = [lo, hi]
+
+        def psum(shape):
+            return banks.tile(shape, F32, name="bank", tag="bank")
+
+        def add_turned(bank, b, term, start=False, stop=False):
+            for u in range(2):
+                turn(bank[:, u, cols[b]], term[:, cols[u]], start and u == 0, stop and u == 1)
+
+        woven_v2 = woven_tile(N, "v2")
+        weave(on_scalar, woven_v2[:], raw["v2"][:])
         h1 = [sbuf([P, S], F32, "h1_0")]
         for u in range(2):
             nc.scalar.copy(out=h1[0][:, halves[u]], in_=bank1[u][:])
         woven_e = woven_tile(V, "e")
         weave(on_vector, woven_e[:], raw["e"][:])
-        q_v3 = quantise(woven_v3, "v3")
-        bank3 = [state_product(q_v3, b * P) for b in range(BLOCKS)]
-        nodes = quantise(woven_e, "e")
-        h1.append(leave_psum(bank1[2], "h1_1"))
-        woven_w3 = woven_tile(N, "w3")
-        weave(on_scalar, woven_w3[:, lo, :], raw["w3"][:, :, lo])
-        weave(on_vector, woven_w3[:, hi, :], raw["w3"][:, :, hi])
-        a_first, a_both = pair("a_first"), pair("a_both")
-        for b in range(BLOCKS):
-            fetch(a_first[:, b, :], h1[b], 0)
-        q_w3 = quantise(woven_w3, "w3")
-        ebank3 = [node_block(q_w3, b) for b in range(BLOCKS)]
-        for b in range(BLOCKS):
-            fetch_with(a_both[:, b, :], h1[b], 1, a_first[:, b, :], ALU.add)
-
-        woven_v2 = woven_tile(N, "v2")
-        weave(on_scalar, woven_v2[:], raw["v2"][:])
-        h3 = [leave_psum(bank3[0], "h3_0", 0)]
-        e3 = [leave_psum(ebank3[b], "e3_%d" % b, 4 * S + 4 * V * b) for b in range(BLOCKS)]
         q_v2 = quantise(woven_v2, "v2")
         bank2 = [state_product(q_v2, b * P) for b in range(BLOCKS)]
-        h3.append(leave_psum(bank3[1], "h3_1", "woven_v2"))
-        woven_w2 = woven_tile(N, "w2")
+        nodes = quantise(woven_e, "e")
+        h1.append(leave_psum(bank1[2], "h1_1"))
+        a_bank = psum([P, 2, N])
+        for b in range(BLOCKS):
+            for d in range(2):
+                term = row("a_term%d_%d" % (b, d))
+                fetch(term[:], h1[b], d)
+                add_turned(a_bank, b, term, start=(b + d == 0))
+        woven_v3, woven_w3 = woven_tile(N, "v3"), woven_tile(N, "w3")
+        weave(on_scalar, woven_v3[:], raw["v3"][:])
+        h2 = [leave_psum(bank2[b], "h2_%d" % b, 4 * S * b) for b in range(BLOCKS)]
+        q_v3 = quantise(woven_v3, "v3")
+        bank3 = [state_product(q_v3, b * P) for b in range(BLOCKS)]
+        weave(on_vector, woven_w3[:], raw["w3"][:])
+        woven_w2, woven_w1 = woven_tile(N, "w2"), woven_tile(N, "w1")
         weave(on_scalar, woven_w2[:], raw["w2"][:])
+        weave(on_scalar, woven_w1[:], raw["w1"][:])
+        h3 = [leave_psum(bank3[0], "h3_0", 4096)]
+        g_bank, g_first = psum([P, 2, N]), []
+
+        def g_term(b, d, tag=None):
+            term = row("g_term%d_%d" % (b, d), tag)
+            if d == 0:
+                fetch(term[:], h2[b], d)
+                g_first.append(term)
+            else:
+                fetch_with(term[:], h2[b], d, g_first[b][:], ALU.add)
+                add_turned(g_bank, b, term, start=(b == 0))
+
+        g_term(0, 0)
+        q_w3 = quantise(woven_w3, "w3")
+        ebank3 = [node_block(q_w3, b) for b in range(BLOCKS)]
+        g_term(0, 1, "raw_w3")
+        ebank2 = node_product(quantise(woven_w2, "w2"), 0)
+        g_term(1, 0, 4096 + 4 * S)
+        ebank1 = node_product(quantise(woven_w1, "w1"), 0)
+        g_term(1, 1, 8192 + 4 * S)
+        e3 = [leave_psum(ebank3[b], "e3_%d" % b, 8192 + 4 * V * b) for b in range(BLOCKS)]
+        h3.append(leave_psum(bank3[1], "h3_1", "woven_w1"))
+        e2 = leave_psum(ebank2, "e2", 8192 + 4 * S + 4 * V)
+        e1 = leave_psum(ebank1, "e1")
+        for bank, e in ((g_bank, e2), (a_bank, e1)):
+            for b in range(BLOCKS):
+                add_turned(bank, b, e[:, b, :], stop=(b == BLOCKS - 1))
 
         f_pre, f = [pair("f_pre%d" % b) for b in range(BLOCKS)], [pair("f%d" % b) for b in range(BLOCKS)]
         for b in range(BLOCKS):
             for d in range(2):
                 fetch_with(f_pre[b][:, d, :], h3[b], d, e3[b][:], ALU.add)
-        q_w2 = quantise(woven_w2, "w2")
-        ebank2 = [node_block(q_w2, b) for b in range(BLOCKS)]
+        a_turned, g_turned = pair("a_turned"), pair("g_turned")
         nc.scalar.activation(f[0][:], f_pre[0][:], ACT.Sigmoid)
-        h2 = [leave_psum(bank2[0], "h2_0")]
-        woven_w1 = woven_tile(N, "w1")
-        weave(on_scalar, woven_w1[:], raw["w1"][:])
-        e2 = [leave_psum(ebank2[0], "e2_0")]
-        h2.append(leave_psum(bank2[1], "h2_1", "raw_w1"))
-        e2.append(leave_psum(ebank2[1], "e2_1"))
+        nc.scalar.activation(g_turned[:], g_bank[:], ACT.Tanh)
+        nc.scalar.activation(a_turned[:], a_bank[:], ACT.Sigmoid)
         nc.scalar.activation(f[1][:], f_pre[1][:], ACT.Sigmoid)
 
-        fc0 = pair("fc0")
+        fc = [pair("fc%d" % b) for b in range(BLOCKS)]
+        kept_bank = psum([P, 2, P])
         for d in range(2):
-            fetch_with(fc0[:, d, :], cells[0], d, f[0][:, d, :], ALU.mult)
-        ebank1 = node_product(quantise(woven_w1, "w1"), 0)
-        g_first, g_pre, g = pair("g_first"), pair("g_pre"), pair("g")
-        fetch_with(g_first[:, 0, :], h2[0], 0, e2[0][:], ALU.add)
-        kept0 = row("kept0", "woven_w1")
-        nc.vector.tensor_tensor(kept0[:], fc0[:, 0, :], fc0[:, 1, :], ALU.add)
-        fetch_with(g_first[:, 1, :], h2[1], 0, e2[1][:], ALU.add)
-        a_pre, a = pair("a_pre"), pair("a")
-        nc.vector.tensor_tensor(a_pre[:], a_both[:], ebank1[:], ALU.add)
-        nc.scalar.activation(a[:], a_pre[:], ACT.Sigmoid)
-        for b in range(BLOCKS):
-            fetch_with(g_pre[:, b, :], h2[b], 1, g_first[:, b, :], ALU.add)
-            nc.scalar.activation(g[:, b, :], g_pre[:, b, :], ACT.Tanh)
-        fc1 = pair("fc1", "a_both")
-        for d in range(2):
-            fetch_with(fc1[:, d, :], cells[1], d, f[1][:, d, :], ALU.mult)
-        fresh0, kept1, fresh1 = row("fresh0"), row("kept1"), row("fresh1")
-        nc.vector.tensor_tensor(fresh0[:], a[:, 0, :], g[:, 0, :], ALU.mult)
-        nc.vector.tensor_tensor(kept1[:], fc1[:, 0, :], fc1[:, 1, :], ALU.add)
-        nc.vector.tensor_tensor(fresh1[:], a[:, 1, :], g[:, 1, :], ALU.mult)
-        terms = [(kept0, fresh0), (kept1, fresh1)]
-        for b in range(BLOCKS):
-            state, result = row("state%d" % b), row("result%d" % b)
-            nc.vector.tensor_tensor(state[:], terms[b][0][:], terms[b][1][:], ALU.add)
+            fetch_with(fc[0][:, d, :], cells[0], d, f[0][:, d, :], ALU.mult)
+            add_turned(kept_bank, 0, fc[0][:, d, :], start=(d == 0), stop=(d == 1))
+        kept0_turned = leave_psum(kept_bank, "kept0_turned")
+        fresh_turned = pair("fresh_turned")
+        nc.vector.tensor_tensor(fresh_turned[:], a_turned[:], g_turned[:], ALU.mult)
+        state_bank = [psum([P, V]) for b in range(BLOCKS)]
+        for u in range(2):
+            turn(state_bank[1][:, cols[u]], fresh_turned[:, u, hi], True, True)
+        for u in range(2):
+            turn(state_bank[0][:, cols[u]], fresh_turned[:, u, lo], u == 0, False)
+        for u in range(2):
+            turn(state_bank[0][:, cols[u]], kept0_turned[:, u, :], False, u == 1)
+        fetch_with(fc[1][:, 0, :], cells[1], 0, f[1][:, 0, :], ALU.mult)
+        last = [sbuf([P, P], F32, "last0"), None]
+
+        def fetch_last(u):
+            nc.vector.tensor_tensor(last[u][:], cells[1][:].indirect(pos[1][:, 8 * u : 8 * (u + 1)]), f[1][:, 1, cols[u]], ALU.mult)
+
+        fetch_last(0)
+        part1 = row("part1")
+        nc.vector.tensor_tensor(part1[:], fc[1][:, 0, :], state_bank[1][:], ALU.add)
+        last[1] = sbuf([P, P], F32, "last1", "fresh_turned")
+        fetch_last(1)
+        result0 = row("result0")
+        nc.scalar.activation(result0[:], state_bank[0][:], ACT.Tanh)
+        nc.sync.dma_start(out=out[lo, :], in_=result0[:])
+        for u in range(2):
+            state, result = sbuf([P, P], F32, "state1_%d" % u), sbuf([P, P], F32, "result1_%d" % u)
+            nc.vector.tensor_tensor(state[:], part1[:, cols[u]], last[u][:], ALU.add)
             nc.scalar.activation(result[:], state[:], ACT.Tanh)
-            nc.sync.dma_start(out=out[b * P : (b + 1) * P, :], in_=result[:])
+            nc.sync.dma_start(out=out[hi, cols[u]], in_=result[:])

@@ -116,7 +116,7 @@ def tile_picked_ztree_tanh_p_kernel(tc, x_words, x_scales, eT, w1, w2, w3, v1, v
         raw["e"] = load_matrix(eT, "e")
         pos.append(load_list(pos1, "pos1_t"))
         pos.append(load_list(pos2, "pos2_t"))
-        raw["v3"] = load_matrix(v3, "v3", 0)
+        raw["v3"] = load_matrix(v3, "v3")
         raw["w3"] = load_matrix(w3, "w3")
         raw["w2"] = load_matrix(w2, "w2", 4096)
         raw["w1"] = load_matrix(w1, "w1", 8192)
@@ -146,6 +146,9 @@ def tile_picked_ztree_tanh_p_kernel(tc, x_words, x_scales, eT, w1, w2, w3, v1, v
 
         cols = [lo, hi]
 
+        def weave_on_gpsimd(dst, src):
+            nc.gpsimd.tensor_scalar(dst, src.rearrange("p j c -> p c j"), 1.0, 0.0, ALU.mult, ALU.add)
+
         def psum(shape):
             return banks.tile(shape, F32, name="bank", tag="bank")
 
@@ -171,11 +174,13 @@ def tile_picked_ztree_tanh_p_kernel(tc, x_words, x_scales, eT, w1, w2, w3, v1, v
                 fetch(term[:], h1[b], d)
                 add_turned(a_bank, b, term, start=(b + d == 0))
         woven_v3, woven_w3 = woven_tile(N, "v3"), woven_tile(N, "w3")
-        weave(on_scalar, woven_v3[:], raw["v3"][:])
-        h2 = [leave_psum(bank2[b], "h2_%d" % b, 4 * S * b) for b in range(BLOCKS)]
+        for part in cols:
+            weave_on_gpsimd(woven_v3[:, part, :], raw["v3"][:, :, part])
+        weave_on_gpsimd(woven_w3[:, lo, :], raw["w3"][:, :, lo])
+        h2 = [leave_psum(bank2[b], "h2_%d" % b) for b in range(BLOCKS)]
         q_v3 = quantise(woven_v3, "v3")
         bank3 = [state_product(q_v3, b * P) for b in range(BLOCKS)]
-        weave(on_vector, woven_w3[:], raw["w3"][:])
+        weave(on_scalar, woven_w3[:, hi, :], raw["w3"][:, :, hi])
         woven_w2, woven_w1 = woven_tile(N, "w2"), woven_tile(N, "w1")
         weave(on_scalar, woven_w2[:], raw["w2"][:])
         weave(on_scalar, woven_w1[:], raw["w1"][:])

@@ -98,8 +98,6 @@ def tile_picked_ztree_tanh_p_kernel(tc, x_words, x_scales, eT, w1, w2, w3, v1, v
         def turn(dst, term, start, stop):
             nc.tensor.matmul(dst, term, identity[:], start=start, stop=stop, is_transpose=True)
 
-        identity = sbuf([P, P], F32, "identity")
-        make_identity(nc, identity[:])
         on_scalar, on_vector = nc.scalar.copy, nc.vector.tensor_copy
         lo, hi = slice(0, P), slice(P, 2 * P)
 
@@ -116,8 +114,8 @@ def tile_picked_ztree_tanh_p_kernel(tc, x_words, x_scales, eT, w1, w2, w3, v1, v
         raw["e"] = load_matrix(eT, "e")
         pos.append(load_list(pos1, "pos1_t"))
         pos.append(load_list(pos2, "pos2_t"))
-        raw["v3"] = load_matrix(v3, "v3")
-        raw["w3"] = load_matrix(w3, "w3")
+        raw["v3"] = load_matrix(v3, "v3", 12288)
+        raw["w3"] = load_matrix(w3, "w3", 0)
         raw["w2"] = load_matrix(w2, "w2", 4096)
         raw["w1"] = load_matrix(w1, "w1", 8192)
         cells.append(load_cells(0))
@@ -126,6 +124,9 @@ def tile_picked_ztree_tanh_p_kernel(tc, x_words, x_scales, eT, w1, w2, w3, v1, v
         warm = sbuf([P, 16], F32, "warm")
         nc.vector.memset(warm[:, 0:8], 0.0)
         nc.scalar.activation(warm[:, 8:16], warm[:, 0:8], ACT.Sigmoid)
+        identity = sbuf([P, P], F32, "identity")
+        nc.vector.memset(identity[:], 0.0)
+        make_identity(nc, identity[:], nomemset=True)
 
         def node_block(weights, b):
             bank = banks.tile([P, V], F32, name="bank", tag="bank")
@@ -167,43 +168,46 @@ def tile_picked_ztree_tanh_p_kernel(tc, x_words, x_scales, eT, w1, w2, w3, v1, v
         bank2 = [state_product(q_v2, b * P) for b in range(BLOCKS)]
         nodes = quantise(woven_e, "e")
         h1.append(leave_psum(bank1[2], "h1_1"))
-        a_bank = psum([P, 2, N])
+        a_bank, g_bank = psum([P, 2, N]), psum([P, 2, N])
+
+        def gate_term(bank, window, b, d, name, tag=None):
+            term = row("%s%d%d" % (name, b, d), tag)
+            fetch(term[:], window[b], d)
+            add_turned(bank, b, term, start=(b + d == 0))
+
+        def g_first(b, tag):
+            term = row("g%d0" % b, tag)
+            fetch(term[:], h2[b], 0)
+            return term
+
+        def g_second(b, first, tag):
+            term = row("g%d1" % b, tag)
+            fetch_with(term[:], h2[b], 1, first[:], ALU.add)
+            add_turned(g_bank, b, term, start=(b == 0))
+
+        woven_v3, woven_w3 = woven_tile(N, "v3"), woven_tile(N, "w3")
+        weave(on_scalar, woven_v3[:, lo, :], raw["v3"][:, :, lo])
+        weave_on_gpsimd(woven_v3[:, hi, :], raw["v3"][:, :, hi])
+        for part in cols:
+            weave_on_gpsimd(woven_w3[:, part, :], raw["w3"][:, :, part])
         for b in range(BLOCKS):
             for d in range(2):
-                term = row("a_term%d_%d" % (b, d))
-                fetch(term[:], h1[b], d)
-                add_turned(a_bank, b, term, start=(b + d == 0))
-        woven_v3, woven_w3 = woven_tile(N, "v3"), woven_tile(N, "w3")
-        for part in cols:
-            weave_on_gpsimd(woven_v3[:, part, :], raw["v3"][:, :, part])
-        weave_on_gpsimd(woven_w3[:, lo, :], raw["w3"][:, :, lo])
-        h2 = [leave_psum(bank2[b], "h2_%d" % b) for b in range(BLOCKS)]
+                gate_term(a_bank, h1, b, d, "a")
+        h2 = [leave_psum(bank2[b], "h2_%d" % b, 12288 + 4 * S * b) for b in range(BLOCKS)]
+        first = g_first(0, None)
         q_v3 = quantise(woven_v3, "v3")
         bank3 = [state_product(q_v3, b * P) for b in range(BLOCKS)]
-        weave(on_scalar, woven_w3[:, hi, :], raw["w3"][:, :, hi])
+        q_w3 = quantise(woven_w3, "w3")
+        ebank3 = [node_block(q_w3, b) for b in range(BLOCKS)]
         woven_w2, woven_w1 = woven_tile(N, "w2"), woven_tile(N, "w1")
         weave(on_scalar, woven_w2[:], raw["w2"][:])
         weave(on_scalar, woven_w1[:], raw["w1"][:])
         h3 = [leave_psum(bank3[0], "h3_0", 4096)]
-        g_bank, g_first = psum([P, 2, N]), []
-
-        def g_term(b, d, tag=None):
-            term = row("g_term%d_%d" % (b, d), tag)
-            if d == 0:
-                fetch(term[:], h2[b], d)
-                g_first.append(term)
-            else:
-                fetch_with(term[:], h2[b], d, g_first[b][:], ALU.add)
-                add_turned(g_bank, b, term, start=(b == 0))
-
-        g_term(0, 0)
-        q_w3 = quantise(woven_w3, "w3")
-        ebank3 = [node_block(q_w3, b) for b in range(BLOCKS)]
-        g_term(0, 1, "raw_w3")
+        g_second(0, first, 0)
         ebank2 = node_product(quantise(woven_w2, "w2"), 0)
-        g_term(1, 0, 4096 + 4 * S)
+        first = g_first(1, 4096 + 4 * S)
         ebank1 = node_product(quantise(woven_w1, "w1"), 0)
-        g_term(1, 1, 8192 + 4 * S)
+        g_second(1, first, 8192 + 4 * S)
         e3 = [leave_psum(ebank3[b], "e3_%d" % b, 8192 + 4 * V * b) for b in range(BLOCKS)]
         h3.append(leave_psum(bank3[1], "h3_1", "woven_w1"))
         e2 = leave_psum(ebank2, "e2", 8192 + 4 * S + 4 * V)

@@ -20,6 +20,10 @@ P = 128
 PACK = 4
 RUN = 4
 BLOCKS = N // P
+BANK = 2048
+RAW = PACK * N * 4
+ROW = V * 4
+E_SHARE, V3_SHARE, W3_SHARE, W2_SHARE = 160, 160, 144, 160
 
 
 def tile_picked_ztree_tanh_p_kernel(tc, x_words, x_scales, eT, w1, w2, w3, v1, v2, v3, cell, offs, pos1, pos2, out):
@@ -27,21 +31,24 @@ def tile_picked_ztree_tanh_p_kernel(tc, x_words, x_scales, eT, w1, w2, w3, v1, v
     with ExitStack() as ctx:
         keep = ctx.enter_context(tc.tile_pool(name="keep", bufs=1))
         shared = ctx.enter_context(tc.tile_pool(name="shared", bufs=1))
-        banks = ctx.enter_context(tc.psum_pool(name="banks", bufs=8))
+        banks = ctx.enter_context(tc.psum_pool(name="banks", bufs=1))
 
-        def sbuf(shape, dtype, name, tag=None):
-            if isinstance(tag, int):
-                return shared.tile(shape, dtype, name=name, offset=tag, align_bytes=64)
-            return keep.tile(shape, dtype, name=name, tag=tag or name, align_bytes=64)
+        def sbuf(shape, dtype, name, at=None):
+            if at is None:
+                return keep.tile(shape, dtype, name=name, align_bytes=64)
+            return shared.tile(shape, dtype, name=name, offset=at, align_bytes=64)
+
+        def psum(shape, name, bank):
+            return banks.tile(shape, F32, name=name, offset=bank * BANK)
 
         def load_list(src, name):
             lst = keep.tile(list(src.shape), U16, name=name)
             nc.sync.dma_start(lst[:], src)
             return lst
 
-        def load_matrix(src, name, tag=None):
-            rows = sbuf([P, PACK, src.shape[1]], F32, "raw_" + name, tag)
-            nc.sync.dma_start(out=rows[:], in_=src.rearrange("(p j) c -> p j c", j=PACK))
+        def load_matrix(src, name, queue=nc.sync):
+            rows = sbuf([P, PACK, N], F32, "raw_" + name, place[name])
+            queue.dma_start(out=rows[:], in_=src.rearrange("(p j) c -> p j c", j=PACK))
             return rows
 
         def load_cells(b):
@@ -50,76 +57,74 @@ def tile_picked_ztree_tanh_p_kernel(tc, x_words, x_scales, eT, w1, w2, w3, v1, v
             return rows
 
         def weave(copy, dst, src):
-            copy(out=dst.rearrange("p (c i) j -> p c j i", i=RUN), in_=src.rearrange("p j (c i) -> p c j i", i=RUN))
+            copy(out=dst.rearrange("p (c i j) -> p c j i", i=RUN, j=PACK), in_=src.rearrange("p j (c i) -> p c j i", i=RUN))
 
-        def woven_tile(width, name, tag=None):
-            return sbuf([P, width, PACK], BF16, "woven_" + name, tag)
+        def weave_on_gpsimd(dst, src):
+            nc.gpsimd.tensor_scalar(dst.rearrange("p (c j) -> p c j", j=PACK), src.rearrange("p j c -> p c j"), 1.0, 0.0, ALU.mult, ALU.add)
 
-        def quantise(woven, name, tag=None):
-            width = woven.shape[1]
-            codes = sbuf([P, width], U32, name + "_codes", tag)
-            scales = sbuf([P, width], U8, name + "_scales")
-            nc.vector.quantize_mx(out=codes[:].bitcast(FP8X4), scales=scales[:], in_=woven[:].rearrange("p c j -> p (c j)"))
+        def woven_cols(tile, first, count):
+            return tile[:, PACK * first : PACK * (first + count)]
+
+        def mx_tiles(name, width):
+            return sbuf([P, width], U32, name + "_codes"), sbuf([P, width], U8, name + "_scales")
+
+        def quantise(woven, name):
+            codes, scales = mx_tiles(name, woven.shape[1] // PACK)
+            nc.vector.quantize_mx(out=codes[:].bitcast(FP8X4), scales=scales[:], in_=woven)
             return codes, scales
 
-        def product(dst, weights, first, moving, cols):
-            rows = slice(first, first + P)
+        def product(dst, weights, rows, moving, cols):
             nc.tensor.matmul_mx(out=dst, lhsT=weights[0][:, rows].bitcast(FP8X4), lhsT_scale=weights[1][:, rows],
                                 rhs=moving[0][:, cols].bitcast(FP8X4), rhs_scale=moving[1][:, cols], start=True, stop=True)
 
-        def state_product(weights, first, cols=slice(0, S)):
-            bank = banks.tile([P, cols.stop - cols.start], F32, name="bank", tag="bank")
-            product(bank[:], weights, first, picked, cols)
-            return bank
+        def state_product(weights, rows, name, bank, cols=slice(0, S)):
+            dst = psum([P, cols.stop - cols.start], name, bank)
+            product(dst[:], weights, rows, picked, cols)
+            return dst
 
-        def node_product(weights, first):
-            bank = banks.tile([P, BLOCKS, V], F32, name="bank", tag="bank")
-            for b in range(BLOCKS):
-                product(bank[:, b, :], weights, first + b * P, nodes, slice(0, V))
-            return bank
-
-        def leave_psum(bank, name, tag=None):
-            rows = sbuf(list(bank.shape), F32, name, tag)
-            nc.scalar.copy(out=rows[:], in_=bank[:])
+        def leave_psum(src, name, at=None):
+            rows = sbuf(list(src.shape), F32, name, at)
+            nc.scalar.copy(out=rows[:], in_=src[:])
             return rows
 
-        def fetch(dst, window, d):
-            nc.vector.tensor_copy(dst, window[:].indirect(pos[d][:]))
-
-        def fetch_with(dst, window, d, other, op):
-            nc.vector.tensor_tensor(dst, window[:].indirect(pos[d][:]), other, op)
-
-        def row(name, tag=None):
-            return sbuf([P, V], F32, name, tag)
-
-        def pair(name, tag=None):
-            return sbuf([P, 2, V], F32, name, tag)
+        def fetch_with(dst, window, offsets, other, op):
+            nc.vector.tensor_tensor(dst, window[:].indirect(offsets), other, op)
 
         def turn(dst, term, start, stop):
             nc.tensor.matmul(dst, term, identity[:], start=start, stop=stop, is_transpose=True)
 
+        def add_turned(sums, term, start=False, stop=False):
+            for u in range(2):
+                turn(sums[:, u, :], term[:, cols[u]], start and u == 0, stop and u == 1)
+
+        def gate_term(sums, window, d, term, start=False):
+            nc.vector.tensor_copy(term, window[:].indirect(pos[d][:]))
+            add_turned(sums, term, start=start)
+
+        def pair(name, at=None):
+            return sbuf([P, 2, V], F32, name, at)
+
         on_scalar, on_vector = nc.scalar.copy, nc.vector.tensor_copy
         lo, hi = slice(0, P), slice(P, 2 * P)
+        cols = [lo, hi]
+        everyone = slice(0, V)
+        place = {name: (3 * i + 1) * RAW for i, name in enumerate(("v1", "v2", "e", "v3", "w3", "w1", "w2", "g_turned"))}
 
         scale_table = sbuf([P, T], U8, "scale_table")
         nc.vector.memset(scale_table[:].bitcast(I32), 0)
+        offs_t = load_list(offs, "offs_t")
+        raw = {"v1": load_matrix(v1, "v1", nc.scalar)}
+        for q in range(4):
+            queue = nc.sync if q < 2 else nc.scalar
+            queue.dma_start(out=scale_table[32 * q : 32 * q + 4, :].bitcast(I32), in_=x_scales[0, 4 * q : 4 * q + 4, :].bitcast(I32))
         word_table = sbuf([P, T], U32, "word_table")
         nc.sync.dma_start(out=word_table[:].bitcast(I32), in_=x_words[0].rearrange("p c r -> p (c r)").bitcast(I32))
-        offs_t = load_list(offs, "offs_t")
-        for q in range(4):
-            nc.sync.dma_start(out=scale_table[32 * q : 32 * q + 4, :].bitcast(I32), in_=x_scales[0, 4 * q : 4 * q + 4, :].bitcast(I32))
-        raw, pos, cells = {}, [], []
-        raw["v1"] = load_matrix(v1, "v1")
+        pos = [load_list(pos1, "pos1_t")]
         raw["v2"] = load_matrix(v2, "v2")
-        raw["e"] = load_matrix(eT, "e")
-        pos.append(load_list(pos1, "pos1_t"))
         pos.append(load_list(pos2, "pos2_t"))
-        raw["v3"] = load_matrix(v3, "v3", 12288)
-        raw["w3"] = load_matrix(w3, "w3", 0)
-        raw["w2"] = load_matrix(w2, "w2", 4096)
-        raw["w1"] = load_matrix(w1, "w1", 8192)
-        cells.append(load_cells(0))
-        cells.append(load_cells(1))
+        for name, src in (("e", eT), ("v3", v3), ("w3", w3), ("w1", w1), ("w2", w2)):
+            raw[name] = load_matrix(src, name)
+        cells = [load_cells(b) for b in range(BLOCKS)]
 
         warm = sbuf([P, 16], F32, "warm")
         nc.vector.memset(warm[:, 0:8], 0.0)
@@ -128,135 +133,128 @@ def tile_picked_ztree_tanh_p_kernel(tc, x_words, x_scales, eT, w1, w2, w3, v1, v
         nc.vector.memset(identity[:], 0.0)
         make_identity(nc, identity[:], nomemset=True)
 
-        def node_block(weights, b):
-            bank = banks.tile([P, V], F32, name="bank", tag="bank")
-            product(bank[:], weights, b * P, nodes, slice(0, V))
-            return bank
-
         x_codes = sbuf([P, S], U32, "x_codes")
         x_bytes = sbuf([P, S], U8, "x_bytes")
-        nc.vector.tensor_copy(x_codes[:], word_table[:].indirect(offs_t[:]))
-        nc.vector.tensor_copy(x_bytes[:], scale_table[:].indirect(offs_t[:]))
         picked = (x_codes, x_bytes)
-        woven_v1 = [woven_tile(P, "v1_%d" % b) for b in range(BLOCKS)]
-        weave(on_scalar, woven_v1[0][:], raw["v1"][:, :, lo])
-        weave(on_scalar, woven_v1[1][:], raw["v1"][:, :, hi])
-        q_v1 = [quantise(woven_v1[b], "v1_%d" % b) for b in range(BLOCKS)]
-        halves = [slice(u * V, (u + 1) * V) for u in range(2)]
-        bank1 = [state_product(q_v1[0], 0, halves[u]) for u in range(2)] + [state_product(q_v1[1], 0)]
-
-        cols = [lo, hi]
-
-        def weave_on_gpsimd(dst, src):
-            nc.gpsimd.tensor_scalar(dst, src.rearrange("p j c -> p c j"), 1.0, 0.0, ALU.mult, ALU.add)
-
-        def psum(shape):
-            return banks.tile(shape, F32, name="bank", tag="bank")
-
-        def add_turned(bank, b, term, start=False, stop=False):
-            for u in range(2):
-                turn(bank[:, u, cols[b]], term[:, cols[u]], start and u == 0, stop and u == 1)
-
-        woven_v2 = woven_tile(N, "v2")
-        weave(on_scalar, woven_v2[:], raw["v2"][:])
+        nc.vector.tensor_copy(x_bytes[:], scale_table[:].indirect(offs_t[:]))
+        woven_v1 = [sbuf([P, PACK * P], BF16, "woven_v1_%d" % b) for b in range(BLOCKS)]
+        for b in range(BLOCKS):
+            weave(on_scalar, woven_v1[b][:], raw["v1"][:, :, cols[b]])
+        q_v1 = [quantise(woven_v1[0][:], "v1_0")]
+        pieces = [slice(0, 256), slice(256, 384), slice(384, 512)]
         h1 = [sbuf([P, S], F32, "h1_0")]
-        for u in range(2):
-            nc.scalar.copy(out=h1[0][:, halves[u]], in_=bank1[u][:])
-        woven_e = woven_tile(V, "e")
-        weave(on_vector, woven_e[:], raw["e"][:])
-        q_v2 = quantise(woven_v2, "v2")
-        bank2 = [state_product(q_v2, b * P) for b in range(BLOCKS)]
-        nodes = quantise(woven_e, "e")
-        h1.append(leave_psum(bank1[2], "h1_1"))
-        a_bank, g_bank = psum([P, 2, N]), psum([P, 2, N])
+        for i, piece in enumerate(pieces):
+            nc.vector.tensor_copy(x_codes[:, piece], word_table[:].indirect(offs_t[:, piece.start // 16 : piece.stop // 16]))
+            nc.scalar.copy(out=h1[0][:, piece], in_=state_product(q_v1[0], lo, "h1_0_%d" % i, i, piece)[:])
+        q_v1.append(quantise(woven_v1[1][:], "v1_1"))
+        h1.append(leave_psum(state_product(q_v1[1], lo, "h1_1_bank", 3), "h1_1"))
 
-        def gate_term(bank, window, b, d, name, tag=None):
-            term = row("%s%d%d" % (name, b, d), tag)
-            fetch(term[:], window[b], d)
-            add_turned(bank, b, term, start=(b + d == 0))
-
-        def g_first(b, tag):
-            term = row("g%d0" % b, tag)
-            fetch(term[:], h2[b], 0)
-            return term
-
-        def g_second(b, first, tag):
-            term = row("g%d1" % b, tag)
-            fetch_with(term[:], h2[b], 1, first[:], ALU.add)
-            add_turned(g_bank, b, term, start=(b == 0))
-
-        woven_v3, woven_w3 = woven_tile(N, "v3"), woven_tile(N, "w3")
-        weave(on_scalar, woven_v3[:, lo, :], raw["v3"][:, :, lo])
-        weave_on_gpsimd(woven_v3[:, hi, :], raw["v3"][:, :, hi])
-        for part in cols:
-            weave_on_gpsimd(woven_w3[:, part, :], raw["w3"][:, :, part])
+        ring = sbuf([P, PACK * (P + 2 * N - W3_SHARE)], BF16, "ring")
         for b in range(BLOCKS):
-            for d in range(2):
-                gate_term(a_bank, h1, b, d, "a")
-        h2 = [leave_psum(bank2[b], "h2_%d" % b, 12288 + 4 * S * b) for b in range(BLOCKS)]
-        first = g_first(0, None)
-        q_v3 = quantise(woven_v3, "v3")
-        bank3 = [state_product(q_v3, b * P) for b in range(BLOCKS)]
-        q_w3 = quantise(woven_w3, "w3")
-        ebank3 = [node_block(q_w3, b) for b in range(BLOCKS)]
-        woven_w2, woven_w1 = woven_tile(N, "w2"), woven_tile(N, "w1")
-        weave(on_scalar, woven_w2[:], raw["w2"][:])
-        weave(on_scalar, woven_w1[:], raw["w1"][:])
-        h3 = [leave_psum(bank3[0], "h3_0", 4096)]
-        g_second(0, first, 0)
-        ebank2 = node_product(quantise(woven_w2, "w2"), 0)
-        first = g_first(1, 4096 + 4 * S)
-        ebank1 = node_product(quantise(woven_w1, "w1"), 0)
-        g_second(1, first, 8192 + 4 * S)
-        e3 = [leave_psum(ebank3[b], "e3_%d" % b, 8192 + 4 * V * b) for b in range(BLOCKS)]
-        h3.append(leave_psum(bank3[1], "h3_1", "woven_w1"))
-        e2 = leave_psum(ebank2, "e2", 8192 + 4 * S + 4 * V)
-        e1 = leave_psum(ebank1, "e1")
-        for bank, e in ((g_bank, e2), (a_bank, e1)):
+            weave(on_vector, woven_cols(ring, (1 - b) * P, P), raw["v2"][:, :, cols[b]])
+        q_v2 = [quantise(woven_cols(ring, (1 - b) * P, P), "v2_%d" % b) for b in range(BLOCKS)]
+        bank2 = [state_product(q_v2[b], lo, "h2_bank%d" % b, 4 + b) for b in range(BLOCKS)]
+        a_bank = psum([P, 2, N], "a_bank", 6)
+        a_sums = [a_bank[:, :, cols[b]] for b in range(BLOCKS)]
+
+        def weave_shared(tile, first, src, gpsimd_cols, copy=on_scalar):
+            weave_on_gpsimd(woven_cols(tile, first, gpsimd_cols), src[:, :, :gpsimd_cols])
+            weave(copy, woven_cols(tile, first + gpsimd_cols, N - gpsimd_cols), src[:, :, gpsimd_cols:])
+            return woven_cols(tile, first, N)
+
+        def node_product(weights, name, bank):
+            dst = psum([P, BLOCKS, V], name, bank)
             for b in range(BLOCKS):
-                add_turned(bank, b, e[:, b, :], stop=(b == BLOCKS - 1))
+                product(dst[:, b, :], weights, cols[b], nodes, everyone)
+            return dst
 
-        f_pre, f = [pair("f_pre%d" % b) for b in range(BLOCKS)], [pair("f%d" % b) for b in range(BLOCKS)]
+        woven_e = weave_shared(ring, P, raw["e"], E_SHARE)
+        woven_v3 = weave_shared(sbuf([P, PACK * N], BF16, "woven_v3"), 0, raw["v3"], V3_SHARE)
+        after_v2 = sbuf([P, 4, V], F32, "after_v2", place["v2"])
         for b in range(BLOCKS):
             for d in range(2):
-                fetch_with(f_pre[b][:, d, :], h3[b], d, e3[b][:], ALU.add)
-        a_turned, g_turned = pair("a_turned"), pair("g_turned")
-        nc.scalar.activation(f[0][:], f_pre[0][:], ACT.Sigmoid)
-        nc.scalar.activation(g_turned[:], g_bank[:], ACT.Tanh)
-        nc.scalar.activation(a_turned[:], a_bank[:], ACT.Sigmoid)
-        nc.scalar.activation(f[1][:], f_pre[1][:], ACT.Sigmoid)
+                gate_term(a_sums[b], h1[b], d, after_v2[:, 2 * b + d, :], start=(b + d == 0))
+        nodes = quantise(woven_e, "e")
+        q_v3 = quantise(woven_v3, "v3")
+        h2 = [leave_psum(bank2[b], "h2_%d" % b, place["v3"] if b else place["e"]) for b in range(BLOCKS)]
+        bank3 = [state_product(q_v3, cols[b], "h3_bank%d" % b, b) for b in range(BLOCKS)]
 
-        fc = [pair("fc%d" % b) for b in range(BLOCKS)]
-        kept_bank = psum([P, 2, P])
+        woven_w3 = weave_shared(ring, P + N - W3_SHARE, raw["w3"], W3_SHARE)
+        g_terms = sbuf([P, 2, V], F32, "g_terms", place["v3"] + 2 * ROW)
+        g_sums = [psum([P, 2, P], "g_bank0", 7)]
         for d in range(2):
-            fetch_with(fc[0][:, d, :], cells[0], d, f[0][:, d, :], ALU.mult)
-            add_turned(kept_bank, 0, fc[0][:, d, :], start=(d == 0), stop=(d == 1))
+            gate_term(g_sums[0], h2[0], d, g_terms[:, d, :], start=(d == 0))
+        woven_w1 = sbuf([P, PACK * N], BF16, "woven_w1")
+        weave(on_scalar, woven_w1[:], raw["w1"][:])
+        q_w3 = quantise(woven_w3, "w3")
+        ebank3 = [psum([P, V], "e3_bank%d" % b, 2 + b) for b in range(BLOCKS)]
+        for b in range(BLOCKS):
+            product(ebank3[b][:], q_w3, cols[b], nodes, everyone)
+
+        after_w3 = sbuf([P, 2, V], F32, "after_w3", place["w3"])
+        for d in range(2):
+            nc.vector.tensor_copy(after_w3[:, d, :], h2[1][:].indirect(pos[d][:]))
+        h3 = [leave_psum(bank3[0], "h3_0", place["w1"] - ROW)]
+        woven_w2 = weave_shared(sbuf([P, PACK * N], BF16, "woven_w2", place["e"]), 0, raw["w2"], W2_SHARE, on_vector)
+        e3 = sbuf([P, 2, V], F32, "e3", place["w1"] + 3 * ROW)
+        nc.scalar.copy(out=e3[:, 0, :], in_=ebank3[0][:])
+        ebank1 = node_product(quantise(woven_w1[:], "w1"), "e1_bank", 4)
+        ebank2 = node_product(quantise(woven_w2, "w2"), "e2_bank", 5)
+        h3.append(leave_psum(bank3[1], "h3_1", place["w1"] + ROW))
+        nc.scalar.copy(out=e3[:, 1, :], in_=ebank3[1][:])
+        g_sums.append(psum([P, 2, P], "g_bank1", 1))
+        for d in range(2):
+            add_turned(g_sums[1], after_w3[:, d, :], start=(d == 0))
+        e1 = leave_psum(ebank1, "e1")
+        for b in range(BLOCKS):
+            add_turned(a_sums[b], e1[:, b, :], stop=(b == BLOCKS - 1))
+
+        f_pre = [pair("f_pre%d" % b, place["w2"] + 2 * ROW * b) for b in range(BLOCKS)]
+        f = [pair("f%d" % b) for b in range(BLOCKS)]
+        for b in range(BLOCKS):
+            for d in range(2):
+                fetch_with(f_pre[b][:, d, :], h3[b], pos[d][:], e3[:, b, :], ALU.add)
+        nc.scalar.activation(f[0][:], f_pre[0][:], ACT.Sigmoid)
+        e2 = leave_psum(ebank2, "e2")
+        for b in reversed(range(BLOCKS)):
+            add_turned(g_sums[b], e2[:, b, :], stop=True)
+        a_turned = pair("a_turned")
+        g_turned = [sbuf([P, 2, P], F32, "g_turned%d" % b, place["g_turned"] + ROW * b) for b in range(BLOCKS)]
+        nc.scalar.activation(f[1][:], f_pre[1][:], ACT.Sigmoid)
+        nc.scalar.activation(a_turned[:], a_bank[:], ACT.Sigmoid)
+        for b in reversed(range(BLOCKS)):
+            nc.scalar.activation(g_turned[b][:], g_sums[b][:], ACT.Tanh)
+
+        fc0 = pair("fc0")
+        kept_bank = psum([P, 2, P], "kept_bank", 0)
+        for d in range(2):
+            fetch_with(fc0[:, d, :], cells[0], pos[d][:], f[0][:, d, :], ALU.mult)
+            add_turned(kept_bank, fc0[:, d, :], start=(d == 0), stop=(d == 1))
         kept0_turned = leave_psum(kept_bank, "kept0_turned")
-        fresh_turned = pair("fresh_turned")
-        nc.vector.tensor_tensor(fresh_turned[:], a_turned[:], g_turned[:], ALU.mult)
-        state_bank = [psum([P, V]) for b in range(BLOCKS)]
+        state_bank = [psum([P, V], "state_bank%d" % b, 2 + b) for b in range(BLOCKS)]
+        fresh_turned = [sbuf([P, 2, P], F32, "fresh_turned%d" % b) for b in range(BLOCKS)]
+        half_list = V // 2 // 16
+        first1 = sbuf([P, V], F32, "first1")
+        fetch_with(first1[:], cells[1], pos[0][:], f[1][:, 0, :], ALU.mult)
+        nc.vector.tensor_tensor(fresh_turned[1][:], a_turned[:, :, hi], g_turned[1][:], ALU.mult)
         for u in range(2):
-            turn(state_bank[1][:, cols[u]], fresh_turned[:, u, hi], True, True)
+            turn(state_bank[1][:, cols[u]], fresh_turned[1][:, u, :], True, True)
+        nc.vector.tensor_tensor(fresh_turned[0][:], a_turned[:, :, lo], g_turned[0][:], ALU.mult)
         for u in range(2):
-            turn(state_bank[0][:, cols[u]], fresh_turned[:, u, lo], u == 0, False)
+            turn(state_bank[0][:, cols[u]], fresh_turned[0][:, u, :], u == 0, False)
         for u in range(2):
             turn(state_bank[0][:, cols[u]], kept0_turned[:, u, :], False, u == 1)
-        fetch_with(fc[1][:, 0, :], cells[1], 0, f[1][:, 0, :], ALU.mult)
-        last = [sbuf([P, P], F32, "last0"), None]
-
-        def fetch_last(u):
-            nc.vector.tensor_tensor(last[u][:], cells[1][:].indirect(pos[1][:, 8 * u : 8 * (u + 1)]), f[1][:, 1, cols[u]], ALU.mult)
-
-        fetch_last(0)
-        part1 = row("part1")
-        nc.vector.tensor_tensor(part1[:], fc[1][:, 0, :], state_bank[1][:], ALU.add)
-        last[1] = sbuf([P, P], F32, "last1", "fresh_turned")
-        fetch_last(1)
-        result0 = row("result0")
+        last = [sbuf([P, P], F32, "last%d" % u, place["g_turned"] + ROW if u else None) for u in range(2)]
+        for u in range(2):
+            fetch_with(last[u][:], cells[1], pos[1][:, half_list * u : half_list * (u + 1)], f[1][:, 1, cols[u]], ALU.mult)
+        kept1 = sbuf([P, V], F32, "kept1", place["g_turned"])
+        for u in range(2):
+            nc.vector.tensor_tensor(kept1[:, cols[u]], first1[:, cols[u]], last[u][:], ALU.add)
+        result0 = sbuf([P, V], F32, "result0")
         nc.scalar.activation(result0[:], state_bank[0][:], ACT.Tanh)
         nc.sync.dma_start(out=out[lo, :], in_=result0[:])
         for u in range(2):
             state, result = sbuf([P, P], F32, "state1_%d" % u), sbuf([P, P], F32, "result1_%d" % u)
-            nc.vector.tensor_tensor(state[:], part1[:, cols[u]], last[u][:], ALU.add)
+            nc.vector.tensor_tensor(state[:], kept1[:, cols[u]], state_bank[1][:, cols[u]], ALU.add)
             nc.scalar.activation(result[:], state[:], ACT.Tanh)
             nc.sync.dma_start(out=out[hi, cols[u]], in_=result[:])

@@ -23,7 +23,8 @@ BLOCKS = N // P
 BANK = 2048
 RAW = PACK * N * 4
 ROW = V * 4
-E_SHARE, V3_SHARE, W3_SHARE, W2_SHARE = 160, 160, 144, 160
+W3_SHARE = 80
+W2_SHARES = (80, 64, 112)
 
 
 def tile_picked_ztree_tanh_p_kernel(tc, x_words, x_scales, eT, w1, w2, w3, v1, v2, v3, cell, offs, pos1, pos2, out):
@@ -46,9 +47,9 @@ def tile_picked_ztree_tanh_p_kernel(tc, x_words, x_scales, eT, w1, w2, w3, v1, v
             nc.sync.dma_start(lst[:], src)
             return lst
 
-        def load_matrix(src, name, queue=nc.sync):
+        def load_matrix(src, name):
             rows = sbuf([P, PACK, N], F32, "raw_" + name, place[name])
-            queue.dma_start(out=rows[:], in_=src.rearrange("(p j) c -> p j c", j=PACK))
+            nc.sync.dma_start(out=rows[:], in_=src.rearrange("(p j) c -> p j c", j=PACK))
             return rows
 
         def load_cells(b):
@@ -108,15 +109,17 @@ def tile_picked_ztree_tanh_p_kernel(tc, x_words, x_scales, eT, w1, w2, w3, v1, v
         lo, hi = slice(0, P), slice(P, 2 * P)
         cols = [lo, hi]
         everyone = slice(0, V)
-        place = {name: (3 * i + 1) * RAW for i, name in enumerate(("v1", "v2", "e", "v3", "w3", "w1", "w2", "g_turned"))}
+        place = {name: (3 * i + 1) * RAW for i, name in enumerate(("v1", "v2", "e", "v3", "w3", "w1", "w2", "g_turned", "h2", "ring"))}
 
         scale_table = sbuf([P, T], U8, "scale_table")
         nc.vector.memset(scale_table[:].bitcast(I32), 0)
         offs_t = load_list(offs, "offs_t")
-        raw = {"v1": load_matrix(v1, "v1", nc.scalar)}
+        raw = {"v1": sbuf([P, PACK, N], F32, "raw_v1", place["v1"])}
+        v1_rows = v1.rearrange("(p j) c -> p j c", j=PACK)
+        nc.sync.dma_start(out=raw["v1"][:, : PACK - 1, :], in_=v1_rows[:, : PACK - 1, :])
         for q in range(4):
-            queue = nc.sync if q < 2 else nc.scalar
-            queue.dma_start(out=scale_table[32 * q : 32 * q + 4, :].bitcast(I32), in_=x_scales[0, 4 * q : 4 * q + 4, :].bitcast(I32))
+            nc.sync.dma_start(out=scale_table[32 * q : 32 * q + 4, :].bitcast(I32), in_=x_scales[0, 4 * q : 4 * q + 4, :].bitcast(I32))
+        nc.sync.dma_start(out=raw["v1"][:, PACK - 1, :], in_=v1_rows[:, PACK - 1, :])
         word_table = sbuf([P, T], U32, "word_table")
         nc.sync.dma_start(out=word_table[:].bitcast(I32), in_=x_words[0].rearrange("p c r -> p (c r)").bitcast(I32))
         pos = [load_list(pos1, "pos1_t")]
@@ -149,7 +152,7 @@ def tile_picked_ztree_tanh_p_kernel(tc, x_words, x_scales, eT, w1, w2, w3, v1, v
         q_v1.append(quantise(woven_v1[1][:], "v1_1"))
         h1.append(leave_psum(state_product(q_v1[1], lo, "h1_1_bank", 3), "h1_1"))
 
-        ring = sbuf([P, PACK * (P + 2 * N - W3_SHARE)], BF16, "ring")
+        ring = sbuf([P, PACK * (P + N)], BF16, "ring", place["ring"])
         for b in range(BLOCKS):
             weave(on_vector, woven_cols(ring, (1 - b) * P, P), raw["v2"][:, :, cols[b]])
         q_v2 = [quantise(woven_cols(ring, (1 - b) * P, P), "v2_%d" % b) for b in range(BLOCKS)]
@@ -157,9 +160,9 @@ def tile_picked_ztree_tanh_p_kernel(tc, x_words, x_scales, eT, w1, w2, w3, v1, v
         a_bank = psum([P, 2, N], "a_bank", 6)
         a_sums = [a_bank[:, :, cols[b]] for b in range(BLOCKS)]
 
-        def weave_shared(tile, first, src, gpsimd_cols, copy=on_scalar):
+        def weave_shared(tile, first, src, gpsimd_cols):
             weave_on_gpsimd(woven_cols(tile, first, gpsimd_cols), src[:, :, :gpsimd_cols])
-            weave(copy, woven_cols(tile, first + gpsimd_cols, N - gpsimd_cols), src[:, :, gpsimd_cols:])
+            weave(on_scalar, woven_cols(tile, first + gpsimd_cols, N - gpsimd_cols), src[:, :, gpsimd_cols:])
             return woven_cols(tile, first, N)
 
         def node_product(weights, name, bank):
@@ -168,25 +171,28 @@ def tile_picked_ztree_tanh_p_kernel(tc, x_words, x_scales, eT, w1, w2, w3, v1, v
                 product(dst[:, b, :], weights, cols[b], nodes, everyone)
             return dst
 
-        woven_e = weave_shared(ring, P, raw["e"], E_SHARE)
-        woven_v3 = weave_shared(sbuf([P, PACK * N], BF16, "woven_v3"), 0, raw["v3"], V3_SHARE)
+        woven_e = woven_cols(ring, P, N)
+        weave_on_gpsimd(woven_e, raw["e"][:])
         after_v2 = sbuf([P, 4, V], F32, "after_v2", place["v2"])
         for b in range(BLOCKS):
             for d in range(2):
                 gate_term(a_sums[b], h1[b], d, after_v2[:, 2 * b + d, :], start=(b + d == 0))
         nodes = quantise(woven_e, "e")
-        q_v3 = quantise(woven_v3, "v3")
-        h2 = [leave_psum(bank2[b], "h2_%d" % b, place["v3"] if b else place["e"]) for b in range(BLOCKS)]
-        bank3 = [state_product(q_v3, cols[b], "h3_bank%d" % b, b) for b in range(BLOCKS)]
+        h2 = [leave_psum(bank2[b], "h2_%d" % b, place["h2"] + 2 * ROW * b) for b in range(BLOCKS)]
+        woven_v3 = sbuf([P, PACK * N], BF16, "woven_v3")
+        weave(on_scalar, woven_v3[:], raw["v3"][:])
 
-        woven_w3 = weave_shared(ring, P + N - W3_SHARE, raw["w3"], W3_SHARE)
-        g_terms = sbuf([P, 2, V], F32, "g_terms", place["v3"] + 2 * ROW)
+        woven_w3 = sbuf([P, PACK * N], BF16, "woven_w3", place["ring"])
+        woven_w3 = weave_shared(woven_w3, 0, raw["w3"], W3_SHARE)
+        g_terms = sbuf([P, 2, V], F32, "g_terms", place["e"])
         g_sums = [psum([P, 2, P], "g_bank0", 7)]
         for d in range(2):
             gate_term(g_sums[0], h2[0], d, g_terms[:, d, :], start=(d == 0))
         woven_w1 = sbuf([P, PACK * N], BF16, "woven_w1")
         weave(on_scalar, woven_w1[:], raw["w1"][:])
+        q_v3 = quantise(woven_v3[:], "v3")
         q_w3 = quantise(woven_w3, "w3")
+        bank3 = [state_product(q_v3, cols[b], "h3_bank%d" % b, b) for b in range(BLOCKS)]
         ebank3 = [psum([P, V], "e3_bank%d" % b, 2 + b) for b in range(BLOCKS)]
         for b in range(BLOCKS):
             product(ebank3[b][:], q_w3, cols[b], nodes, everyone)
@@ -194,12 +200,20 @@ def tile_picked_ztree_tanh_p_kernel(tc, x_words, x_scales, eT, w1, w2, w3, v1, v
         after_w3 = sbuf([P, 2, V], F32, "after_w3", place["w3"])
         for d in range(2):
             nc.vector.tensor_copy(after_w3[:, d, :], h2[1][:].indirect(pos[d][:]))
+        woven_w2 = sbuf([P, PACK * N], BF16, "woven_w2", place["ring"])
+        first = 0
+        for copy, count in zip((None, on_scalar, on_vector), W2_SHARES):
+            dst, src = woven_cols(woven_w2, first, count), raw["w2"][:, :, first : first + count]
+            if copy is None:
+                weave_on_gpsimd(dst, src)
+            else:
+                weave(copy, dst, src)
+            first += count
         h3 = [leave_psum(bank3[0], "h3_0", place["w1"] - ROW)]
-        woven_w2 = weave_shared(sbuf([P, PACK * N], BF16, "woven_w2", place["e"]), 0, raw["w2"], W2_SHARE, on_vector)
         e3 = sbuf([P, 2, V], F32, "e3", place["w1"] + 3 * ROW)
         nc.scalar.copy(out=e3[:, 0, :], in_=ebank3[0][:])
         ebank1 = node_product(quantise(woven_w1[:], "w1"), "e1_bank", 4)
-        ebank2 = node_product(quantise(woven_w2, "w2"), "e2_bank", 5)
+        ebank2 = node_product(quantise(woven_w2[:], "w2"), "e2_bank", 5)
         h3.append(leave_psum(bank3[1], "h3_1", place["w1"] + ROW))
         nc.scalar.copy(out=e3[:, 1, :], in_=ebank3[1][:])
         g_sums.append(psum([P, 2, P], "g_bank1", 1))

@@ -24,7 +24,7 @@ BANK = 2048
 RAW = PACK * N * 4
 ROW = V * 4
 W3_SHARE = 80
-W2_SHARES = (80, 64, 112)
+W2_SHARES = (96, 160)
 
 
 def tile_picked_ztree_tanh_p_kernel(tc, x_words, x_scales, eT, w1, w2, w3, v1, v2, v3, cell, offs, pos1, pos2, out):
@@ -185,9 +185,8 @@ def tile_picked_ztree_tanh_p_kernel(tc, x_words, x_scales, eT, w1, w2, w3, v1, v
         woven_w3 = sbuf([P, PACK * N], BF16, "woven_w3", place["ring"])
         woven_w3 = weave_shared(woven_w3, 0, raw["w3"], W3_SHARE)
         g_terms = sbuf([P, 2, V], F32, "g_terms", place["e"])
-        g_sums = [psum([P, 2, P], "g_bank0", 7)]
-        for d in range(2):
-            gate_term(g_sums[0], h2[0], d, g_terms[:, d, :], start=(d == 0))
+        for b in range(BLOCKS):
+            nc.vector.tensor_copy(g_terms[:, b, :], h2[b][:].indirect(pos[0][:]))
         woven_w1 = sbuf([P, PACK * N], BF16, "woven_w1")
         weave(on_scalar, woven_w1[:], raw["w1"][:])
         q_v3 = quantise(woven_v3[:], "v3")
@@ -198,16 +197,14 @@ def tile_picked_ztree_tanh_p_kernel(tc, x_words, x_scales, eT, w1, w2, w3, v1, v
             product(ebank3[b][:], q_w3, cols[b], nodes, everyone)
 
         after_w3 = sbuf([P, 2, V], F32, "after_w3", place["w3"])
-        for d in range(2):
-            nc.vector.tensor_copy(after_w3[:, d, :], h2[1][:].indirect(pos[d][:]))
-        woven_w2 = sbuf([P, PACK * N], BF16, "woven_w2", place["ring"])
+        for b in range(BLOCKS):
+            fetch_with(after_w3[:, b, :], h2[b], pos[1][:], g_terms[:, b, :], ALU.add)
+        g_sums = [psum([P, 2, P], "g_bank0", 7)]
+        add_turned(g_sums[0], after_w3[:, 0, :], start=True)
+        woven_w2 = sbuf([P, PACK * N], BF16, "woven_w2")
         first = 0
-        for copy, count in zip((None, on_scalar, on_vector), W2_SHARES):
-            dst, src = woven_cols(woven_w2, first, count), raw["w2"][:, :, first : first + count]
-            if copy is None:
-                weave_on_gpsimd(dst, src)
-            else:
-                weave(copy, dst, src)
+        for copy, count in zip((on_scalar, on_vector), W2_SHARES):
+            weave(copy, woven_cols(woven_w2, first, count), raw["w2"][:, :, first : first + count])
             first += count
         h3 = [leave_psum(bank3[0], "h3_0", place["w1"] - ROW)]
         e3 = sbuf([P, 2, V], F32, "e3", place["w1"] + 3 * ROW)
@@ -217,8 +214,7 @@ def tile_picked_ztree_tanh_p_kernel(tc, x_words, x_scales, eT, w1, w2, w3, v1, v
         h3.append(leave_psum(bank3[1], "h3_1", place["w1"] + ROW))
         nc.scalar.copy(out=e3[:, 1, :], in_=ebank3[1][:])
         g_sums.append(psum([P, 2, P], "g_bank1", 1))
-        for d in range(2):
-            add_turned(g_sums[1], after_w3[:, d, :], start=(d == 0))
+        add_turned(g_sums[1], after_w3[:, 1, :], start=True)
         e1 = leave_psum(ebank1, "e1")
         for b in range(BLOCKS):
             add_turned(a_sums[b], e1[:, b, :], stop=(b == BLOCKS - 1))

@@ -23,8 +23,7 @@ BLOCKS = N // P
 BANK = 2048
 RAW = PACK * N * 4
 ROW = V * 4
-W3_SHARE = 80
-W2_SHARES = (96, 160)
+W3_SHARE = 192
 
 
 def tile_picked_ztree_tanh_p_kernel(tc, x_words, x_scales, eT, w1, w2, w3, v1, v2, v3, cell, offs, pos1, pos2, out):
@@ -109,23 +108,18 @@ def tile_picked_ztree_tanh_p_kernel(tc, x_words, x_scales, eT, w1, w2, w3, v1, v
         lo, hi = slice(0, P), slice(P, 2 * P)
         cols = [lo, hi]
         everyone = slice(0, V)
-        place = {name: (3 * i + 1) * RAW for i, name in enumerate(("v1", "v2", "e", "v3", "w3", "w1", "w2", "g_turned", "h2", "ring"))}
+        place = {name: (3 * i + 1) * RAW for i, name in enumerate(("v1", "v2", "e", "v3", "w3", "w1", "w2", "fresh", "woven"))}
 
         scale_table = sbuf([P, T], U8, "scale_table")
         nc.vector.memset(scale_table[:].bitcast(I32), 0)
-        offs_t = load_list(offs, "offs_t")
-        raw = {"v1": sbuf([P, PACK, N], F32, "raw_v1", place["v1"])}
-        v1_rows = v1.rearrange("(p j) c -> p j c", j=PACK)
-        nc.sync.dma_start(out=raw["v1"][:, : PACK - 1, :], in_=v1_rows[:, : PACK - 1, :])
-        for q in range(4):
-            nc.sync.dma_start(out=scale_table[32 * q : 32 * q + 4, :].bitcast(I32), in_=x_scales[0, 4 * q : 4 * q + 4, :].bitcast(I32))
-        nc.sync.dma_start(out=raw["v1"][:, PACK - 1, :], in_=v1_rows[:, PACK - 1, :])
         word_table = sbuf([P, T], U32, "word_table")
         nc.sync.dma_start(out=word_table[:].bitcast(I32), in_=x_words[0].rearrange("p c r -> p (c r)").bitcast(I32))
-        pos = [load_list(pos1, "pos1_t")]
-        raw["v2"] = load_matrix(v2, "v2")
-        pos.append(load_list(pos2, "pos2_t"))
-        for name, src in (("e", eT), ("v3", v3), ("w3", w3), ("w1", w1), ("w2", w2)):
+        offs_t = load_list(offs, "offs_t")
+        for q in range(4):
+            nc.sync.dma_start(out=scale_table[32 * q : 32 * q + 4, :].bitcast(I32), in_=x_scales[0, 4 * q : 4 * q + 4, :].bitcast(I32))
+        raw = {name: load_matrix(src, name) for name, src in (("v1", v1), ("v2", v2), ("e", eT))}
+        pos = [load_list(pos1, "pos1_t"), load_list(pos2, "pos2_t")]
+        for name, src in (("v3", v3), ("w3", w3), ("w1", w1), ("w2", w2)):
             raw[name] = load_matrix(src, name)
         cells = [load_cells(b) for b in range(BLOCKS)]
 
@@ -139,31 +133,26 @@ def tile_picked_ztree_tanh_p_kernel(tc, x_words, x_scales, eT, w1, w2, w3, v1, v
         x_codes = sbuf([P, S], U32, "x_codes")
         x_bytes = sbuf([P, S], U8, "x_bytes")
         picked = (x_codes, x_bytes)
+        nc.vector.tensor_copy(x_codes[:], word_table[:].indirect(offs_t[:]))
         nc.vector.tensor_copy(x_bytes[:], scale_table[:].indirect(offs_t[:]))
         woven_v1 = [sbuf([P, PACK * P], BF16, "woven_v1_%d" % b) for b in range(BLOCKS)]
         for b in range(BLOCKS):
             weave(on_scalar, woven_v1[b][:], raw["v1"][:, :, cols[b]])
         q_v1 = [quantise(woven_v1[0][:], "v1_0")]
-        pieces = [slice(0, 256), slice(256, 384), slice(384, 512)]
         h1 = [sbuf([P, S], F32, "h1_0")]
-        for i, piece in enumerate(pieces):
-            nc.vector.tensor_copy(x_codes[:, piece], word_table[:].indirect(offs_t[:, piece.start // 16 : piece.stop // 16]))
-            nc.scalar.copy(out=h1[0][:, piece], in_=state_product(q_v1[0], lo, "h1_0_%d" % i, i, piece)[:])
+        for u in range(2):
+            half = slice(u * V, (u + 1) * V)
+            nc.scalar.copy(out=h1[0][:, half], in_=state_product(q_v1[0], lo, "h1_0_%d" % u, u, half)[:])
         q_v1.append(quantise(woven_v1[1][:], "v1_1"))
         h1.append(leave_psum(state_product(q_v1[1], lo, "h1_1_bank", 3), "h1_1"))
 
-        ring = sbuf([P, PACK * (P + N)], BF16, "ring", place["ring"])
+        woven_v2 = sbuf([P, PACK * N], BF16, "woven_v2")
         for b in range(BLOCKS):
-            weave(on_vector, woven_cols(ring, (1 - b) * P, P), raw["v2"][:, :, cols[b]])
-        q_v2 = [quantise(woven_cols(ring, (1 - b) * P, P), "v2_%d" % b) for b in range(BLOCKS)]
-        bank2 = [state_product(q_v2[b], lo, "h2_bank%d" % b, 4 + b) for b in range(BLOCKS)]
+            weave((on_scalar, on_vector)[b], woven_cols(woven_v2, b * P, P), raw["v2"][:, :, cols[b]])
+        q_v2 = quantise(woven_v2[:], "v2")
+        bank2 = [state_product(q_v2, cols[b], "h2_bank%d" % b, 4 + b) for b in range(BLOCKS)]
         a_bank = psum([P, 2, N], "a_bank", 6)
         a_sums = [a_bank[:, :, cols[b]] for b in range(BLOCKS)]
-
-        def weave_shared(tile, first, src, gpsimd_cols):
-            weave_on_gpsimd(woven_cols(tile, first, gpsimd_cols), src[:, :, :gpsimd_cols])
-            weave(on_scalar, woven_cols(tile, first + gpsimd_cols, N - gpsimd_cols), src[:, :, gpsimd_cols:])
-            return woven_cols(tile, first, N)
 
         def node_product(weights, name, bank):
             dst = psum([P, BLOCKS, V], name, bank)
@@ -171,69 +160,67 @@ def tile_picked_ztree_tanh_p_kernel(tc, x_words, x_scales, eT, w1, w2, w3, v1, v
                 product(dst[:, b, :], weights, cols[b], nodes, everyone)
             return dst
 
-        woven_e = woven_cols(ring, P, N)
-        weave_on_gpsimd(woven_e, raw["e"][:])
-        after_v2 = sbuf([P, 4, V], F32, "after_v2", place["v2"])
+        woven_e = sbuf([P, PACK * N], BF16, "woven_e", place["woven"])
+        weave(on_vector, woven_e[:], raw["e"][:])
+        gate_term(a_sums[0], h1[0], 0, sbuf([P, V], F32, "a_first")[:], start=True)
+        nodes = quantise(woven_e[:], "e")
+        after_e = sbuf([P, 4, V], F32, "after_e", place["e"])
+        gate_term(a_sums[1], h1[1], 0, after_e[:, 0, :])
+        h2 = [leave_psum(bank2[b], "h2_%d" % b) for b in range(BLOCKS)]
         for b in range(BLOCKS):
-            for d in range(2):
-                gate_term(a_sums[b], h1[b], d, after_v2[:, 2 * b + d, :], start=(b + d == 0))
-        nodes = quantise(woven_e, "e")
-        h2 = [leave_psum(bank2[b], "h2_%d" % b, place["h2"] + 2 * ROW * b) for b in range(BLOCKS)]
+            gate_term(a_sums[b], h1[b], 1, after_e[:, 1 + b, :])
+        g_first = [after_e[:, 3, :]]
+        nc.vector.tensor_copy(g_first[0], h2[0][:].indirect(pos[0][:]))
         woven_v3 = sbuf([P, PACK * N], BF16, "woven_v3")
         weave(on_scalar, woven_v3[:], raw["v3"][:])
-
-        woven_w3 = sbuf([P, PACK * N], BF16, "woven_w3", place["ring"])
-        woven_w3 = weave_shared(woven_w3, 0, raw["w3"], W3_SHARE)
-        g_terms = sbuf([P, 2, V], F32, "g_terms", place["e"])
-        for b in range(BLOCKS):
-            nc.vector.tensor_copy(g_terms[:, b, :], h2[b][:].indirect(pos[0][:]))
+        woven_w3 = sbuf([P, PACK * N], BF16, "woven_w3", place["woven"])
+        weave_on_gpsimd(woven_cols(woven_w3, 0, W3_SHARE), raw["w3"][:, :, :W3_SHARE])
+        weave(on_scalar, woven_cols(woven_w3, W3_SHARE, N - W3_SHARE), raw["w3"][:, :, W3_SHARE:])
         woven_w1 = sbuf([P, PACK * N], BF16, "woven_w1")
         weave(on_scalar, woven_w1[:], raw["w1"][:])
         q_v3 = quantise(woven_v3[:], "v3")
-        q_w3 = quantise(woven_w3, "w3")
+        q_w3 = quantise(woven_w3[:], "w3")
         bank3 = [state_product(q_v3, cols[b], "h3_bank%d" % b, b) for b in range(BLOCKS)]
         ebank3 = [psum([P, V], "e3_bank%d" % b, 2 + b) for b in range(BLOCKS)]
         for b in range(BLOCKS):
             product(ebank3[b][:], q_w3, cols[b], nodes, everyone)
-
-        after_w3 = sbuf([P, 2, V], F32, "after_w3", place["w3"])
-        for b in range(BLOCKS):
-            fetch_with(after_w3[:, b, :], h2[b], pos[1][:], g_terms[:, b, :], ALU.add)
-        g_sums = [psum([P, 2, P], "g_bank0", 7)]
-        add_turned(g_sums[0], after_w3[:, 0, :], start=True)
-        woven_w2 = sbuf([P, PACK * N], BF16, "woven_w2")
-        first = 0
-        for copy, count in zip((on_scalar, on_vector), W2_SHARES):
-            weave(copy, woven_cols(woven_w2, first, count), raw["w2"][:, :, first : first + count])
-            first += count
-        h3 = [leave_psum(bank3[0], "h3_0", place["w1"] - ROW)]
-        e3 = sbuf([P, 2, V], F32, "e3", place["w1"] + 3 * ROW)
-        nc.scalar.copy(out=e3[:, 0, :], in_=ebank3[0][:])
+        g_first.append(sbuf([P, V], F32, "g_first1", place["w3"])[:])
+        nc.vector.tensor_copy(g_first[1], h2[1][:].indirect(pos[0][:]))
+        after_w1 = sbuf([P, 4, V], F32, "after_w1", place["w1"] + 3 * ROW)
+        g_both = [after_w1[:, 2 + b, :] for b in range(BLOCKS)]
         ebank1 = node_product(quantise(woven_w1[:], "w1"), "e1_bank", 4)
+        for b in range(BLOCKS):
+            fetch_with(g_both[b], h2[b], pos[1][:], g_first[b], ALU.add)
+        g_sums = [psum([P, 2, P], "g_bank0", 7)]
+        add_turned(g_sums[0], g_both[0], start=True)
+        woven_w2 = sbuf([P, PACK * N], BF16, "woven_w2")
+        weave(on_scalar, woven_w2[:], raw["w2"][:])
+        h3 = [leave_psum(bank3[0], "h3_0", place["w1"] - ROW)]
+        nc.scalar.copy(out=after_w1[:, 0, :], in_=ebank3[0][:])
         ebank2 = node_product(quantise(woven_w2[:], "w2"), "e2_bank", 5)
         h3.append(leave_psum(bank3[1], "h3_1", place["w1"] + ROW))
-        nc.scalar.copy(out=e3[:, 1, :], in_=ebank3[1][:])
+        nc.scalar.copy(out=after_w1[:, 1, :], in_=ebank3[1][:])
         g_sums.append(psum([P, 2, P], "g_bank1", 1))
-        add_turned(g_sums[1], after_w3[:, 1, :], start=True)
+        add_turned(g_sums[1], g_both[1], start=True)
         e1 = leave_psum(ebank1, "e1")
         for b in range(BLOCKS):
             add_turned(a_sums[b], e1[:, b, :], stop=(b == BLOCKS - 1))
+        e2 = leave_psum(ebank2, "e2")
+        for b in reversed(range(BLOCKS)):
+            add_turned(g_sums[b], e2[:, b, :], stop=True)
 
         f_pre = [pair("f_pre%d" % b, place["w2"] + 2 * ROW * b) for b in range(BLOCKS)]
         f = [pair("f%d" % b) for b in range(BLOCKS)]
         for b in range(BLOCKS):
             for d in range(2):
-                fetch_with(f_pre[b][:, d, :], h3[b], pos[d][:], e3[:, b, :], ALU.add)
+                fetch_with(f_pre[b][:, d, :], h3[b], pos[d][:], after_w1[:, b, :], ALU.add)
         nc.scalar.activation(f[0][:], f_pre[0][:], ACT.Sigmoid)
-        e2 = leave_psum(ebank2, "e2")
-        for b in reversed(range(BLOCKS)):
-            add_turned(g_sums[b], e2[:, b, :], stop=True)
         a_turned = pair("a_turned")
-        g_turned = [sbuf([P, 2, P], F32, "g_turned%d" % b, place["g_turned"] + ROW * b) for b in range(BLOCKS)]
-        nc.scalar.activation(f[1][:], f_pre[1][:], ACT.Sigmoid)
+        g_turned = pair("g_turned")
         nc.scalar.activation(a_turned[:], a_bank[:], ACT.Sigmoid)
         for b in reversed(range(BLOCKS)):
-            nc.scalar.activation(g_turned[b][:], g_sums[b][:], ACT.Tanh)
+            nc.scalar.activation(g_turned[:, :, cols[b]], g_sums[b][:], ACT.Tanh)
+        nc.scalar.activation(f[1][:], f_pre[1][:], ACT.Sigmoid)
 
         fc0 = pair("fc0")
         kept_bank = psum([P, 2, P], "kept_bank", 0)
@@ -241,30 +228,28 @@ def tile_picked_ztree_tanh_p_kernel(tc, x_words, x_scales, eT, w1, w2, w3, v1, v
             fetch_with(fc0[:, d, :], cells[0], pos[d][:], f[0][:, d, :], ALU.mult)
             add_turned(kept_bank, fc0[:, d, :], start=(d == 0), stop=(d == 1))
         kept0_turned = leave_psum(kept_bank, "kept0_turned")
+        fresh_turned = pair("fresh_turned", place["fresh"])
+        nc.vector.tensor_tensor(fresh_turned[:], a_turned[:], g_turned[:], ALU.mult)
         state_bank = [psum([P, V], "state_bank%d" % b, 2 + b) for b in range(BLOCKS)]
-        fresh_turned = [sbuf([P, 2, P], F32, "fresh_turned%d" % b) for b in range(BLOCKS)]
-        half_list = V // 2 // 16
-        first1 = sbuf([P, V], F32, "first1")
-        fetch_with(first1[:], cells[1], pos[0][:], f[1][:, 0, :], ALU.mult)
-        nc.vector.tensor_tensor(fresh_turned[1][:], a_turned[:, :, hi], g_turned[1][:], ALU.mult)
         for u in range(2):
-            turn(state_bank[1][:, cols[u]], fresh_turned[1][:, u, :], True, True)
-        nc.vector.tensor_tensor(fresh_turned[0][:], a_turned[:, :, lo], g_turned[0][:], ALU.mult)
+            turn(state_bank[1][:, cols[u]], fresh_turned[:, u, hi], True, True)
         for u in range(2):
-            turn(state_bank[0][:, cols[u]], fresh_turned[0][:, u, :], u == 0, False)
+            turn(state_bank[0][:, cols[u]], fresh_turned[:, u, lo], u == 0, False)
         for u in range(2):
             turn(state_bank[0][:, cols[u]], kept0_turned[:, u, :], False, u == 1)
-        last = [sbuf([P, P], F32, "last%d" % u, place["g_turned"] + ROW if u else None) for u in range(2)]
-        for u in range(2):
-            fetch_with(last[u][:], cells[1], pos[1][:, half_list * u : half_list * (u + 1)], f[1][:, 1, cols[u]], ALU.mult)
-        kept1 = sbuf([P, V], F32, "kept1", place["g_turned"])
-        for u in range(2):
-            nc.vector.tensor_tensor(kept1[:, cols[u]], first1[:, cols[u]], last[u][:], ALU.add)
+        first1 = sbuf([P, V], F32, "first1")
+        fetch_with(first1[:], cells[1], pos[0][:], f[1][:, 0, :], ALU.mult)
+        half_list = V // 2 // 16
+        last = [sbuf([P, P], F32, "last0"), sbuf([P, P], F32, "last1", place["fresh"])]
+        fetch_with(last[0][:], cells[1], pos[1][:, :half_list], f[1][:, 1, lo], ALU.mult)
+        part1 = sbuf([P, V], F32, "part1")
+        nc.vector.tensor_tensor(part1[:], first1[:], state_bank[1][:], ALU.add)
+        fetch_with(last[1][:], cells[1], pos[1][:, half_list:], f[1][:, 1, hi], ALU.mult)
         result0 = sbuf([P, V], F32, "result0")
         nc.scalar.activation(result0[:], state_bank[0][:], ACT.Tanh)
         nc.sync.dma_start(out=out[lo, :], in_=result0[:])
         for u in range(2):
             state, result = sbuf([P, P], F32, "state1_%d" % u), sbuf([P, P], F32, "result1_%d" % u)
-            nc.vector.tensor_tensor(state[:], kept1[:, cols[u]], state_bank[1][:, cols[u]], ALU.add)
+            nc.vector.tensor_tensor(state[:], part1[:, cols[u]], last[u][:], ALU.add)
             nc.scalar.activation(result[:], state[:], ACT.Tanh)
             nc.sync.dma_start(out=out[hi, cols[u]], in_=result[:])

@@ -21,9 +21,8 @@ PACK = 4
 RUN = 4
 BLOCKS = N // P
 BANK = 2048
-RAW = PACK * N * 4
 ROW = V * 4
-W3_SHARE = 192
+LEAD = P
 
 
 def tile_picked_ztree_tanh_p_kernel(tc, x_words, x_scales, eT, w1, w2, w3, v1, v2, v3, cell, offs, pos1, pos2, out):
@@ -46,46 +45,57 @@ def tile_picked_ztree_tanh_p_kernel(tc, x_words, x_scales, eT, w1, w2, w3, v1, v
             nc.sync.dma_start(lst[:], src)
             return lst
 
-        def load_matrix(src, name):
-            rows = sbuf([P, PACK, N], F32, "raw_" + name, place[name])
-            nc.sync.dma_start(out=rows[:], in_=src.rearrange("(p j) c -> p j c", j=PACK))
-            return rows
+        def load_matrix(src, name, at=None):
+            flat = sbuf([P, 2 * LEAD + PACK * N], F32, "raw_" + name, at)
+            nc.sync.dma_start(out=flat[:, LEAD : LEAD + PACK * N], in_=src.rearrange("(p j) c -> p (j c)", j=PACK))
+            return flat
 
         def load_cells(b):
             rows = sbuf([P, S], F32, "cell%d" % b)
             nc.sync.dma_start(out=rows[:], in_=cell[b * P : (b + 1) * P, :])
             return rows
 
-        def weave(copy, dst, src):
+        def weave(copy, dst, name, span):
+            src = raw[name][:, LEAD : LEAD + PACK * N].rearrange("p (j c) -> p j c", j=PACK)[:, :, span]
             copy(out=dst.rearrange("p (c i j) -> p c j i", i=RUN, j=PACK), in_=src.rearrange("p j (c i) -> p c j i", i=RUN))
 
-        def weave_on_gpsimd(dst, src):
-            nc.gpsimd.tensor_scalar(dst.rearrange("p (c j) -> p c j", j=PACK), src.rearrange("p j c -> p c j"), 1.0, 0.0, ALU.mult, ALU.add)
-
-        def woven_cols(tile, first, count):
-            return tile[:, PACK * first : PACK * (first + count)]
-
-        def mx_tiles(name, width):
-            return sbuf([P, width], U32, name + "_codes"), sbuf([P, width], U8, name + "_scales")
+        def weave_both(name, engines):
+            woven = sbuf([P, PACK * N], BF16, "woven_" + name)
+            for b in range(BLOCKS):
+                weave(engines[b], woven[:, PACK * P * b : PACK * P * (b + 1)], name, cols[b])
+            return woven
 
         def quantise(woven, name):
-            codes, scales = mx_tiles(name, woven.shape[1] // PACK)
+            width = woven.shape[1] // PACK
+            codes = sbuf([P, width], U32, name + "_codes")
+            scales = sbuf([P, width], U8, name + "_scales")
             nc.vector.quantize_mx(out=codes[:].bitcast(FP8X4), scales=scales[:], in_=woven)
             return codes, scales
 
-        def product(dst, weights, rows, moving, cols):
-            nc.tensor.matmul_mx(out=dst, lhsT=weights[0][:, rows].bitcast(FP8X4), lhsT_scale=weights[1][:, rows],
-                                rhs=moving[0][:, cols].bitcast(FP8X4), rhs_scale=moving[1][:, cols], start=True, stop=True)
+        def product(name, bank, weights, rows, moving, span):
+            dst = psum([P, span.stop - span.start], name, bank)
+            nc.tensor.matmul_mx(out=dst[:], lhsT=weights[0][:, rows].bitcast(FP8X4), lhsT_scale=weights[1][:, rows],
+                                rhs=moving[0][:, span].bitcast(FP8X4), rhs_scale=moving[1][:, span], start=True, stop=True)
+            return dst
 
-        def state_product(weights, rows, name, bank, cols=slice(0, S)):
-            dst = psum([P, cols.stop - cols.start], name, bank)
-            product(dst[:], weights, rows, picked, cols)
+        def node_product(weights, first, name, bank):
+            dst = psum([P, BLOCKS, V], name, bank)
+            for b in range(BLOCKS):
+                rows = slice(first + b * P, first + (b + 1) * P)
+                nc.tensor.matmul_mx(out=dst[:, b, :], lhsT=weights[0][:, rows].bitcast(FP8X4), lhsT_scale=weights[1][:, rows],
+                                    rhs=nodes[0][:].bitcast(FP8X4), rhs_scale=nodes[1][:], start=True, stop=True)
             return dst
 
         def leave_psum(src, name, at=None):
             rows = sbuf(list(src.shape), F32, name, at)
             nc.scalar.copy(out=rows[:], in_=src[:])
             return rows
+
+        def fetch_on_vector(dst, window, offsets):
+            nc.vector.tensor_copy(dst, window[:].indirect(offsets))
+
+        def fetch_on_scalar(dst, window, offsets):
+            nc.scalar.activation(dst, window[:].indirect(offsets), ACT.Copy)
 
         def fetch_with(dst, window, offsets, other, op):
             nc.vector.tensor_tensor(dst, window[:].indirect(offsets), other, op)
@@ -97,9 +107,8 @@ def tile_picked_ztree_tanh_p_kernel(tc, x_words, x_scales, eT, w1, w2, w3, v1, v
             for u in range(2):
                 turn(sums[:, u, :], term[:, cols[u]], start and u == 0, stop and u == 1)
 
-        def gate_term(sums, window, d, term, start=False):
-            nc.vector.tensor_copy(term, window[:].indirect(pos[d][:]))
-            add_turned(sums, term, start=start)
+        def row(name, at=None):
+            return sbuf([P, V], F32, name, at)
 
         def pair(name, at=None):
             return sbuf([P, 2, V], F32, name, at)
@@ -107,8 +116,8 @@ def tile_picked_ztree_tanh_p_kernel(tc, x_words, x_scales, eT, w1, w2, w3, v1, v
         on_scalar, on_vector = nc.scalar.copy, nc.vector.tensor_copy
         lo, hi = slice(0, P), slice(P, 2 * P)
         cols = [lo, hi]
-        everyone = slice(0, V)
-        place = {name: (3 * i + 1) * RAW for i, name in enumerate(("v1", "v2", "e", "v3", "w3", "w1", "w2", "fresh", "woven"))}
+        children, everyone = slice(0, S), slice(0, V)
+        place_fresh, place_e2, place_v2 = 0, 2 * ROW, 4 * ROW
 
         scale_table = sbuf([P, T], U8, "scale_table")
         nc.vector.memset(scale_table[:].bitcast(I32), 0)
@@ -117,9 +126,11 @@ def tile_picked_ztree_tanh_p_kernel(tc, x_words, x_scales, eT, w1, w2, w3, v1, v
         offs_t = load_list(offs, "offs_t")
         for q in range(4):
             nc.sync.dma_start(out=scale_table[32 * q : 32 * q + 4, :].bitcast(I32), in_=x_scales[0, 4 * q : 4 * q + 4, :].bitcast(I32))
-        raw = {name: load_matrix(src, name) for name, src in (("v1", v1), ("v2", v2), ("e", eT))}
-        pos = [load_list(pos1, "pos1_t"), load_list(pos2, "pos2_t")]
-        for name, src in (("v3", v3), ("w3", w3), ("w1", w1), ("w2", w2)):
+        raw = {"v1": load_matrix(v1, "v1"), "v2": load_matrix(v2, "v2", place_v2)}
+        pos = [load_list(pos1, "pos1_t")]
+        raw["v3"] = load_matrix(v3, "v3")
+        pos.append(load_list(pos2, "pos2_t"))
+        for name, src in (("e", eT), ("w3", w3), ("w1", w1), ("w2", w2)):
             raw[name] = load_matrix(src, name)
         cells = [load_cells(b) for b in range(BLOCKS)]
 
@@ -135,117 +146,106 @@ def tile_picked_ztree_tanh_p_kernel(tc, x_words, x_scales, eT, w1, w2, w3, v1, v
         picked = (x_codes, x_bytes)
         nc.vector.tensor_copy(x_codes[:], word_table[:].indirect(offs_t[:]))
         nc.vector.tensor_copy(x_bytes[:], scale_table[:].indirect(offs_t[:]))
+
         woven_v1 = [sbuf([P, PACK * P], BF16, "woven_v1_%d" % b) for b in range(BLOCKS)]
         for b in range(BLOCKS):
-            weave(on_scalar, woven_v1[b][:], raw["v1"][:, :, cols[b]])
+            weave(on_scalar, woven_v1[b][:], "v1", cols[b])
         q_v1 = [quantise(woven_v1[0][:], "v1_0")]
-        h1 = [sbuf([P, S], F32, "h1_0")]
+        woven_v2 = weave_both("v2", (on_scalar, on_vector))
+        q_v1.append(quantise(woven_v1[1][:], "v1_1"))
+        q_v2 = quantise(woven_v2[:], "v2")
+        h1 = [sbuf([P, S], F32, "h1_0", place_v2)]
         for u in range(2):
             half = slice(u * V, (u + 1) * V)
-            nc.scalar.copy(out=h1[0][:, half], in_=state_product(q_v1[0], lo, "h1_0_%d" % u, u, half)[:])
-        q_v1.append(quantise(woven_v1[1][:], "v1_1"))
-        h1.append(leave_psum(state_product(q_v1[1], lo, "h1_1_bank", 3), "h1_1"))
+            nc.scalar.copy(out=h1[0][:, half], in_=product("h1_0_%d" % u, u, q_v1[0], lo, picked, half)[:])
+        h1.append(leave_psum(product("h1_1_bank", 2, q_v1[1], lo, picked, children), "h1_1"))
+        h2 = [leave_psum(product("h2_bank%d" % b, 3 + b, q_v2, cols[b], picked, children), "h2_%d" % b) for b in range(BLOCKS)]
 
-        woven_v2 = sbuf([P, PACK * N], BF16, "woven_v2")
+        woven_v3 = [sbuf([P, PACK * P], BF16, "woven_v3_%d" % b) for b in range(BLOCKS)]
         for b in range(BLOCKS):
-            weave((on_scalar, on_vector)[b], woven_cols(woven_v2, b * P, P), raw["v2"][:, :, cols[b]])
-        q_v2 = quantise(woven_v2[:], "v2")
-        bank2 = [state_product(q_v2, cols[b], "h2_bank%d" % b, 4 + b) for b in range(BLOCKS)]
-        a_bank = psum([P, 2, N], "a_bank", 6)
+            weave(on_vector, woven_v3[b][:], "v3", cols[b])
+        q_v3 = [quantise(woven_v3[b][:], "v3_%d" % b) for b in range(BLOCKS)]
+        a_bank = psum([P, 2, N], "a_bank", 5)
         a_sums = [a_bank[:, :, cols[b]] for b in range(BLOCKS)]
+        g_first1 = row("g_first1")
+        fetch_on_scalar(g_first1[:], h2[1], pos[0][:])
+        g_sums = [psum([P, 2, P], "g_bank%d" % b, (2, 7)[b]) for b in range(BLOCKS)]
+        for d in range(2):
+            term = row("g_term0_%d" % d)
+            fetch_on_scalar(term[:], h2[0], pos[d][:])
+            add_turned(g_sums[0], term[:], start=(d == 0))
+        a_terms1 = [row("a_term1_%d" % d) for d in range(2)]
+        for d in range(2):
+            fetch_on_scalar(a_terms1[d][:], h1[1], pos[d][:])
+        h3 = [leave_psum(product("h3_bank%d" % b, b, q_v3[b], lo, picked, children), "h3_%d" % b) for b in range(BLOCKS)]
 
-        def node_product(weights, name, bank):
-            dst = psum([P, BLOCKS, V], name, bank)
-            for b in range(BLOCKS):
-                product(dst[:, b, :], weights, cols[b], nodes, everyone)
-            return dst
-
-        woven_e = sbuf([P, PACK * N], BF16, "woven_e", place["woven"])
-        weave(on_vector, woven_e[:], raw["e"][:])
-        gate_term(a_sums[0], h1[0], 0, sbuf([P, V], F32, "a_first")[:], start=True)
+        woven_e = weave_both("e", (on_vector, on_vector))
+        fetch_on_vector(raw["e"][:, everyone], h1[0], pos[0][:])
+        add_turned(a_sums[0], raw["e"][:, everyone], start=True)
         nodes = quantise(woven_e[:], "e")
-        after_e = sbuf([P, 4, V], F32, "after_e", place["e"])
-        gate_term(a_sums[1], h1[1], 0, after_e[:, 0, :])
-        h2 = [leave_psum(bank2[b], "h2_%d" % b) for b in range(BLOCKS)]
-        for b in range(BLOCKS):
-            gate_term(a_sums[b], h1[b], 1, after_e[:, 1 + b, :])
-        g_first = [after_e[:, 3, :]]
-        nc.vector.tensor_copy(g_first[0], h2[0][:].indirect(pos[0][:]))
-        woven_v3 = sbuf([P, PACK * N], BF16, "woven_v3")
-        weave(on_scalar, woven_v3[:], raw["v3"][:])
-        woven_w3 = sbuf([P, PACK * N], BF16, "woven_w3", place["woven"])
-        weave_on_gpsimd(woven_cols(woven_w3, 0, W3_SHARE), raw["w3"][:, :, :W3_SHARE])
-        weave(on_scalar, woven_cols(woven_w3, W3_SHARE, N - W3_SHARE), raw["w3"][:, :, W3_SHARE:])
-        woven_w1 = sbuf([P, PACK * N], BF16, "woven_w1")
-        weave(on_scalar, woven_w1[:], raw["w1"][:])
-        q_v3 = quantise(woven_v3[:], "v3")
-        q_w3 = quantise(woven_w3[:], "w3")
-        bank3 = [state_product(q_v3, cols[b], "h3_bank%d" % b, b) for b in range(BLOCKS)]
-        ebank3 = [psum([P, V], "e3_bank%d" % b, 2 + b) for b in range(BLOCKS)]
-        for b in range(BLOCKS):
-            product(ebank3[b][:], q_w3, cols[b], nodes, everyone)
-        g_first.append(sbuf([P, V], F32, "g_first1", place["w3"])[:])
-        nc.vector.tensor_copy(g_first[1], h2[1][:].indirect(pos[0][:]))
-        after_w1 = sbuf([P, 4, V], F32, "after_w1", place["w1"] + 3 * ROW)
-        g_both = [after_w1[:, 2 + b, :] for b in range(BLOCKS)]
-        ebank1 = node_product(quantise(woven_w1[:], "w1"), "e1_bank", 4)
-        for b in range(BLOCKS):
-            fetch_with(g_both[b], h2[b], pos[1][:], g_first[b], ALU.add)
-        g_sums = [psum([P, 2, P], "g_bank0", 7)]
-        add_turned(g_sums[0], g_both[0], start=True)
-        woven_w2 = sbuf([P, PACK * N], BF16, "woven_w2")
-        weave(on_scalar, woven_w2[:], raw["w2"][:])
-        h3 = [leave_psum(bank3[0], "h3_0", place["w1"] - ROW)]
-        nc.scalar.copy(out=after_w1[:, 0, :], in_=ebank3[0][:])
-        ebank2 = node_product(quantise(woven_w2[:], "w2"), "e2_bank", 5)
-        h3.append(leave_psum(bank3[1], "h3_1", place["w1"] + ROW))
-        nc.scalar.copy(out=after_w1[:, 1, :], in_=ebank3[1][:])
-        g_sums.append(psum([P, 2, P], "g_bank1", 1))
-        add_turned(g_sums[1], g_both[1], start=True)
-        e1 = leave_psum(ebank1, "e1")
-        for b in range(BLOCKS):
-            add_turned(a_sums[b], e1[:, b, :], stop=(b == BLOCKS - 1))
-        e2 = leave_psum(ebank2, "e2")
-        for b in reversed(range(BLOCKS)):
-            add_turned(g_sums[b], e2[:, b, :], stop=True)
 
-        f_pre = [pair("f_pre%d" % b, place["w2"] + 2 * ROW * b) for b in range(BLOCKS)]
-        f = [pair("f%d" % b) for b in range(BLOCKS)]
+        woven_w3 = weave_both("w3", (on_vector, on_vector))
+        fetch_on_vector(raw["w3"][:, everyone], h1[0], pos[1][:])
+        add_turned(a_sums[0], raw["w3"][:, everyone])
+        q_w3 = quantise(woven_w3[:], "w3")
+        e3 = [leave_psum(product("e3_bank%d" % b, 3 + b, q_w3, cols[b], nodes, everyone), "e3_%d" % b) for b in range(BLOCKS)]
+        for d in range(2):
+            add_turned(a_sums[1], a_terms1[d][:])
+
+        woven_w = sbuf([P, 2 * PACK * N], BF16, "woven_w")
+        weave(on_vector, woven_w[:, : PACK * N], "w1", slice(0, N))
+        for b in range(BLOCKS):
+            weave(on_vector, woven_w[:, PACK * (N + P * b) : PACK * (N + P * (b + 1))], "w2", cols[b])
+        fetch_with(raw["w2"][:, everyone], h2[1], pos[1][:], g_first1[:], ALU.add)
+        q_w = quantise(woven_w[:], "w")
+        add_turned(g_sums[1], raw["w2"][:, everyone], start=True)
+        ebank1 = node_product(q_w, 0, "e1_bank", 0)
+        ebank2 = node_product(q_w, N, "e2_bank", 6)
+        e1 = leave_psum(ebank1, "e1")
+        e2 = leave_psum(ebank2, "e2", place_e2)
+        f_pre = [raw["w2"][:, V + 2 * V * b : V + 2 * V * (b + 1)] for b in range(BLOCKS)]
         for b in range(BLOCKS):
             for d in range(2):
-                fetch_with(f_pre[b][:, d, :], h3[b], pos[d][:], after_w1[:, b, :], ALU.add)
-        nc.scalar.activation(f[0][:], f_pre[0][:], ACT.Sigmoid)
+                fetch_with(f_pre[b][:, d * V : (d + 1) * V], h3[b], pos[d][:], e3[b][:], ALU.add)
+        for b in range(BLOCKS):
+            add_turned(a_sums[b], e1[:, b, :], stop=(b == BLOCKS - 1))
+
+        f = [sbuf([P, 2 * V], F32, "f0")]
+        nc.scalar.activation(f[0][:], f_pre[0], ACT.Sigmoid)
+        for b in reversed(range(BLOCKS)):
+            add_turned(g_sums[b], e2[:, b, :], stop=True)
         a_turned = pair("a_turned")
         g_turned = pair("g_turned")
         nc.scalar.activation(a_turned[:], a_bank[:], ACT.Sigmoid)
         for b in reversed(range(BLOCKS)):
             nc.scalar.activation(g_turned[:, :, cols[b]], g_sums[b][:], ACT.Tanh)
-        nc.scalar.activation(f[1][:], f_pre[1][:], ACT.Sigmoid)
+        f.append(sbuf([P, 2 * V], F32, "f1", place_e2))
+        nc.scalar.activation(f[1][:], f_pre[1], ACT.Sigmoid)
 
         fc0 = pair("fc0")
-        kept_bank = psum([P, 2, P], "kept_bank", 0)
+        kept_bank = psum([P, 2, P], "kept_bank", 6)
         for d in range(2):
-            fetch_with(fc0[:, d, :], cells[0], pos[d][:], f[0][:, d, :], ALU.mult)
+            fetch_with(fc0[:, d, :], cells[0], pos[d][:], f[0][:, d * V : (d + 1) * V], ALU.mult)
             add_turned(kept_bank, fc0[:, d, :], start=(d == 0), stop=(d == 1))
         kept0_turned = leave_psum(kept_bank, "kept0_turned")
-        fresh_turned = pair("fresh_turned", place["fresh"])
+        fresh_turned = pair("fresh_turned", place_fresh)
         nc.vector.tensor_tensor(fresh_turned[:], a_turned[:], g_turned[:], ALU.mult)
-        state_bank = [psum([P, V], "state_bank%d" % b, 2 + b) for b in range(BLOCKS)]
+        state_bank = [psum([P, V], "state_bank%d" % b, (3, 4)[b]) for b in range(BLOCKS)]
         for u in range(2):
             turn(state_bank[1][:, cols[u]], fresh_turned[:, u, hi], True, True)
         for u in range(2):
             turn(state_bank[0][:, cols[u]], fresh_turned[:, u, lo], u == 0, False)
         for u in range(2):
             turn(state_bank[0][:, cols[u]], kept0_turned[:, u, :], False, u == 1)
-        first1 = sbuf([P, V], F32, "first1")
-        fetch_with(first1[:], cells[1], pos[0][:], f[1][:, 0, :], ALU.mult)
+        first1 = row("first1")
+        fetch_with(first1[:], cells[1], pos[0][:], f[1][:, :V], ALU.mult)
         half_list = V // 2 // 16
-        last = [sbuf([P, P], F32, "last0"), sbuf([P, P], F32, "last1", place["fresh"])]
-        fetch_with(last[0][:], cells[1], pos[1][:, :half_list], f[1][:, 1, lo], ALU.mult)
-        part1 = sbuf([P, V], F32, "part1")
+        last = [sbuf([P, P], F32, "last0"), sbuf([P, P], F32, "last1", place_fresh)]
+        fetch_with(last[0][:], cells[1], pos[1][:, :half_list], f[1][:, V : V + P], ALU.mult)
+        part1 = row("part1")
         nc.vector.tensor_tensor(part1[:], first1[:], state_bank[1][:], ALU.add)
-        fetch_with(last[1][:], cells[1], pos[1][:, half_list:], f[1][:, 1, hi], ALU.mult)
-        result0 = sbuf([P, V], F32, "result0")
+        fetch_with(last[1][:], cells[1], pos[1][:, half_list:], f[1][:, V + P :], ALU.mult)
+        result0 = row("result0")
         nc.scalar.activation(result0[:], state_bank[0][:], ACT.Tanh)
         nc.sync.dma_start(out=out[lo, :], in_=result0[:])
         for u in range(2):

@@ -45,8 +45,8 @@ def tile_picked_ztree_tanh_p_kernel(tc, x_words, x_scales, eT, w1, w2, w3, v1, v
             nc.sync.dma_start(lst[:], src)
             return lst
 
-        def load_matrix(src, name, at=None):
-            flat = sbuf([P, 2 * LEAD + PACK * N], F32, "raw_" + name, at)
+        def load_matrix(src, name):
+            flat = sbuf([P, 2 * LEAD + PACK * N], F32, "raw_" + name)
             nc.sync.dma_start(out=flat[:, LEAD : LEAD + PACK * N], in_=src.rearrange("(p j) c -> p (j c)", j=PACK))
             return flat
 
@@ -117,7 +117,7 @@ def tile_picked_ztree_tanh_p_kernel(tc, x_words, x_scales, eT, w1, w2, w3, v1, v
         lo, hi = slice(0, P), slice(P, 2 * P)
         cols = [lo, hi]
         children, everyone = slice(0, S), slice(0, V)
-        place_fresh, place_e2, place_v2 = 0, 2 * ROW, 4 * ROW
+        place_e2 = ROW
 
         scale_table = sbuf([P, T], U8, "scale_table")
         nc.vector.memset(scale_table[:].bitcast(I32), 0)
@@ -126,7 +126,7 @@ def tile_picked_ztree_tanh_p_kernel(tc, x_words, x_scales, eT, w1, w2, w3, v1, v
         offs_t = load_list(offs, "offs_t")
         for q in range(4):
             nc.sync.dma_start(out=scale_table[32 * q : 32 * q + 4, :].bitcast(I32), in_=x_scales[0, 4 * q : 4 * q + 4, :].bitcast(I32))
-        raw = {"v1": load_matrix(v1, "v1"), "v2": load_matrix(v2, "v2", place_v2)}
+        raw = {"v1": load_matrix(v1, "v1"), "v2": load_matrix(v2, "v2")}
         pos = [load_list(pos1, "pos1_t")]
         raw["v3"] = load_matrix(v3, "v3")
         pos.append(load_list(pos2, "pos2_t"))
@@ -154,7 +154,7 @@ def tile_picked_ztree_tanh_p_kernel(tc, x_words, x_scales, eT, w1, w2, w3, v1, v
         woven_v2 = weave_both("v2", (on_scalar, on_vector))
         q_v1.append(quantise(woven_v1[1][:], "v1_1"))
         q_v2 = quantise(woven_v2[:], "v2")
-        h1 = [sbuf([P, S], F32, "h1_0", place_v2)]
+        h1 = [sbuf([P, S], F32, "h1_0")]
         for u in range(2):
             half = slice(u * V, (u + 1) * V)
             nc.scalar.copy(out=h1[0][:, half], in_=product("h1_0_%d" % u, u, q_v1[0], lo, picked, half)[:])
@@ -165,10 +165,9 @@ def tile_picked_ztree_tanh_p_kernel(tc, x_words, x_scales, eT, w1, w2, w3, v1, v
         for b in range(BLOCKS):
             weave(on_vector, woven_v3[b][:], "v3", cols[b])
         q_v3 = [quantise(woven_v3[b][:], "v3_%d" % b) for b in range(BLOCKS)]
+        bank3 = [product("h3_bank%d" % b, b, q_v3[b], lo, picked, children) for b in range(BLOCKS)]
         a_bank = psum([P, 2, N], "a_bank", 5)
         a_sums = [a_bank[:, :, cols[b]] for b in range(BLOCKS)]
-        g_first1 = row("g_first1")
-        fetch_on_scalar(g_first1[:], h2[1], pos[0][:])
         g_sums = [psum([P, 2, P], "g_bank%d" % b, (2, 7)[b]) for b in range(BLOCKS)]
         for d in range(2):
             term = row("g_term0_%d" % d)
@@ -177,30 +176,32 @@ def tile_picked_ztree_tanh_p_kernel(tc, x_words, x_scales, eT, w1, w2, w3, v1, v
         a_terms1 = [row("a_term1_%d" % d) for d in range(2)]
         for d in range(2):
             fetch_on_scalar(a_terms1[d][:], h1[1], pos[d][:])
-        h3 = [leave_psum(product("h3_bank%d" % b, b, q_v3[b], lo, picked, children), "h3_%d" % b) for b in range(BLOCKS)]
+        g_first1 = row("g_first1")
+        fetch_on_scalar(g_first1[:], h2[1], pos[0][:])
+        h3 = [leave_psum(bank3[b], "h3_%d" % b) for b in range(BLOCKS)]
 
         woven_e = weave_both("e", (on_vector, on_vector))
         fetch_on_vector(raw["e"][:, everyone], h1[0], pos[0][:])
         add_turned(a_sums[0], raw["e"][:, everyone], start=True)
         nodes = quantise(woven_e[:], "e")
-
-        woven_w3 = weave_both("w3", (on_vector, on_vector))
-        fetch_on_vector(raw["w3"][:, everyone], h1[0], pos[1][:])
-        add_turned(a_sums[0], raw["w3"][:, everyone])
-        q_w3 = quantise(woven_w3[:], "w3")
-        e3 = [leave_psum(product("e3_bank%d" % b, 3 + b, q_w3, cols[b], nodes, everyone), "e3_%d" % b) for b in range(BLOCKS)]
         for d in range(2):
             add_turned(a_sums[1], a_terms1[d][:])
 
         woven_w = sbuf([P, 2 * PACK * N], BF16, "woven_w")
-        weave(on_vector, woven_w[:, : PACK * N], "w1", slice(0, N))
+        weave(on_vector, woven_w[:, : PACK * N], "w3", slice(0, N))
         for b in range(BLOCKS):
-            weave(on_vector, woven_w[:, PACK * (N + P * b) : PACK * (N + P * (b + 1))], "w2", cols[b])
-        fetch_with(raw["w2"][:, everyone], h2[1], pos[1][:], g_first1[:], ALU.add)
+            weave(on_vector, woven_w[:, PACK * (N + P * b) : PACK * (N + P * (b + 1))], "w1", cols[b])
+        fetch_on_vector(raw["w1"][:, everyone], h1[0], pos[1][:])
+        add_turned(a_sums[0], raw["w1"][:, everyone])
         q_w = quantise(woven_w[:], "w")
+        ebank3 = [product("e3_bank%d" % b, 3 + b, q_w, cols[b], nodes, everyone) for b in range(BLOCKS)]
+        ebank1 = node_product(q_w, N, "e1_bank", 6)
+        e3 = [leave_psum(ebank3[b], "e3_%d" % b) for b in range(BLOCKS)]
+
+        woven_w2 = weave_both("w2", (on_vector, on_vector))
+        fetch_with(raw["w2"][:, everyone], h2[1], pos[1][:], g_first1[:], ALU.add)
         add_turned(g_sums[1], raw["w2"][:, everyone], start=True)
-        ebank1 = node_product(q_w, 0, "e1_bank", 0)
-        ebank2 = node_product(q_w, N, "e2_bank", 6)
+        ebank2 = node_product(quantise(woven_w2[:], "w2"), 0, "e2_bank", 0)
         e1 = leave_psum(ebank1, "e1")
         e2 = leave_psum(ebank2, "e2", place_e2)
         f_pre = [raw["w2"][:, V + 2 * V * b : V + 2 * V * (b + 1)] for b in range(BLOCKS)]
@@ -219,16 +220,18 @@ def tile_picked_ztree_tanh_p_kernel(tc, x_words, x_scales, eT, w1, w2, w3, v1, v
         nc.scalar.activation(a_turned[:], a_bank[:], ACT.Sigmoid)
         for b in reversed(range(BLOCKS)):
             nc.scalar.activation(g_turned[:, :, cols[b]], g_sums[b][:], ACT.Tanh)
-        f.append(sbuf([P, 2 * V], F32, "f1", place_e2))
+        f.append(sbuf([P, 2 * V], F32, "f1", place_e2 - ROW))
         nc.scalar.activation(f[1][:], f_pre[1], ACT.Sigmoid)
+        cells11 = row("cells11", place_e2 + ROW)
+        fetch_on_scalar(cells11[:], cells[1], pos[1][:])
 
         fc0 = pair("fc0")
-        kept_bank = psum([P, 2, P], "kept_bank", 6)
+        kept_bank = psum([P, 2, P], "kept_bank", 0)
         for d in range(2):
             fetch_with(fc0[:, d, :], cells[0], pos[d][:], f[0][:, d * V : (d + 1) * V], ALU.mult)
             add_turned(kept_bank, fc0[:, d, :], start=(d == 0), stop=(d == 1))
         kept0_turned = leave_psum(kept_bank, "kept0_turned")
-        fresh_turned = pair("fresh_turned", place_fresh)
+        fresh_turned = pair("fresh_turned")
         nc.vector.tensor_tensor(fresh_turned[:], a_turned[:], g_turned[:], ALU.mult)
         state_bank = [psum([P, V], "state_bank%d" % b, (3, 4)[b]) for b in range(BLOCKS)]
         for u in range(2):
@@ -239,17 +242,16 @@ def tile_picked_ztree_tanh_p_kernel(tc, x_words, x_scales, eT, w1, w2, w3, v1, v
             turn(state_bank[0][:, cols[u]], kept0_turned[:, u, :], False, u == 1)
         first1 = row("first1")
         fetch_with(first1[:], cells[1], pos[0][:], f[1][:, :V], ALU.mult)
-        half_list = V // 2 // 16
-        last = [sbuf([P, P], F32, "last0"), sbuf([P, P], F32, "last1", place_fresh)]
-        fetch_with(last[0][:], cells[1], pos[1][:, :half_list], f[1][:, V : V + P], ALU.mult)
-        part1 = row("part1")
-        nc.vector.tensor_tensor(part1[:], first1[:], state_bank[1][:], ALU.add)
-        fetch_with(last[1][:], cells[1], pos[1][:, half_list:], f[1][:, V + P :], ALU.mult)
+        last1 = row("last1")
+        nc.vector.tensor_tensor(last1[:], cells11[:], f[1][:, V:], ALU.mult)
+        part1 = [sbuf([P, P], F32, "part1_%d" % u) for u in range(2)]
+        for u in range(2):
+            nc.vector.tensor_tensor(part1[u][:], first1[:, cols[u]], state_bank[1][:, cols[u]], ALU.add)
         result0 = row("result0")
         nc.scalar.activation(result0[:], state_bank[0][:], ACT.Tanh)
         nc.sync.dma_start(out=out[lo, :], in_=result0[:])
         for u in range(2):
             state, result = sbuf([P, P], F32, "state1_%d" % u), sbuf([P, P], F32, "result1_%d" % u)
-            nc.vector.tensor_tensor(state[:], part1[:, cols[u]], last[u][:], ALU.add)
+            nc.vector.tensor_tensor(state[:], part1[u][:], last1[:, cols[u]], ALU.add)
             nc.scalar.activation(result[:], state[:], ACT.Tanh)
             nc.sync.dma_start(out=out[hi, cols[u]], in_=result[:])

@@ -23,6 +23,7 @@ BLOCKS = N // P
 BANK = 2048
 ROW = V * 4
 LEAD = P
+V2_SHARE = 96
 
 
 def tile_picked_ztree_tanh_p_kernel(tc, x_words, x_scales, eT, w1, w2, w3, v1, v2, v3, cell, offs, pos1, pos2, out):
@@ -59,10 +60,10 @@ def tile_picked_ztree_tanh_p_kernel(tc, x_words, x_scales, eT, w1, w2, w3, v1, v
             src = raw[name][:, LEAD : LEAD + PACK * N].rearrange("p (j c) -> p j c", j=PACK)[:, :, span]
             copy(out=dst.rearrange("p (c i j) -> p c j i", i=RUN, j=PACK), in_=src.rearrange("p j (c i) -> p c j i", i=RUN))
 
-        def weave_both(name, engines):
-            woven = sbuf([P, PACK * N], BF16, "woven_" + name)
-            for b in range(BLOCKS):
-                weave(engines[b], woven[:, PACK * P * b : PACK * P * (b + 1)], name, cols[b])
+        def weave_both(name, engines, at=None, cut=P):
+            woven = sbuf([P, PACK * N], BF16, "woven_" + name, at)
+            for engine, span in zip(engines, (slice(0, cut), slice(cut, N))):
+                weave(engine, woven[:, PACK * span.start : PACK * span.stop], name, span)
             return woven
 
         def quantise(woven, name):
@@ -91,6 +92,13 @@ def tile_picked_ztree_tanh_p_kernel(tc, x_words, x_scales, eT, w1, w2, w3, v1, v
             nc.scalar.copy(out=rows[:], in_=src[:])
             return rows
 
+        def state_row_in_halves(name, first_bank, weights, rows):
+            dst = sbuf([P, S], F32, name)
+            for u in range(2):
+                half = slice(u * V, (u + 1) * V)
+                nc.scalar.copy(out=dst[:, half], in_=product("%s_bank%d" % (name, u), first_bank + u, weights, rows, picked, half)[:])
+            return dst
+
         def fetch_on_vector(dst, window, offsets):
             nc.vector.tensor_copy(dst, window[:].indirect(offsets))
 
@@ -117,7 +125,7 @@ def tile_picked_ztree_tanh_p_kernel(tc, x_words, x_scales, eT, w1, w2, w3, v1, v
         lo, hi = slice(0, P), slice(P, 2 * P)
         cols = [lo, hi]
         children, everyone = slice(0, S), slice(0, V)
-        place_e2 = ROW
+        place_e2, place_e1, place_v3 = ROW, 4 * ROW, 6 * ROW
 
         scale_table = sbuf([P, T], U8, "scale_table")
         nc.vector.memset(scale_table[:].bitcast(I32), 0)
@@ -151,31 +159,29 @@ def tile_picked_ztree_tanh_p_kernel(tc, x_words, x_scales, eT, w1, w2, w3, v1, v
         for b in range(BLOCKS):
             weave(on_scalar, woven_v1[b][:], "v1", cols[b])
         q_v1 = [quantise(woven_v1[0][:], "v1_0")]
-        woven_v2 = weave_both("v2", (on_scalar, on_vector))
+        woven_v2 = weave_both("v2", (on_scalar, on_vector), cut=V2_SHARE)
         q_v1.append(quantise(woven_v1[1][:], "v1_1"))
         q_v2 = quantise(woven_v2[:], "v2")
-        h1 = [sbuf([P, S], F32, "h1_0")]
-        for u in range(2):
-            half = slice(u * V, (u + 1) * V)
-            nc.scalar.copy(out=h1[0][:, half], in_=product("h1_0_%d" % u, u, q_v1[0], lo, picked, half)[:])
-        h1.append(leave_psum(product("h1_1_bank", 2, q_v1[1], lo, picked, children), "h1_1"))
-        h2 = [leave_psum(product("h2_bank%d" % b, 3 + b, q_v2, cols[b], picked, children), "h2_%d" % b) for b in range(BLOCKS)]
+        h1 = [state_row_in_halves("h1_%d" % b, 2 * b, q_v1[b], lo) for b in range(BLOCKS)]
+        h2 = [state_row_in_halves("h2_0", 0, q_v2, lo)]
+        bank2 = product("h2_bank1", 4, q_v2, hi, picked, children)
 
-        woven_v3 = [sbuf([P, PACK * P], BF16, "woven_v3_%d" % b) for b in range(BLOCKS)]
+        woven_v3 = [sbuf([P, PACK * P], BF16, "woven_v3_%d" % b, (None, place_v3)[b]) for b in range(BLOCKS)]
         for b in range(BLOCKS):
             weave(on_vector, woven_v3[b][:], "v3", cols[b])
         q_v3 = [quantise(woven_v3[b][:], "v3_%d" % b) for b in range(BLOCKS)]
-        bank3 = [product("h3_bank%d" % b, b, q_v3[b], lo, picked, children) for b in range(BLOCKS)]
+        bank3 = [product("h3_bank%d" % b, 2 + b, q_v3[b], lo, picked, children) for b in range(BLOCKS)]
         a_bank = psum([P, 2, N], "a_bank", 5)
         a_sums = [a_bank[:, :, cols[b]] for b in range(BLOCKS)]
-        g_sums = [psum([P, 2, P], "g_bank%d" % b, (2, 7)[b]) for b in range(BLOCKS)]
+        a_terms1 = [row("a_term1_%d" % d) for d in range(2)]
+        fetch_on_scalar(a_terms1[0][:], h1[1], pos[0][:])
+        g_sums = [psum([P, 2, P], "g_bank0", 7)]
         for d in range(2):
             term = row("g_term0_%d" % d)
             fetch_on_scalar(term[:], h2[0], pos[d][:])
             add_turned(g_sums[0], term[:], start=(d == 0))
-        a_terms1 = [row("a_term1_%d" % d) for d in range(2)]
-        for d in range(2):
-            fetch_on_scalar(a_terms1[d][:], h1[1], pos[d][:])
+        h2.append(leave_psum(bank2, "h2_1", place_v3))
+        fetch_on_scalar(a_terms1[1][:], h1[1], pos[1][:])
         g_first1 = row("g_first1")
         fetch_on_scalar(g_first1[:], h2[1], pos[0][:])
         h3 = [leave_psum(bank3[b], "h3_%d" % b) for b in range(BLOCKS)]
@@ -194,15 +200,16 @@ def tile_picked_ztree_tanh_p_kernel(tc, x_words, x_scales, eT, w1, w2, w3, v1, v
         fetch_on_vector(raw["w1"][:, everyone], h1[0], pos[1][:])
         add_turned(a_sums[0], raw["w1"][:, everyone])
         q_w = quantise(woven_w[:], "w")
-        ebank3 = [product("e3_bank%d" % b, 3 + b, q_w, cols[b], nodes, everyone) for b in range(BLOCKS)]
+        ebank3 = [product("e3_bank%d" % b, b, q_w, cols[b], nodes, everyone) for b in range(BLOCKS)]
         ebank1 = node_product(q_w, N, "e1_bank", 6)
         e3 = [leave_psum(ebank3[b], "e3_%d" % b) for b in range(BLOCKS)]
 
-        woven_w2 = weave_both("w2", (on_vector, on_vector))
+        woven_w2 = weave_both("w2", (on_vector, on_vector), place_e1)
         fetch_with(raw["w2"][:, everyone], h2[1], pos[1][:], g_first1[:], ALU.add)
-        add_turned(g_sums[1], raw["w2"][:, everyone], start=True)
-        ebank2 = node_product(quantise(woven_w2[:], "w2"), 0, "e2_bank", 0)
-        e1 = leave_psum(ebank1, "e1")
+        ebank2 = node_product(quantise(woven_w2[:], "w2"), 0, "e2_bank", 4)
+        cells00 = row("cells00")
+        fetch_on_scalar(cells00[:], cells[0], pos[0][:])
+        e1 = leave_psum(ebank1, "e1", place_e1)
         e2 = leave_psum(ebank2, "e2", place_e2)
         f_pre = [raw["w2"][:, V + 2 * V * b : V + 2 * V * (b + 1)] for b in range(BLOCKS)]
         for b in range(BLOCKS):
@@ -210,6 +217,8 @@ def tile_picked_ztree_tanh_p_kernel(tc, x_words, x_scales, eT, w1, w2, w3, v1, v
                 fetch_with(f_pre[b][:, d * V : (d + 1) * V], h3[b], pos[d][:], e3[b][:], ALU.add)
         for b in range(BLOCKS):
             add_turned(a_sums[b], e1[:, b, :], stop=(b == BLOCKS - 1))
+        g_sums.append(psum([P, 2, P], "g_bank1", 6))
+        add_turned(g_sums[1], raw["w2"][:, everyone], start=True)
 
         f = [sbuf([P, 2 * V], F32, "f0")]
         nc.scalar.activation(f[0][:], f_pre[0], ACT.Sigmoid)
@@ -226,14 +235,15 @@ def tile_picked_ztree_tanh_p_kernel(tc, x_words, x_scales, eT, w1, w2, w3, v1, v
         fetch_on_scalar(cells11[:], cells[1], pos[1][:])
 
         fc0 = pair("fc0")
-        kept_bank = psum([P, 2, P], "kept_bank", 0)
+        kept_bank = psum([P, 2, P], "kept_bank", 4)
+        nc.vector.tensor_tensor(fc0[:, 0, :], cells00[:], f[0][:, :V], ALU.mult)
+        fetch_with(fc0[:, 1, :], cells[0], pos[1][:], f[0][:, V:], ALU.mult)
         for d in range(2):
-            fetch_with(fc0[:, d, :], cells[0], pos[d][:], f[0][:, d * V : (d + 1) * V], ALU.mult)
             add_turned(kept_bank, fc0[:, d, :], start=(d == 0), stop=(d == 1))
         kept0_turned = leave_psum(kept_bank, "kept0_turned")
         fresh_turned = pair("fresh_turned")
         nc.vector.tensor_tensor(fresh_turned[:], a_turned[:], g_turned[:], ALU.mult)
-        state_bank = [psum([P, V], "state_bank%d" % b, (3, 4)[b]) for b in range(BLOCKS)]
+        state_bank = [psum([P, V], "state_bank%d" % b, 2 + b) for b in range(BLOCKS)]
         for u in range(2):
             turn(state_bank[1][:, cols[u]], fresh_turned[:, u, hi], True, True)
         for u in range(2):

@@ -58,7 +58,10 @@ def tile_picked_ztree_tanh_p_kernel(tc, x_words, x_scales, eT, w1, w2, w3, v1, v
 
         def weave(copy, dst, name, span):
             src = raw[name][:, LEAD : LEAD + PACK * N].rearrange("p (j c) -> p j c", j=PACK)[:, :, span]
-            copy(out=dst.rearrange("p (c i j) -> p c j i", i=RUN, j=PACK), in_=src.rearrange("p j (c i) -> p c j i", i=RUN))
+            if copy is on_vector:
+                copy(out=dst.rearrange("p (c i h j) -> p c h i j", i=RUN, h=2, j=2), in_=src.rearrange("p (h j) (c i) -> p c h i j", i=RUN, j=2))
+            else:
+                copy(out=dst.rearrange("p (c i j) -> p c j i", i=RUN, j=PACK), in_=src.rearrange("p j (c i) -> p c j i", i=RUN))
 
         def weave_both(name, engines, at=None, cut=P):
             woven = sbuf([P, PACK * N], BF16, "woven_" + name, at)
@@ -73,17 +76,22 @@ def tile_picked_ztree_tanh_p_kernel(tc, x_words, x_scales, eT, w1, w2, w3, v1, v
             nc.vector.quantize_mx(out=codes[:].bitcast(FP8X4), scales=scales[:], in_=woven)
             return codes, scales
 
+        def round_and_quantise_in_halves(name):
+            woven = [sbuf([P, PACK * P], BF16, "woven_%s_%d" % (name, b)) for b in range(BLOCKS)]
+            for b in range(BLOCKS):
+                weave(on_vector, woven[b][:], name, cols[b])
+            return [quantise(woven[b][:], "%s_%d" % (name, b)) for b in range(BLOCKS)]
+
         def product(name, bank, weights, rows, moving, span):
             dst = psum([P, span.stop - span.start], name, bank)
             nc.tensor.matmul_mx(out=dst[:], lhsT=weights[0][:, rows].bitcast(FP8X4), lhsT_scale=weights[1][:, rows],
                                 rhs=moving[0][:, span].bitcast(FP8X4), rhs_scale=moving[1][:, span], start=True, stop=True)
             return dst
 
-        def node_product(weights, first, name, bank):
+        def node_product(weights, name, bank):
             dst = psum([P, BLOCKS, V], name, bank)
             for b in range(BLOCKS):
-                rows = slice(first + b * P, first + (b + 1) * P)
-                nc.tensor.matmul_mx(out=dst[:, b, :], lhsT=weights[0][:, rows].bitcast(FP8X4), lhsT_scale=weights[1][:, rows],
+                nc.tensor.matmul_mx(out=dst[:, b, :], lhsT=weights[b][0][:].bitcast(FP8X4), lhsT_scale=weights[b][1][:],
                                     rhs=nodes[0][:].bitcast(FP8X4), rhs_scale=nodes[1][:], start=True, stop=True)
             return dst
 
@@ -140,7 +148,7 @@ def tile_picked_ztree_tanh_p_kernel(tc, x_words, x_scales, eT, w1, w2, w3, v1, v
         pos.append(load_list(pos2, "pos2_t"))
         for name, src in (("e", eT), ("w3", w3), ("w1", w1), ("w2", w2)):
             raw[name] = load_matrix(src, name)
-        cells = [load_cells(b) for b in range(BLOCKS)]
+        cells = {b: load_cells(b) for b in reversed(range(BLOCKS))}
 
         warm = sbuf([P, 16], F32, "warm")
         nc.vector.memset(warm[:, 0:8], 0.0)
@@ -166,50 +174,49 @@ def tile_picked_ztree_tanh_p_kernel(tc, x_words, x_scales, eT, w1, w2, w3, v1, v
         h2 = [state_row_in_halves("h2_0", 0, q_v2, lo)]
         bank2 = product("h2_bank1", 4, q_v2, hi, picked, children)
 
-        woven_v3 = [sbuf([P, PACK * P], BF16, "woven_v3_%d" % b, (None, place_v3)[b]) for b in range(BLOCKS)]
-        for b in range(BLOCKS):
-            weave(on_vector, woven_v3[b][:], "v3", cols[b])
-        q_v3 = [quantise(woven_v3[b][:], "v3_%d" % b) for b in range(BLOCKS)]
-        bank3 = [product("h3_bank%d" % b, 2 + b, q_v3[b], lo, picked, children) for b in range(BLOCKS)]
+        woven_v3 = weave_both("v3", (on_vector, on_vector), place_v3)
         a_bank = psum([P, 2, N], "a_bank", 5)
         a_sums = [a_bank[:, :, cols[b]] for b in range(BLOCKS)]
+        fetch_on_vector(raw["v3"][:, everyone], h1[0], pos[0][:])
+        add_turned(a_sums[0], raw["v3"][:, everyone], start=True)
+        q_v3 = quantise(woven_v3[:], "v3")
+        bank3 = [product("h3_bank%d" % b, 2 + b, q_v3, cols[b], picked, children) for b in range(BLOCKS)]
         a_terms1 = [row("a_term1_%d" % d) for d in range(2)]
+        g_terms0 = [row("g_term0_%d" % d) for d in range(2)]
         fetch_on_scalar(a_terms1[0][:], h1[1], pos[0][:])
+        add_turned(a_sums[1], a_terms1[0][:])
         g_sums = [psum([P, 2, P], "g_bank0", 7)]
         for d in range(2):
-            term = row("g_term0_%d" % d)
-            fetch_on_scalar(term[:], h2[0], pos[d][:])
-            add_turned(g_sums[0], term[:], start=(d == 0))
-        h2.append(leave_psum(bank2, "h2_1", place_v3))
+            fetch_on_scalar(g_terms0[d][:], h2[0], pos[d][:])
+            add_turned(g_sums[0], g_terms0[d][:], start=(d == 0))
         fetch_on_scalar(a_terms1[1][:], h1[1], pos[1][:])
+        add_turned(a_sums[1], a_terms1[1][:])
+        h2.append(leave_psum(bank2, "h2_1", place_v3))
+        h3 = [leave_psum(bank3[0], "h3_0")]
         g_first1 = row("g_first1")
         fetch_on_scalar(g_first1[:], h2[1], pos[0][:])
-        h3 = [leave_psum(bank3[b], "h3_%d" % b) for b in range(BLOCKS)]
+        h3.append(leave_psum(bank3[1], "h3_1"))
 
         woven_e = weave_both("e", (on_vector, on_vector))
-        fetch_on_vector(raw["e"][:, everyone], h1[0], pos[0][:])
-        add_turned(a_sums[0], raw["e"][:, everyone], start=True)
+        fetch_on_vector(raw["e"][:, everyone], h1[0], pos[1][:])
+        add_turned(a_sums[0], raw["e"][:, everyone])
         nodes = quantise(woven_e[:], "e")
-        for d in range(2):
-            add_turned(a_sums[1], a_terms1[d][:])
 
-        woven_w = sbuf([P, 2 * PACK * N], BF16, "woven_w")
-        weave(on_vector, woven_w[:, : PACK * N], "w3", slice(0, N))
-        for b in range(BLOCKS):
-            weave(on_vector, woven_w[:, PACK * (N + P * b) : PACK * (N + P * (b + 1))], "w1", cols[b])
-        fetch_on_vector(raw["w1"][:, everyone], h1[0], pos[1][:])
-        add_turned(a_sums[0], raw["w1"][:, everyone])
-        q_w = quantise(woven_w[:], "w")
-        ebank3 = [product("e3_bank%d" % b, b, q_w, cols[b], nodes, everyone) for b in range(BLOCKS)]
-        ebank1 = node_product(q_w, N, "e1_bank", 6)
+        q_w3 = round_and_quantise_in_halves("w3")
+        ebank3 = [product("e3_bank%d" % b, b, q_w3[b], lo, nodes, everyone) for b in range(BLOCKS)]
         e3 = [leave_psum(ebank3[b], "e3_%d" % b) for b in range(BLOCKS)]
 
-        woven_w2 = weave_both("w2", (on_vector, on_vector), place_e1)
+        ebank1 = node_product(round_and_quantise_in_halves("w1"), "e1_bank", 6)
+        woven_w2 = [sbuf([P, PACK * P], BF16, "woven_w2_%d" % b, (place_e1, None)[b]) for b in range(BLOCKS)]
+        for b in range(BLOCKS):
+            weave(on_vector, woven_w2[b][:], "w2", cols[b])
+        q_w2 = [quantise(woven_w2[0][:], "w2_0")]
         fetch_with(raw["w2"][:, everyone], h2[1], pos[1][:], g_first1[:], ALU.add)
-        ebank2 = node_product(quantise(woven_w2[:], "w2"), 0, "e2_bank", 4)
+        q_w2.append(quantise(woven_w2[1][:], "w2_1"))
+        ebank2 = node_product(q_w2, "e2_bank", 4)
+        e1 = leave_psum(ebank1, "e1", place_e1)
         cells00 = row("cells00")
         fetch_on_scalar(cells00[:], cells[0], pos[0][:])
-        e1 = leave_psum(ebank1, "e1", place_e1)
         e2 = leave_psum(ebank2, "e2", place_e2)
         f_pre = [raw["w2"][:, V + 2 * V * b : V + 2 * V * (b + 1)] for b in range(BLOCKS)]
         for b in range(BLOCKS):

@@ -24,6 +24,7 @@ BANK = 2048
 ROW = V * 4
 LEAD = P
 V2_SHARE = 96
+HALF_LIST = P // 16
 
 
 def tile_picked_ztree_tanh_p_kernel(tc, x_words, x_scales, eT, w1, w2, w3, v1, v2, v3, cell, offs, pos1, pos2, out):
@@ -69,18 +70,12 @@ def tile_picked_ztree_tanh_p_kernel(tc, x_words, x_scales, eT, w1, w2, w3, v1, v
                 weave(engine, woven[:, PACK * span.start : PACK * span.stop], name, span)
             return woven
 
-        def quantise(woven, name):
+        def quantise(woven, name, at=None):
             width = woven.shape[1] // PACK
-            codes = sbuf([P, width], U32, name + "_codes")
+            codes = sbuf([P, width], U32, name + "_codes", at)
             scales = sbuf([P, width], U8, name + "_scales")
             nc.vector.quantize_mx(out=codes[:].bitcast(FP8X4), scales=scales[:], in_=woven)
             return codes, scales
-
-        def round_and_quantise_in_halves(name):
-            woven = [sbuf([P, PACK * P], BF16, "woven_%s_%d" % (name, b)) for b in range(BLOCKS)]
-            for b in range(BLOCKS):
-                weave(on_vector, woven[b][:], name, cols[b])
-            return [quantise(woven[b][:], "%s_%d" % (name, b)) for b in range(BLOCKS)]
 
         def product(name, bank, weights, rows, moving, span):
             dst = psum([P, span.stop - span.start], name, bank)
@@ -123,6 +118,11 @@ def tile_picked_ztree_tanh_p_kernel(tc, x_words, x_scales, eT, w1, w2, w3, v1, v
             for u in range(2):
                 turn(sums[:, u, :], term[:, cols[u]], start and u == 0, stop and u == 1)
 
+        def gate_half(name, d, u, start=False):
+            term = raw[name][:, LEAD : LEAD + P]
+            fetch_on_vector(term, h1[0], pos[d][:, u * HALF_LIST : (u + 1) * HALF_LIST])
+            turn(a_sums[0][:, u, :], term, start, False)
+
         def row(name, at=None):
             return sbuf([P, V], F32, name, at)
 
@@ -133,7 +133,7 @@ def tile_picked_ztree_tanh_p_kernel(tc, x_words, x_scales, eT, w1, w2, w3, v1, v
         lo, hi = slice(0, P), slice(P, 2 * P)
         cols = [lo, hi]
         children, everyone = slice(0, S), slice(0, V)
-        place_e2, place_e1, place_v3 = ROW, 4 * ROW, 6 * ROW
+        place_e2, place_w2, place_v3, place_w3 = ROW, 6 * ROW, 8 * ROW, 10 * ROW
 
         scale_table = sbuf([P, T], U8, "scale_table")
         nc.vector.memset(scale_table[:].bitcast(I32), 0)
@@ -148,7 +148,7 @@ def tile_picked_ztree_tanh_p_kernel(tc, x_words, x_scales, eT, w1, w2, w3, v1, v
         pos.append(load_list(pos2, "pos2_t"))
         for name, src in (("e", eT), ("w3", w3), ("w1", w1), ("w2", w2)):
             raw[name] = load_matrix(src, name)
-        cells = {b: load_cells(b) for b in reversed(range(BLOCKS))}
+        cells = [load_cells(b) for b in range(BLOCKS)]
 
         warm = sbuf([P, 16], F32, "warm")
         nc.vector.memset(warm[:, 0:8], 0.0)
@@ -177,8 +177,7 @@ def tile_picked_ztree_tanh_p_kernel(tc, x_words, x_scales, eT, w1, w2, w3, v1, v
         woven_v3 = weave_both("v3", (on_vector, on_vector), place_v3)
         a_bank = psum([P, 2, N], "a_bank", 5)
         a_sums = [a_bank[:, :, cols[b]] for b in range(BLOCKS)]
-        fetch_on_vector(raw["v3"][:, everyone], h1[0], pos[0][:])
-        add_turned(a_sums[0], raw["v3"][:, everyone], start=True)
+        gate_half("v3", 0, 0, start=True)
         q_v3 = quantise(woven_v3[:], "v3")
         bank3 = [product("h3_bank%d" % b, 2 + b, q_v3, cols[b], picked, children) for b in range(BLOCKS)]
         a_terms1 = [row("a_term1_%d" % d) for d in range(2)]
@@ -195,28 +194,34 @@ def tile_picked_ztree_tanh_p_kernel(tc, x_words, x_scales, eT, w1, w2, w3, v1, v
         h3 = [leave_psum(bank3[0], "h3_0")]
         g_first1 = row("g_first1")
         fetch_on_scalar(g_first1[:], h2[1], pos[0][:])
-        h3.append(leave_psum(bank3[1], "h3_1"))
 
         woven_e = weave_both("e", (on_vector, on_vector))
-        fetch_on_vector(raw["e"][:, everyone], h1[0], pos[1][:])
-        add_turned(a_sums[0], raw["e"][:, everyone])
+        gate_half("e", 0, 1)
         nodes = quantise(woven_e[:], "e")
 
-        q_w3 = round_and_quantise_in_halves("w3")
-        ebank3 = [product("e3_bank%d" % b, b, q_w3[b], lo, nodes, everyone) for b in range(BLOCKS)]
-        e3 = [leave_psum(ebank3[b], "e3_%d" % b) for b in range(BLOCKS)]
+        woven_w3 = weave_both("w3", (on_vector, on_vector))
+        gate_half("w3", 1, 0)
+        q_w3 = quantise(woven_w3[:], "w3", place_w3)
+        ebank3 = [product("e3_bank%d" % b, b, q_w3, cols[b], nodes, everyone) for b in range(BLOCKS)]
+        e3 = [leave_psum(ebank3[0], "e3_0")]
+        h3.append(leave_psum(bank3[1], "h3_1", place_w3))
+        e3.append(leave_psum(ebank3[1], "e3_1"))
 
-        ebank1 = node_product(round_and_quantise_in_halves("w1"), "e1_bank", 6)
-        woven_w2 = [sbuf([P, PACK * P], BF16, "woven_w2_%d" % b, (place_e1, None)[b]) for b in range(BLOCKS)]
+        woven_w1 = weave_both("w1", (on_vector, on_vector))
+        gate_half("w1", 1, 1)
+        q_w1 = quantise(woven_w1[:], "w1")
+        ebank1 = node_product([(q_w1[0][:, cols[b]], q_w1[1][:, cols[b]]) for b in range(BLOCKS)], "e1_bank", 6)
+        woven_w2 = [sbuf([P, PACK * P], BF16, "woven_w2_%d" % b, (place_w2, None)[b]) for b in range(BLOCKS)]
         for b in range(BLOCKS):
             weave(on_vector, woven_w2[b][:], "w2", cols[b])
         q_w2 = [quantise(woven_w2[0][:], "w2_0")]
-        fetch_with(raw["w2"][:, everyone], h2[1], pos[1][:], g_first1[:], ALU.add)
+        g_both1 = raw["w2"][:, LEAD : LEAD + P]
+        fetch_with(g_both1, h2[1], pos[1][:, :HALF_LIST], g_first1[:, lo], ALU.add)
         q_w2.append(quantise(woven_w2[1][:], "w2_1"))
         ebank2 = node_product(q_w2, "e2_bank", 4)
-        e1 = leave_psum(ebank1, "e1", place_e1)
-        cells00 = row("cells00")
-        fetch_on_scalar(cells00[:], cells[0], pos[0][:])
+        e1 = leave_psum(ebank1, "e1", place_w2 - 3 * ROW // 2)
+        g_second1 = sbuf([P, P], F32, "g_second1", place_w2 + ROW // 2)
+        fetch_on_scalar(g_second1[:], h2[1], pos[1][:, HALF_LIST:])
         e2 = leave_psum(ebank2, "e2", place_e2)
         f_pre = [raw["w2"][:, V + 2 * V * b : V + 2 * V * (b + 1)] for b in range(BLOCKS)]
         for b in range(BLOCKS):
@@ -225,7 +230,9 @@ def tile_picked_ztree_tanh_p_kernel(tc, x_words, x_scales, eT, w1, w2, w3, v1, v
         for b in range(BLOCKS):
             add_turned(a_sums[b], e1[:, b, :], stop=(b == BLOCKS - 1))
         g_sums.append(psum([P, 2, P], "g_bank1", 6))
-        add_turned(g_sums[1], raw["w2"][:, everyone], start=True)
+        turn(g_sums[1][:, 0, :], g_both1, True, False)
+        turn(g_sums[1][:, 1, :], g_first1[:, hi], False, False)
+        turn(g_sums[1][:, 1, :], g_second1[:], False, False)
 
         f = [sbuf([P, 2 * V], F32, "f0")]
         nc.scalar.activation(f[0][:], f_pre[0], ACT.Sigmoid)
@@ -243,29 +250,29 @@ def tile_picked_ztree_tanh_p_kernel(tc, x_words, x_scales, eT, w1, w2, w3, v1, v
 
         fc0 = pair("fc0")
         kept_bank = psum([P, 2, P], "kept_bank", 4)
-        nc.vector.tensor_tensor(fc0[:, 0, :], cells00[:], f[0][:, :V], ALU.mult)
-        fetch_with(fc0[:, 1, :], cells[0], pos[1][:], f[0][:, V:], ALU.mult)
         for d in range(2):
+            fetch_with(fc0[:, d, :], cells[0], pos[d][:], f[0][:, d * V : (d + 1) * V], ALU.mult)
             add_turned(kept_bank, fc0[:, d, :], start=(d == 0), stop=(d == 1))
         kept0_turned = leave_psum(kept_bank, "kept0_turned")
         fresh_turned = pair("fresh_turned")
         nc.vector.tensor_tensor(fresh_turned[:], a_turned[:], g_turned[:], ALU.mult)
-        state_bank = [psum([P, V], "state_bank%d" % b, 2 + b) for b in range(BLOCKS)]
+        state_bank1 = psum([P, V], "state_bank1", 3)
         for u in range(2):
-            turn(state_bank[1][:, cols[u]], fresh_turned[:, u, hi], True, True)
+            turn(state_bank1[:, cols[u]], fresh_turned[:, u, hi], True, True)
+        state_banks0 = [psum([P, P], "state_bank0_%d" % u, (2, 0)[u]) for u in range(2)]
         for u in range(2):
-            turn(state_bank[0][:, cols[u]], fresh_turned[:, u, lo], u == 0, False)
-        for u in range(2):
-            turn(state_bank[0][:, cols[u]], kept0_turned[:, u, :], False, u == 1)
+            turn(state_banks0[u][:], fresh_turned[:, u, lo], True, False)
+            turn(state_banks0[u][:], kept0_turned[:, u, :], False, True)
         first1 = row("first1")
         fetch_with(first1[:], cells[1], pos[0][:], f[1][:, :V], ALU.mult)
         last1 = row("last1")
         nc.vector.tensor_tensor(last1[:], cells11[:], f[1][:, V:], ALU.mult)
         part1 = [sbuf([P, P], F32, "part1_%d" % u) for u in range(2)]
         for u in range(2):
-            nc.vector.tensor_tensor(part1[u][:], first1[:, cols[u]], state_bank[1][:, cols[u]], ALU.add)
+            nc.vector.tensor_tensor(part1[u][:], first1[:, cols[u]], state_bank1[:, cols[u]], ALU.add)
         result0 = row("result0")
-        nc.scalar.activation(result0[:], state_bank[0][:], ACT.Tanh)
+        for u in range(2):
+            nc.scalar.activation(result0[:, cols[u]], state_banks0[u][:], ACT.Tanh)
         nc.sync.dma_start(out=out[lo, :], in_=result0[:])
         for u in range(2):
             state, result = sbuf([P, P], F32, "state1_%d" % u), sbuf([P, P], F32, "result1_%d" % u)

@@ -262,6 +262,7 @@ def tile_picked_ztree_tanh_p_kernel(tc, x_words, x_scales, eT, w1, w2, w3, v1, v
         state_banks0 = [psum([P, P], "state_bank0_%d" % u, (2, 0)[u]) for u in range(2)]
         for u in range(2):
             turn(state_banks0[u][:], fresh_turned[:, u, lo], True, False)
+        for u in range(2):
             turn(state_banks0[u][:], kept0_turned[:, u, :], False, True)
         first1 = row("first1")
         fetch_with(first1[:], cells[1], pos[0][:], f[1][:, :V], ALU.mult)

from contextlib import ExitStack

import concourse.mybir as mybir
from concourse.masks import make_identity

K, T, S, V, N = 512, 1024, 512, 256, 256
FLOPS = 2 * K * N * 3 * (V + S)

F32 = mybir.dt.float32
BF16 = mybir.dt.bfloat16
I32 = mybir.dt.int32
U32 = mybir.dt.uint32
U16 = mybir.dt.uint16
U8 = mybir.dt.uint8
FP8X4 = mybir.dt.float8_e4m3fn_x4
ACT = mybir.ActivationFunctionType
ALU = mybir.AluOpType

P = 128
PACK = 4
RUN = 4
BLOCKS = N // P
BANK = 2048
ROW = V * 4
LEAD = P
V2_SHARE = 96
HALF_LIST = P // 16


def tile_picked_ztree_tanh_p_kernel(tc, x_words, x_scales, eT, w1, w2, w3, v1, v2, v3, cell, offs, pos1, pos2, out):
    nc = tc.nc
    with ExitStack() as ctx:
        keep = ctx.enter_context(tc.tile_pool(name="keep", bufs=1))
        shared = ctx.enter_context(tc.tile_pool(name="shared", bufs=1))
        banks = ctx.enter_context(tc.psum_pool(name="banks", bufs=1))

        def sbuf(shape, dtype, name, at=None):
            if at is None:
                return keep.tile(shape, dtype, name=name, align_bytes=64)
            return shared.tile(shape, dtype, name=name, offset=at, align_bytes=64)

        def psum(shape, name, bank):
            return banks.tile(shape, F32, name=name, offset=bank * BANK)

        def load_list(src, name):
            lst = keep.tile(list(src.shape), U16, name=name)
            nc.sync.dma_start(lst[:], src)
            return lst

        def load_matrix(src, name):
            flat = sbuf([P, 2 * LEAD + PACK * N], F32, "raw_" + name)
            nc.sync.dma_start(out=flat[:, LEAD : LEAD + PACK * N], in_=src.rearrange("(p j) c -> p (j c)", j=PACK))
            return flat

        def load_cells(b):
            rows = sbuf([P, S], F32, "cell%d" % b)
            nc.sync.dma_start(out=rows[:], in_=cell[b * P : (b + 1) * P, :])
            return rows

        def weave(copy, dst, name, span):
            src = raw[name][:, LEAD : LEAD + PACK * N].rearrange("p (j c) -> p j c", j=PACK)[:, :, span]
            if copy is on_vector:
                copy(out=dst.rearrange("p (c i h j) -> p c h i j", i=RUN, h=2, j=2), in_=src.rearrange("p (h j) (c i) -> p c h i j", i=RUN, j=2))
            else:
                copy(out=dst.rearrange("p (c i j) -> p c j i", i=RUN, j=PACK), in_=src.rearrange("p j (c i) -> p c j i", i=RUN))

        def weave_both(name, engines, at=None, cut=P):
            woven = sbuf([P, PACK * N], BF16, "woven_" + name, at)
            for engine, span in zip(engines, (slice(0, cut), slice(cut, N))):
                weave(engine, woven[:, PACK * span.start : PACK * span.stop], name, span)
            return woven

        def quantise(woven, name, at=None):
            width = woven.shape[1] // PACK
            codes = sbuf([P, width], U32, name + "_codes", at)
            scales = sbuf([P, width], U8, name + "_scales")
            nc.vector.quantize_mx(out=codes[:].bitcast(FP8X4), scales=scales[:], in_=woven)
            return codes, scales

        def product(name, bank, weights, rows, moving, span):
            dst = psum([P, span.stop - span.start], name, bank)
            nc.tensor.matmul_mx(out=dst[:], lhsT=weights[0][:, rows].bitcast(FP8X4), lhsT_scale=weights[1][:, rows],
                                rhs=moving[0][:, span].bitcast(FP8X4), rhs_scale=moving[1][:, span], start=True, stop=True)
            return dst

        def node_product(weights, name, bank):
            dst = psum([P, BLOCKS, V], name, bank)
            for b in range(BLOCKS):
                nc.tensor.matmul_mx(out=dst[:, b, :], lhsT=weights[b][0][:].bitcast(FP8X4), lhsT_scale=weights[b][1][:],
                                    rhs=nodes[0][:].bitcast(FP8X4), rhs_scale=nodes[1][:], start=True, stop=True)
            return dst

        def leave_psum(src, name, at=None):
            rows = sbuf(list(src.shape), F32, name, at)
            nc.scalar.copy(out=rows[:], in_=src[:])
            return rows

        def state_row_in_halves(name, first_bank, weights, rows):
            dst = sbuf([P, S], F32, name)
            for u in range(2):
                half = slice(u * V, (u + 1) * V)
                nc.scalar.copy(out=dst[:, half], in_=product("%s_bank%d" % (name, u), first_bank + u, weights, rows, picked, half)[:])
            return dst

        def fetch_on_vector(dst, window, offsets):
            nc.vector.tensor_copy(dst, window[:].indirect(offsets))

        def fetch_on_scalar(dst, window, offsets):
            nc.scalar.activation(dst, window[:].indirect(offsets), ACT.Copy)

        def fetch_with(dst, window, offsets, other, op):
            nc.vector.tensor_tensor(dst, window[:].indirect(offsets), other, op)

        def turn(dst, term, start, stop):
            nc.tensor.matmul(dst, term, identity[:], start=start, stop=stop, is_transpose=True)

        def add_turned(sums, term, start=False, stop=False):
            for u in range(2):
                turn(sums[:, u, :], term[:, cols[u]], start and u == 0, stop and u == 1)

        def gate_half(name, d, u, start=False):
            term = raw[name][:, LEAD : LEAD + P]
            fetch_on_vector(term, h1[0], pos[d][:, u * HALF_LIST : (u + 1) * HALF_LIST])
            turn(a_sums[0][:, u, :], term, start, False)

        def row(name, at=None):
            return sbuf([P, V], F32, name, at)

        def pair(name, at=None):
            return sbuf([P, 2, V], F32, name, at)

        on_scalar, on_vector = nc.scalar.copy, nc.vector.tensor_copy
        lo, hi = slice(0, P), slice(P, 2 * P)
        cols = [lo, hi]
        children, everyone = slice(0, S), slice(0, V)
        place_e2, place_w2, place_v3, place_w3 = ROW, 6 * ROW, 8 * ROW, 10 * ROW

        scale_table = sbuf([P, T], U8, "scale_table")
        nc.vector.memset(scale_table[:].bitcast(I32), 0)
        word_table = sbuf([P, T], U32, "word_table")
        nc.sync.dma_start(out=word_table[:].bitcast(I32), in_=x_words[0].rearrange("p c r -> p (c r)").bitcast(I32))
        offs_t = load_list(offs, "offs_t")
        for q in range(4):
            nc.sync.dma_start(out=scale_table[32 * q : 32 * q + 4, :].bitcast(I32), in_=x_scales[0, 4 * q : 4 * q + 4, :].bitcast(I32))
        raw = {"v1": load_matrix(v1, "v1"), "v2": load_matrix(v2, "v2")}
        pos = [load_list(pos1, "pos1_t")]
        raw["v3"] = load_matrix(v3, "v3")
        pos.append(load_list(pos2, "pos2_t"))
        for name, src in (("e", eT), ("w3", w3), ("w1", w1), ("w2", w2)):
            raw[name] = load_matrix(src, name)
        cells = [load_cells(b) for b in range(BLOCKS)]

        warm = sbuf([P, 16], F32, "warm")
        nc.vector.memset(warm[:, 0:8], 0.0)
        nc.scalar.activation(warm[:, 8:16], warm[:, 0:8], ACT.Sigmoid)
        identity = sbuf([P, P], F32, "identity")
        nc.vector.memset(identity[:], 0.0)
        make_identity(nc, identity[:], nomemset=True)

        x_codes = sbuf([P, S], U32, "x_codes")
        x_bytes = sbuf([P, S], U8, "x_bytes")
        picked = (x_codes, x_bytes)
        nc.vector.tensor_copy(x_codes[:], word_table[:].indirect(offs_t[:]))
        nc.vector.tensor_copy(x_bytes[:], scale_table[:].indirect(offs_t[:]))

        woven_v1 = [sbuf([P, PACK * P], BF16, "woven_v1_%d" % b) for b in range(BLOCKS)]
        for b in range(BLOCKS):
            weave(on_scalar, woven_v1[b][:], "v1", cols[b])
        q_v1 = [quantise(woven_v1[0][:], "v1_0")]
        woven_v2 = weave_both("v2", (on_scalar, on_vector), cut=V2_SHARE)
        q_v1.append(quantise(woven_v1[1][:], "v1_1"))
        q_v2 = quantise(woven_v2[:], "v2")
        h1 = [state_row_in_halves("h1_%d" % b, 2 * b, q_v1[b], lo) for b in range(BLOCKS)]
        h2 = [state_row_in_halves("h2_0", 0, q_v2, lo)]
        bank2 = product("h2_bank1", 4, q_v2, hi, picked, children)

        woven_v3 = weave_both("v3", (on_vector, on_vector), place_v3)
        a_bank = psum([P, 2, N], "a_bank", 5)
        a_sums = [a_bank[:, :, cols[b]] for b in range(BLOCKS)]
        gate_half("v3", 0, 0, start=True)
        q_v3 = quantise(woven_v3[:], "v3")
        bank3 = [product("h3_bank%d" % b, 2 + b, q_v3, cols[b], picked, children) for b in range(BLOCKS)]
        a_terms1 = [row("a_term1_%d" % d) for d in range(2)]
        g_terms0 = [row("g_term0_%d" % d) for d in range(2)]
        fetch_on_scalar(a_terms1[0][:], h1[1], pos[0][:])
        add_turned(a_sums[1], a_terms1[0][:])
        g_sums = [psum([P, 2, P], "g_bank0", 7)]
        for d in range(2):
            fetch_on_scalar(g_terms0[d][:], h2[0], pos[d][:])
            add_turned(g_sums[0], g_terms0[d][:], start=(d == 0))
        fetch_on_scalar(a_terms1[1][:], h1[1], pos[1][:])
        add_turned(a_sums[1], a_terms1[1][:])
        h2.append(leave_psum(bank2, "h2_1", place_v3))
        h3 = [leave_psum(bank3[0], "h3_0")]
        g_first1 = row("g_first1")
        fetch_on_scalar(g_first1[:], h2[1], pos[0][:])

        woven_e = weave_both("e", (on_vector, on_vector))
        gate_half("e", 0, 1)
        nodes = quantise(woven_e[:], "e")

        woven_w3 = weave_both("w3", (on_vector, on_vector))
        gate_half("w3", 1, 0)
        q_w3 = quantise(woven_w3[:], "w3", place_w3)
        ebank3 = [product("e3_bank%d" % b, b, q_w3, cols[b], nodes, everyone) for b in range(BLOCKS)]
        e3 = [leave_psum(ebank3[0], "e3_0")]
        h3.append(leave_psum(bank3[1], "h3_1", place_w3))
        e3.append(leave_psum(ebank3[1], "e3_1"))

        woven_w1 = weave_both("w1", (on_vector, on_vector))
        gate_half("w1", 1, 1)
        q_w1 = quantise(woven_w1[:], "w1")
        ebank1 = node_product([(q_w1[0][:, cols[b]], q_w1[1][:, cols[b]]) for b in range(BLOCKS)], "e1_bank", 6)
        woven_w2 = [sbuf([P, PACK * P], BF16, "woven_w2_%d" % b, (place_w2, None)[b]) for b in range(BLOCKS)]
        for b in range(BLOCKS):
            weave(on_vector, woven_w2[b][:], "w2", cols[b])
        q_w2 = [quantise(woven_w2[0][:], "w2_0")]
        g_both1 = raw["w2"][:, LEAD : LEAD + P]
        fetch_with(g_both1, h2[1], pos[1][:, :HALF_LIST], g_first1[:, lo], ALU.add)
        q_w2.append(quantise(woven_w2[1][:], "w2_1"))
        ebank2 = node_product(q_w2, "e2_bank", 4)
        e1 = leave_psum(ebank1, "e1", place_w2 - 3 * ROW // 2)
        g_second1 = sbuf([P, P], F32, "g_second1", place_w2 + ROW // 2)
        fetch_on_scalar(g_second1[:], h2[1], pos[1][:, HALF_LIST:])
        e2 = leave_psum(ebank2, "e2", place_e2)
        f_pre = [raw["w2"][:, V + 2 * V * b : V + 2 * V * (b + 1)] for b in range(BLOCKS)]
        for b in range(BLOCKS):
            for d in range(2):
                fetch_with(f_pre[b][:, d * V : (d + 1) * V], h3[b], pos[d][:], e3[b][:], ALU.add)
        for b in range(BLOCKS):
            add_turned(a_sums[b], e1[:, b, :], stop=(b == BLOCKS - 1))
        g_sums.append(psum([P, 2, P], "g_bank1", 6))
        turn(g_sums[1][:, 0, :], g_both1, True, False)
        turn(g_sums[1][:, 1, :], g_first1[:, hi], False, False)
        turn(g_sums[1][:, 1, :], g_second1[:], False, False)

        f = [sbuf([P, 2 * V], F32, "f0")]
        nc.scalar.activation(f[0][:], f_pre[0], ACT.Sigmoid)
        for b in reversed(range(BLOCKS)):
            add_turned(g_sums[b], e2[:, b, :], stop=True)
        a_turned = pair("a_turned")
        g_turned = pair("g_turned")
        nc.scalar.activation(a_turned[:], a_bank[:], ACT.Sigmoid)
        for b in reversed(range(BLOCKS)):
            nc.scalar.activation(g_turned[:, :, cols[b]], g_sums[b][:], ACT.Tanh)
        f.append(sbuf([P, 2 * V], F32, "f1", place_e2 - ROW))
        nc.scalar.activation(f[1][:], f_pre[1], ACT.Sigmoid)
        cells11 = row("cells11", place_e2 + ROW)
        fetch_on_scalar(cells11[:], cells[1], pos[1][:])

        fc0 = pair("fc0")
        kept_bank = psum([P, 2, P], "kept_bank", 4)
        for d in range(2):
            fetch_with(fc0[:, d, :], cells[0], pos[d][:], f[0][:, d * V : (d + 1) * V], ALU.mult)
            add_turned(kept_bank, fc0[:, d, :], start=(d == 0), stop=(d == 1))
        kept0_turned = leave_psum(kept_bank, "kept0_turned")
        fresh_turned = pair("fresh_turned")
        nc.vector.tensor_tensor(fresh_turned[:], a_turned[:], g_turned[:], ALU.mult)
        state_bank1 = psum([P, V], "state_bank1", 3)
        for u in range(2):
            turn(state_bank1[:, cols[u]], fresh_turned[:, u, hi], True, True)
        state_banks0 = [psum([P, P], "state_bank0_%d" % u, (2, 0)[u]) for u in range(2)]
        for u in range(2):
            turn(state_banks0[u][:], fresh_turned[:, u, lo], True, False)
        for u in range(2):
            turn(state_banks0[u][:], kept0_turned[:, u, :], False, True)
        first1 = row("first1")
        fetch_with(first1[:], cells[1], pos[0][:], f[1][:, :V], ALU.mult)
        last1 = row("last1")
        nc.vector.tensor_tensor(last1[:], cells11[:], f[1][:, V:], ALU.mult)
        part1 = [sbuf([P, P], F32, "part1_%d" % u) for u in range(2)]
        for u in range(2):
            nc.vector.tensor_tensor(part1[u][:], first1[:, cols[u]], state_bank1[:, cols[u]], ALU.add)
        result0 = row("result0")
        for u in range(2):
            nc.scalar.activation(result0[:, cols[u]], state_banks0[u][:], ACT.Tanh)
        nc.sync.dma_start(out=out[lo, :], in_=result0[:])
        for u in range(2):
            state, result = sbuf([P, P], F32, "state1_%d" % u), sbuf([P, P], F32, "result1_%d" % u)
            nc.vector.tensor_tensor(state[:], part1[u][:], last1[:, cols[u]], ALU.add)
            nc.scalar.activation(result[:], state[:], ACT.Tanh)
            nc.sync.dma_start(out=out[hi, cols[u]], in_=result[:])
